import numpy as np
import ml_dtypes


def mxq(x, axis, fmt="e4m3"):
    dtype, down = {"e4m3": (ml_dtypes.float8_e4m3fn, 7), "e5m2": (ml_dtypes.float8_e5m2, 14)}[fmt]
    v = np.moveaxis(np.asarray(x, np.float32).astype(ml_dtypes.bfloat16).astype(np.float64), axis, -1)
    blocks = v.reshape(v.shape[:-1] + (-1, 32))
    amax = np.abs(blocks).max(-1, keepdims=True)
    byte = np.maximum(np.where(amax > 0, np.frexp(amax)[1] - 1 + 127, 0) - down, 1)
    scale = np.exp2(byte - 127.0)
    codes = (blocks / scale).astype(np.float32).astype(dtype).astype(np.float64)
    return np.moveaxis((codes * scale).reshape(v.shape), -1, axis)


WIDE = False


def mx_kscale(k):
    if not WIDE:
        return np.ones(k)
    levels = np.array([24, -24, 12, -12, 0])
    if k % 512:
        return np.exp2(np.random.permutation(np.resize(levels, k // 32))).repeat(32)
    a = np.empty((k // 512, 16))
    for p in range(k // 512):
        a[p, :8] = np.random.permutation(np.resize(levels, 8))
        for g in range(8):
            far = levels[np.abs(levels - a[p, g]) >= 10]
            a[p, g + 8] = far[np.random.randint(len(far))]
    return np.exp2(a.ravel()).repeat(32)


def f64(x):
    return np.asarray(x).astype(np.float64)


def striped(idx):
    return np.tile(idx.reshape(-1, 16).T, (8, 1)).astype(np.uint16)


def unstriped(offs):
    return offs[:16].T.reshape(-1).astype(np.int64)


E2M1 = np.array([0.0, 0.5, 1.0, 1.5, 2.0, 3.0, 4.0, 6.0, -0.0, -0.5, -1.0, -1.5, -2.0, -3.0, -4.0, -6.0])


def pack_weight(w, fmt):
    k, n = w.shape
    w = f64(np.asarray(w, np.float32).astype(ml_dtypes.bfloat16)).reshape(k // 32, 32, n)
    amax = np.abs(w).max(1)
    if fmt == "e4m3":
        byte = np.frexp(amax)[1] - 1 + 127 - 7
    else:
        mant, ex = np.frexp(amax / 6.0)
        byte = np.where(mant > 0.5, ex, ex - 1) + 127
    byte = np.clip(np.where(amax > 0, byte, 1), 1, 254)
    scaled = (w * np.exp2(127.0 - byte)[:, None, :]).reshape(k, n).astype(np.float32)
    by_word = np.ascontiguousarray(scaled.reshape(k // 512, 128, 4, n).transpose(0, 1, 3, 2))
    if fmt == "e4m3":
        words = by_word.astype(ml_dtypes.float8_e4m3fn).view(np.uint8)
    else:
        c = by_word.astype(ml_dtypes.float4_e2m1fn).view(np.uint8) & 0xF
        words = (c[..., 0::2] | (c[..., 1::2] << 4)).reshape(k // 512, 128, 2 * n)
    return np.ascontiguousarray(words), np.ascontiguousarray(byte.astype(np.uint8).reshape(k // 512, 16, n))


def unpack_weight(words, scales, fmt):
    g, _, n = scales.shape
    words = np.ascontiguousarray(words).reshape(g, 128, n, -1)
    if fmt == "e4m3":
        vals = words.view(ml_dtypes.float8_e4m3fn).astype(np.float64)
    else:
        nib = np.empty((g, 128, n, 4), np.uint8)
        nib[..., 0::2] = words & 0xF
        nib[..., 1::2] = words >> 4
        vals = E2M1[nib]
    vals = vals * np.repeat(np.exp2(scales.astype(np.float64) - 127.0), 8, axis=1)[..., None]
    return vals.transpose(0, 1, 3, 2).reshape(g * 512, n)


def planes(y):
    n, m = y.shape
    v = y.astype(np.float32).astype(ml_dtypes.bfloat16).astype(np.float64).reshape(n // 32, 32, m)
    top = np.abs(v).max(1)
    byte = np.clip(np.where(top > 0, np.frexp(top)[1] - 1 + 127 - 7, 1), 1, 254)
    codes = (v * np.exp2(127.0 - byte)[:, None, :]).reshape(n, m).astype(np.float32).astype(ml_dtypes.float8_e4m3fn).view(np.uint8)
    words = codes.reshape(n // 512, 128, 4, m).transpose(0, 1, 3, 2)
    return np.ascontiguousarray(words), np.ascontiguousarray(byte.astype(np.uint8).reshape(n // 512, 16, m))


K, R, N, T, J = 1024, 1024, 512, 2048, 1024


def setup_inputs():
    n = np.random.standard_normal
    s = mx_kscale(K)[:, None]
    u = mx_kscale(R)[:, None]
    p_tab = pack_weight(n((K, T)) * s, "e4m3")
    p_ws = pack_weight(n((K, R)) / np.sqrt(2 * K) / s * u.T, "e2m1")
    p_wt = pack_weight(n((K, R)) / np.sqrt(2 * K) / s * u.T, "e4m3")
    p_wd = pack_weight(n((R, N)) / np.sqrt(R) / u, "e4m3")
    return {
        "tab_words": p_tab[0],
        "tab_scales": p_tab[1],
        "ws_words": p_ws[0],
        "ws_scales": p_ws[1],
        "wt_words": p_wt[0],
        "wt_scales": p_wt[1],
        "wd_words": p_wd[0],
        "wd_scales": p_wd[1],
        "b": (0.3 * n(N)).astype(np.float32),
        "wgo": np.tile(np.random.uniform(0.5, 2.0, J), (128, 1)).astype(np.float32),
        "offs": striped(np.random.permutation(T)[:J]),
        "offs2": striped(np.random.permutation(T)[:J]),
    }


def reference(tab_words, tab_scales, ws_words, ws_scales, wt_words, wt_scales, wd_words, wd_scales, b, wgo, offs, offs2):
    idx = unstriped(offs)
    idx2 = unstriped(offs2)
    tab_ = unpack_weight(tab_words, tab_scales, "e4m3")[:, idx]
    tabb_ = unpack_weight(tab_words, tab_scales, "e4m3")[:, idx2]
    ws_ = unpack_weight(ws_words, ws_scales, "e2m1")
    wt_ = unpack_weight(wt_words, wt_scales, "e4m3")
    a = ws_.T @ tab_ + wt_.T @ tabb_
    h = np.maximum(a, 0.0)
    h_ = mxq(h, 0, "e4m3")
    wd_ = unpack_weight(wd_words, wd_scales, "e4m3")
    y = wd_.T @ h_
    out = np.zeros((N, T))
    out[:, idx2] = f64(wgo)[0] * (y + f64(b)[:, None])
    return (out,) + planes(out)

@@ -1,0 +1,286 @@
+from contextlib import ExitStack
+
+import concourse.mybir as mybir
+from concourse.masks import make_identity
+
+K, R, N, T, J = 1024, 1024, 512, 2048, 1024
+FLOPS = 2 * J * (2 * K * R + R * N)
+
+F32 = mybir.dt.float32
+BF16 = mybir.dt.bfloat16
+I32 = mybir.dt.int32
+U32 = mybir.dt.uint32
+U16 = mybir.dt.uint16
+U8 = mybir.dt.uint8
+FP8X4 = mybir.dt.float8_e4m3fn_x4
+FP4X4 = mybir.dt.float4_e2m1fn_x4
+ACT = mybir.ActivationFunctionType
+MULT = mybir.AluOpType.mult
+
+P = 128
+PACK = 4
+PASSES = 2
+BANK = 512
+CHUNK = 256
+CHUNKS = J // CHUNK
+PER_COL = 16
+OUT_WIDTHS = (256, 512, 512, 512, 256)
+
+
+def tile_list_msg_relu_biasP_kernel(
+    tc, tab_words, tab_scales, ws_words, ws_scales, wt_words, wt_scales, wd_words, wd_scales,
+    b, wgo, offs, offs2, out_0, out_1, out_2,
+):
+    nc = tc.nc
+
+    with ExitStack() as ctx:
+        keep = ctx.enter_context(tc.tile_pool(name="keep", bufs=1))
+        loads = ctx.enter_context(tc.tile_pool(name="loads", bufs=1))
+        ring = ctx.enter_context(tc.tile_pool(name="ring", bufs=2))
+        psum = ctx.enter_context(tc.psum_pool(name="psum", bufs=1))
+
+        def sb(name, shape, dtype, tag=None):
+            return keep.tile(shape, dtype, name=name, tag=tag or name, align_bytes=64)
+
+        def entries(lst, first, count):
+            return lst[:, first // PER_COL : (first + count) // PER_COL]
+
+        src_list = keep.tile([P, J // PER_COL], U16, name="src_list")
+        tgt_list = keep.tile([P, J // PER_COL], U16, name="tgt_list")
+        nc.sync.dma_start(src_list[:], offs)
+        nc.sync.dma_start(tgt_list[:], offs2)
+
+        tab_sc = sb("tab_sc", [P, T], U8)
+        nc.vector.memset(tab_sc[:].bitcast(I32), 0)
+        for q in range(4):
+            nc.sync.dma_start(
+                tab_sc[32 * q : 32 * q + 8, :].bitcast(I32), tab_scales[:, 4 * q : 4 * q + 4, :].bitcast(I32)
+            )
+
+        load_words = [T, T, R // 2, R, R // 2, R, PASSES * N, J, 16]
+        w_sc_cols = PASSES * R + N
+        zeros = loads.tile([P, sum(load_words)], I32, name="zeros", offset=0, align_bytes=64)
+        nc.gpsimd.memset(zeros[:, : w_sc_cols // 4], 0)
+        ident = sb("ident", [P, P], F32)
+        make_identity(nc, ident[:])
+        w_sc = sb("w_sc", [P, w_sc_cols], U8)
+        nc.vector.tensor_copy(w_sc[:].bitcast(I32), zeros[:, : w_sc_cols // 4])
+        src_sc1 = sb("src_sc1", [P, J], U8)
+        nc.vector.memset(src_sc1[:].bitcast(I32), 0)
+
+        def landing(name, i, shape, dtype):
+            return loads.tile(shape, dtype, name=name, offset=4 * sum(load_words[:i]), align_bytes=64)
+
+        tab_w = [landing(f"tab_w{a}", a, [P, T], I32) for a in range(PASSES)]
+        ws_w = [landing(f"ws_w{a}", 2 + 2 * a, [P, 2 * R], U8) for a in range(PASSES)]
+        wt_w = [landing(f"wt_w{a}", 3 + 2 * a, [P, R], I32) for a in range(PASSES)]
+        wd_raw = landing("wd_raw", 6, [P, PASSES, N], I32)
+        edge_w = landing("edge_w", 7, [P, J], F32)
+        bias = landing("bias", 8, [P, PACK], F32)
+
+        def load_x4(dst, words):
+            nc.sync.dma_start(dst[:], words.rearrange("p c i -> p (c i)").bitcast(I32))
+
+        def load_w_scales(first_row, scales):
+            for q in range(4):
+                rows = slice(32 * q + first_row, 32 * q + first_row + 4)
+                nc.scalar.dma_start(
+                    w_sc[rows, : PASSES * R].bitcast(I32).rearrange("p (a r) -> p a r", a=PASSES),
+                    scales[:, 4 * q : 4 * q + 4, :].rearrange("a q r -> q a r").bitcast(I32),
+                )
+
+        load_x4(tab_w[0], tab_words[0])
+        load_x4(tab_w[1], tab_words[1])
+        load_w_scales(0, ws_scales)
+        load_w_scales(4, wt_scales)
+        nc.sync.dma_start(ws_w[0][:].bitcast(I32), ws_words[0].bitcast(I32))
+        load_x4(wt_w[0], wt_words[0])
+        nc.sync.dma_start(ws_w[1][:].bitcast(I32), ws_words[1].bitcast(I32))
+        load_x4(wt_w[1], wt_words[1])
+        nc.sync.dma_start(wd_raw[:], wd_words.rearrange("a p n i -> p a (n i)").bitcast(I32))
+        for q in range(4):
+            nc.sync.dma_start(
+                w_sc[32 * q : 32 * q + 8, PASSES * R :].bitcast(I32), wd_scales[:, 4 * q : 4 * q + 4, :].bitcast(I32)
+            )
+        nc.sync.dma_start(bias[:], b.rearrange("(p t) -> p t", t=PACK))
+        nc.sync.dma_start(edge_w[:], wgo)
+
+        pages = []
+        for t in range(PACK):
+            pages.append(sb(f"page{t}", [P, T], F32))
+            nc.gpsimd.memset(pages[t][:], 0.0)
+
+        src_sc = sb("src_sc", [P, J], U8)
+        tgt_sc = sb("tgt_sc", [P, J], U8)
+        picked = {}
+
+        def gather_words(c, a, lst, side):
+            nc.vector.tensor_copy(
+                picked[c][:, 2 * a + side, :],
+                tab_w[a][:].bitcast(U32).indirect(entries(lst, c * CHUNK, CHUNK)),
+            )
+
+        def gather_chunk(c, tag=None):
+            picked[c] = sb(f"picked{c}", [P, 2 * PASSES, CHUNK], U32, tag)
+            for a in range(PASSES):
+                gather_words(c, a, src_list, 0)
+                gather_words(c, a, tgt_list, 1)
+
+        nc.vector.tensor_copy(src_sc[:], tab_sc[:].indirect(src_list[:]))
+        nc.scalar.dma_start(src_sc1[0 : P - 4, :].bitcast(I32), src_sc[4:P, :].bitcast(I32))
+        picked[0] = sb("picked0", [P, 2 * PASSES, CHUNK], U32)
+        gather_words(0, 0, src_list, 0)
+        nc.vector.tensor_copy(tgt_sc[:, :CHUNK], tab_sc[:].indirect(entries(tgt_list, 0, CHUNK)))
+        gather_words(0, 0, tgt_list, 1)
+        gather_words(0, 1, src_list, 0)
+        gather_words(0, 1, tgt_list, 1)
+        nc.vector.tensor_copy(tgt_sc[:, CHUNK:], tab_sc[:].indirect(entries(tgt_list, CHUNK, J - CHUNK)))
+        gather_chunk(1)
+
+        wd_w = sb("wd_w", [P, PASSES, N], I32)
+        nc.vector.tensor_copy(
+            wd_w[:].rearrange("p a (t c i) -> p a c t i", t=PACK, i=4),
+            wd_raw[:].rearrange("p a (c i t) -> p a c t i", t=PACK, i=4),
+        )
+        wd_sc = sb("wd_sc", [P, N], U8)
+        nc.vector.tensor_copy(
+            wd_sc[:].rearrange("p (t m) -> p t m", t=PACK), w_sc[:, PASSES * R :].rearrange("p (m t) -> p t m", t=PACK)
+        )
+        gather_chunk(2)
+
+        def first_pass(acc, blk, half, a, side):
+            c, cols = blk // 2, slice(P * (blk % 2), P * (blk % 2 + 1))
+            edges = slice(P * blk, P * (blk + 1))
+            r_cols = slice(a * R + half * BANK, a * R + (half + 1) * BANK)
+            if side == 0:
+                v_scale = (src_sc, src_sc1)[a][:, edges]
+                w = ws_w[a][:, 2 * half * BANK : 2 * (half + 1) * BANK].bitcast(FP4X4)
+                w_scale = w_sc[:, r_cols]
+            else:
+                v_scale = tgt_sc[4 * a : P, edges]
+                w = wt_w[a][:, half * BANK : (half + 1) * BANK].bitcast(FP8X4)
+                w_scale = w_sc[4:P, r_cols]
+            nc.tensor.matmul_mx(
+                out=acc[:], lhsT=picked[c][:, 2 * a + side, cols].bitcast(FP8X4), lhsT_scale=v_scale,
+                rhs=w, rhs_scale=w_scale, start=(a == 0 and side == 0), stop=(a == 1 and side == 1),
+            )
+
+        order = [(a, side) for a in range(PASSES) for side in range(2)]
+
+        def first_banks(blk):
+            return [psum.tile([P, BANK], F32, name=f"a{blk}_{h}", tag=f"first{2 * (blk % 2) + h}") for h in range(2)]
+
+        def turn(blk, banks, h_in):
+            h_t = ring.tile([P, R], BF16, name=f"h_t{blk}", tag="h_t", align_bytes=64)
+            for half in range(2):
+                nc.scalar.activation(
+                    h_t[:, half * BANK : (half + 1) * BANK].rearrange("j (u p e) -> j u p e", u=2, e=2),
+                    banks[half][:].rearrange("j (p u e) -> j u p e", u=2, e=2),
+                    ACT.Relu,
+                )
+            turned = psum.tile([P, BANK], F32, name=f"turned{blk}", tag=f"turn{blk % 2}")
+            for s in range(4):
+                nc.tensor.transpose(turned[:, P * s : P * (s + 1)], h_t[:].bitcast(F32)[:, P * s : P * (s + 1)], ident[:])
+            nc.scalar.copy(
+                h_in[:].bitcast(F32).rearrange("p (a j u) -> p a j u", a=PASSES, u=2)[:, :, P * (blk % 2) : P * (blk % 2 + 1), :],
+                turned[:].rearrange("p (a u j) -> p a j u", a=PASSES, u=2),
+            )
+
+        h_w, h_sc = {}, {}
+        msg = [sb(f"msg{t}", [P, J], F32) for t in range(PACK)]
+
+        def second(acc, c, t):
+            for a in range(PASSES):
+                nc.tensor.matmul_mx(
+                    out=acc, lhsT=wd_w[:, a, P * t : P * (t + 1)].bitcast(FP8X4),
+                    lhsT_scale=wd_sc[4 * a : P, P * t : P * (t + 1)],
+                    rhs=h_w[c][:, a * CHUNK : (a + 1) * CHUNK].bitcast(FP8X4),
+                    rhs_scale=h_sc[c][:, a * CHUNK : (a + 1) * CHUNK],
+                    start=(a == 0), stop=(a == PASSES - 1),
+                )
+
+        def add_bias(acc, t, first, count):
+            nc.scalar.activation(msg[t][:, first : first + count], acc, ACT.Identity, bias=bias[:, t : t + 1])
+
+        def scatter(t, first, count):
+            nc.vector.tensor_tensor(
+                pages[t][:].indirect(entries(tgt_list, first, count)),
+                msg[t][:, first : first + count], edge_w[:, first : first + count], MULT,
+            )
+
+        def late_slice(c):
+            acc = psum.tile([P, BANK], F32, name=f"late{c}", tag="turn1")
+            second(acc[:, :CHUNK], c, 2)
+            add_bias(acc[:, :CHUNK], 2, c * CHUNK, CHUNK)
+            scatter(2, c * CHUNK, CHUNK)
+
+        for c in range(CHUNKS):
+            h_in = sb(f"h_in{c}", [P, PASSES * CHUNK * PACK], BF16)
+            blocks = (2 * c, 2 * c + 1)
+            if c == 0:
+                banks = {blk: first_banks(blk) for blk in blocks}
+                for side in range(2):
+                    for blk in blocks:
+                        for half in range(2):
+                            first_pass(banks[blk][half], blk, half, 0, side)
+                for blk in blocks:
+                    for half in range(2):
+                        for side in range(2):
+                            first_pass(banks[blk][half], blk, half, 1, side)
+                    turn(blk, banks[blk], h_in)
+            else:
+                for blk in blocks:
+                    pair = first_banks(blk)
+                    for half in range(2):
+                        for a, side in order:
+                            first_pass(pair[half], blk, half, a, side)
+                    turn(blk, pair, h_in)
+            h_w[c] = sb(f"h_w{c}", [P, PASSES * CHUNK], U32)
+            h_sc[c] = sb(f"h_sc{c}", [P, PASSES * CHUNK], U8)
+            nc.vector.quantize_mx(out=h_w[c][:].bitcast(FP8X4), scales=h_sc[c][:], in_=h_in[:])
+            if c == 0:
+                gather_chunk(CHUNKS - 1, "h_in0")
+            else:
+                late_slice(c - 1)
+            acc = psum.tile([P, BANK], F32, name=f"early{c}", tag="second0")
+            for t in range(2):
+                second(acc[:, t * CHUNK : (t + 1) * CHUNK], c, t)
+            for t in range(2):
+                add_bias(acc[:, t * CHUNK : (t + 1) * CHUNK], t, c * CHUNK, CHUNK)
+                scatter(t, c * CHUNK, CHUNK)
+            if c == CHUNKS - 1:
+                late_slice(c)
+            if c % 2 == 1:
+                acc = psum.tile([P, BANK], F32, name=f"last{c}", tag="second1")
+                for i in range(2):
+                    second(acc[:, i * CHUNK : (i + 1) * CHUNK], c - 1 + i, 3)
+                add_bias(acc[:], 3, (c - 1) * CHUNK, 2 * CHUNK)
+        scatter(3, 0, J)
+
+        out_rows = out_0.rearrange("(p t) c -> p t c", t=PACK)
+        starts = [sum(OUT_WIDTHS[:i]) for i in range(len(OUT_WIDTHS))]
+        pairs = [sb(f"pairs{i}", [P, 2, w, 2], BF16) for i, w in enumerate(OUT_WIDTHS)]
+        for t in range(PACK):
+            nc.sync.dma_start(out_rows[:, t, :], pages[t][:])
+            for i, w in enumerate(OUT_WIDTHS):
+                nc.scalar.copy(pairs[i][:, t // 2, :, t % 2], pages[t][:, starts[i] : starts[i] + w])
+        out_sc = sb("out_sc", [P, T], U8)
+        out_words = out_1[0].rearrange("p t i -> p (t i)").bitcast(I32)
+        woven = []
+        for i in range(len(OUT_WIDTHS) + 1):
+            if i < len(OUT_WIDTHS):
+                w = OUT_WIDTHS[i]
+                woven.append(sb(f"woven{i}", [P, w * PACK], BF16))
+                nc.vector.tensor_copy(
+                    woven[i][:].bitcast(F32).rearrange("p (c u) -> p c u", u=2),
+                    pairs[i][:].rearrange("p u c e -> p u (c e)").bitcast(F32).rearrange("p u c -> p c u"),
+                )
+            if i > 0:
+                w, cols = OUT_WIDTHS[i - 1], slice(starts[i - 1], starts[i - 1] + OUT_WIDTHS[i - 1])
+                codes = sb(f"codes{i}", [P, w], I32)
+                nc.vector.quantize_mx(out=codes[:].bitcast(FP8X4), scales=out_sc[:, cols], in_=woven[i - 1][:])
+                nc.sync.dma_start(out_words[:, cols], codes[:])
+        for q in range(4):
+            nc.scalar.dma_start(
+                out_2[0, 4 * q : 4 * q + 4, :].bitcast(I32), out_sc[32 * q : 32 * q + 4, :].bitcast(I32)
+            )

@@ -57,10 +57,10 @@ def tile_list_msg_relu_biasP_kernel(
                 tab_sc[32 * q : 32 * q + 8, :].bitcast(I32), tab_scales[:, 4 * q : 4 * q + 4, :].bitcast(I32)
             )
 
-        load_words = [T, T, R // 2, R, R // 2, R, PASSES * N, J, 16]
+        load_words = [PASSES * T, R // 2, R, R // 2, R, PASSES * N, J, 16, T]
         w_sc_cols = PASSES * R + N
         zeros = loads.tile([P, sum(load_words)], I32, name="zeros", offset=0, align_bytes=64)
-        nc.gpsimd.memset(zeros[:, : w_sc_cols // 4], 0)
+        nc.vector.memset(zeros[:, : w_sc_cols // 4], 0)
         ident = sb("ident", [P, P], F32)
         make_identity(nc, ident[:])
         w_sc = sb("w_sc", [P, w_sc_cols], U8)
@@ -71,12 +71,12 @@ def tile_list_msg_relu_biasP_kernel(
         def landing(name, i, shape, dtype):
             return loads.tile(shape, dtype, name=name, offset=4 * sum(load_words[:i]), align_bytes=64)
 
-        tab_w = [landing(f"tab_w{a}", a, [P, T], I32) for a in range(PASSES)]
-        ws_w = [landing(f"ws_w{a}", 2 + 2 * a, [P, 2 * R], U8) for a in range(PASSES)]
-        wt_w = [landing(f"wt_w{a}", 3 + 2 * a, [P, R], I32) for a in range(PASSES)]
-        wd_raw = landing("wd_raw", 6, [P, PASSES, N], I32)
-        edge_w = landing("edge_w", 7, [P, J], F32)
-        bias = landing("bias", 8, [P, PACK], F32)
+        tab_w = landing("tab_w", 0, [P, PASSES, T], I32)
+        ws_w = [landing(f"ws_w{a}", 1 + 2 * a, [P, 2 * R], U8) for a in range(PASSES)]
+        wt_w = [landing(f"wt_w{a}", 2 + 2 * a, [P, R], I32) for a in range(PASSES)]
+        wd_raw = landing("wd_raw", 5, [P, PASSES, N], I32)
+        edge_w = landing("edge_w", 6, [P, J], F32)
+        bias = landing("bias", 7, [P, PACK], F32)
 
         def load_x4(dst, words):
             nc.sync.dma_start(dst[:], words.rearrange("p c i -> p (c i)").bitcast(I32))
@@ -89,8 +89,7 @@ def tile_list_msg_relu_biasP_kernel(
                     scales[:, 4 * q : 4 * q + 4, :].rearrange("a q r -> q a r").bitcast(I32),
                 )
 
-        load_x4(tab_w[0], tab_words[0])
-        load_x4(tab_w[1], tab_words[1])
+        nc.sync.dma_start(tab_w[:], tab_words.rearrange("a p t i -> p a (t i)").bitcast(I32))
         load_w_scales(0, ws_scales)
         load_w_scales(4, wt_scales)
         nc.sync.dma_start(ws_w[0][:].bitcast(I32), ws_words[0].bitcast(I32))
@@ -106,9 +105,14 @@ def tile_list_msg_relu_biasP_kernel(
         nc.sync.dma_start(edge_w[:], wgo)
 
         pages = []
-        for t in range(PACK):
-            pages.append(sb(f"page{t}", [P, T], F32))
-            nc.gpsimd.memset(pages[t][:], 0.0)
+        def clear(page):
+            for first in range(0, T, BANK):
+                nc.gpsimd.memset(page[:, first : first + BANK], 0.0)
+
+        pages.append(sb("page0", [P, T], F32))
+        nc.vector.memset(pages[0][:], 0.0)
+        pages.append(landing("page1", 8, [P, T], F32))
+        clear(pages[1])
 
         src_sc = sb("src_sc", [P, J], U8)
         tgt_sc = sb("tgt_sc", [P, J], U8)
@@ -117,7 +121,7 @@ def tile_list_msg_relu_biasP_kernel(
         def gather_words(c, a, lst, side):
             nc.vector.tensor_copy(
                 picked[c][:, 2 * a + side, :],
-                tab_w[a][:].bitcast(U32).indirect(entries(lst, c * CHUNK, CHUNK)),
+                tab_w[:, a, :].bitcast(U32).indirect(entries(lst, c * CHUNK, CHUNK)),
             )
 
         def gather_chunk(c, tag=None):
@@ -240,6 +244,9 @@ def tile_list_msg_relu_biasP_kernel(
             nc.vector.quantize_mx(out=h_w[c][:].bitcast(FP8X4), scales=h_sc[c][:], in_=h_in[:])
             if c == 0:
                 gather_chunk(CHUNKS - 1, "h_in0")
+                for t in range(2, PACK):
+                    pages.append(loads.tile([P, T], F32, name=f"page{t}", offset=4 * T * (t - 2), align_bytes=64))
+                    clear(pages[t])
             else:
                 late_slice(c - 1)
             acc = psum.tile([P, BANK], F32, name=f"early{c}", tag="second0")
@@ -248,13 +255,12 @@ def tile_list_msg_relu_biasP_kernel(
             for t in range(2):
                 add_bias(acc[:, t * CHUNK : (t + 1) * CHUNK], t, c * CHUNK, CHUNK)
                 scatter(t, c * CHUNK, CHUNK)
-            if c == CHUNKS - 1:
-                late_slice(c)
-            if c % 2 == 1:
-                acc = psum.tile([P, BANK], F32, name=f"last{c}", tag="second1")
-                for i in range(2):
-                    second(acc[:, i * CHUNK : (i + 1) * CHUNK], c - 1 + i, 3)
-                add_bias(acc[:], 3, (c - 1) * CHUNK, 2 * CHUNK)
+        late_slice(CHUNKS - 1)
+        for c in range(0, CHUNKS, 2):
+            acc = psum.tile([P, BANK], F32, name=f"last{c}", tag="second1")
+            for i in range(2):
+                second(acc[:, i * CHUNK : (i + 1) * CHUNK], c + i, 3)
+            add_bias(acc[:], 3, c * CHUNK, 2 * CHUNK)
         scatter(3, 0, J)
 
         out_rows = out_0.rearrange("(p t) c -> p t c", t=PACK)

@@ -20,10 +20,18 @@ MULT = mybir.AluOpType.mult
 P = 128
 PACK = 4
 PASSES = 2
+QUADRANTS = 4
+QUAD = P // QUADRANTS
+ROWS = 4
 BANK = 512
-CHUNK = 256
+CHUNK = 2 * P
 CHUNKS = J // CHUNK
-PER_COL = 16
+PER_COLUMN = 16
+WORD = 4
+ALIGN = 64
+SOURCE, TARGET = 0, 1
+
+AHEAD_OF_TABLE = 3
 OUT_WIDTHS = (256, 512, 512, 512, 256)
 
 
@@ -36,157 +44,150 @@ def tile_list_msg_relu_biasP_kernel(
     with ExitStack() as ctx:
         keep = ctx.enter_context(tc.tile_pool(name="keep", bufs=1))
         loads = ctx.enter_context(tc.tile_pool(name="loads", bufs=1))
+        late = ctx.enter_context(tc.tile_pool(name="late", bufs=1))
+        dealt = ctx.enter_context(tc.tile_pool(name="dealt", bufs=1))
         ring = ctx.enter_context(tc.tile_pool(name="ring", bufs=2))
         psum = ctx.enter_context(tc.psum_pool(name="psum", bufs=1))
 
         def sb(name, shape, dtype, tag=None):
-            return keep.tile(shape, dtype, name=name, tag=tag or name, align_bytes=64)
+            return keep.tile(shape, dtype, name=name, tag=tag or name, align_bytes=ALIGN)
 
-        def entries(lst, first, count):
-            return lst[:, first // PER_COL : (first + count) // PER_COL]
+        def placed(pool, name, shape, dtype, offset):
+            return pool.tile(shape, dtype, name=name, offset=offset, align_bytes=ALIGN)
 
-        src_list = keep.tile([P, J // PER_COL], U16, name="src_list")
-        tgt_list = keep.tile([P, J // PER_COL], U16, name="tgt_list")
-        nc.sync.dma_start(src_list[:], offs)
-        nc.sync.dma_start(tgt_list[:], offs2)
+        def entries(list_tile, first, count):
+            return list_tile[:, first // PER_COLUMN : (first + count) // PER_COLUMN]
 
-        tab_sc = sb("tab_sc", [P, T], U8)
+        def load_two_planes(plane, scales):
+            for q in range(QUADRANTS):
+                nc.sync.dma_start(
+                    plane[QUAD * q : QUAD * q + PASSES * ROWS, :].bitcast(I32),
+                    scales[:, ROWS * q : ROWS * (q + 1), :].bitcast(I32),
+                )
+
+        lists = [keep.tile([P, J // PER_COLUMN], U16, name=name) for name in ("src_list", "tgt_list")]
+        nc.sync.dma_start(lists[SOURCE][:], offs)
+        nc.sync.dma_start(lists[TARGET][:], offs2)
+
+        wd_bytes = WORD * PASSES * N
+        tab_sc = placed(late, "tab_sc", [P, T], U8, wd_bytes - ALIGN)
         nc.vector.memset(tab_sc[:].bitcast(I32), 0)
-        for q in range(4):
-            nc.sync.dma_start(
-                tab_sc[32 * q : 32 * q + 8, :].bitcast(I32), tab_scales[:, 4 * q : 4 * q + 4, :].bitcast(I32)
-            )
+        load_two_planes(tab_sc, tab_scales)
 
-        load_words = [PASSES * T, R // 2, R, R // 2, R, PASSES * N, J, 16, T]
-        w_sc_cols = PASSES * R + N
-        zeros = loads.tile([P, sum(load_words)], I32, name="zeros", offset=0, align_bytes=64)
-        nc.vector.memset(zeros[:, : w_sc_cols // 4], 0)
-        ident = sb("ident", [P, P], F32)
-        make_identity(nc, ident[:])
-        w_sc = sb("w_sc", [P, w_sc_cols], U8)
-        nc.vector.tensor_copy(w_sc[:].bitcast(I32), zeros[:, : w_sc_cols // 4])
+        load_words = {"tab_w": PASSES * T, "ws_w0": R // 2, "wt_w0": R, "ws_w1": R // 2, "wt_w1": R, "ident": P, "bias": 2 * T}
+        load_names = list(load_words)
+        load_at = {name: WORD * sum(load_words[n] for n in load_names[:i]) for i, name in enumerate(load_names)}
+        w_sc_words = PASSES * R // WORD
+        zeros = placed(loads, "zeros", [P, sum(load_words[n] for n in load_names)], I32, 0)
+        nc.gpsimd.memset(zeros[:, :w_sc_words], 0)
+        w_sc = sb("w_sc", [P, PASSES * R], U8)
+        nc.vector.tensor_copy(w_sc[:].bitcast(I32), zeros[:, :w_sc_words])
         src_sc1 = sb("src_sc1", [P, J], U8)
         nc.vector.memset(src_sc1[:].bitcast(I32), 0)
 
-        def landing(name, i, shape, dtype):
-            return loads.tile(shape, dtype, name=name, offset=4 * sum(load_words[:i]), align_bytes=64)
+        tab_w = placed(loads, "tab_w", [P, PASSES, T], I32, load_at["tab_w"])
+        ws_w = [placed(loads, f"ws_w{a}", [P, 2 * R], U8, load_at[f"ws_w{a}"]) for a in range(PASSES)]
+        wt_w = [placed(loads, f"wt_w{a}", [P, R], I32, load_at[f"wt_w{a}"]) for a in range(PASSES)]
 
-        tab_w = landing("tab_w", 0, [P, PASSES, T], I32)
-        ws_w = [landing(f"ws_w{a}", 1 + 2 * a, [P, 2 * R], U8) for a in range(PASSES)]
-        wt_w = [landing(f"wt_w{a}", 2 + 2 * a, [P, R], I32) for a in range(PASSES)]
-        wd_raw = landing("wd_raw", 5, [P, PASSES, N], I32)
-        edge_w = landing("edge_w", 6, [P, J], F32)
-        bias = landing("bias", 7, [P, PACK], F32)
-
-        def load_x4(dst, words):
-            nc.sync.dma_start(dst[:], words.rearrange("p c i -> p (c i)").bitcast(I32))
-
-        def load_w_scales(first_row, scales):
-            for q in range(4):
-                rows = slice(32 * q + first_row, 32 * q + first_row + 4)
-                nc.scalar.dma_start(
-                    w_sc[rows, : PASSES * R].bitcast(I32).rearrange("p (a r) -> p a r", a=PASSES),
-                    scales[:, 4 * q : 4 * q + 4, :].rearrange("a q r -> q a r").bitcast(I32),
-                )
-
-        nc.sync.dma_start(tab_w[:], tab_words.rearrange("a p t i -> p a (t i)").bitcast(I32))
-        load_w_scales(0, ws_scales)
-        load_w_scales(4, wt_scales)
-        nc.sync.dma_start(ws_w[0][:].bitcast(I32), ws_words[0].bitcast(I32))
-        load_x4(wt_w[0], wt_words[0])
-        nc.sync.dma_start(ws_w[1][:].bitcast(I32), ws_words[1].bitcast(I32))
-        load_x4(wt_w[1], wt_words[1])
-        nc.sync.dma_start(wd_raw[:], wd_words.rearrange("a p n i -> p a (n i)").bitcast(I32))
-        for q in range(4):
+        def load_w_scales(side, q):
+            first_row = QUAD * q + ROWS * side
             nc.sync.dma_start(
-                w_sc[32 * q : 32 * q + 8, PASSES * R :].bitcast(I32), wd_scales[:, 4 * q : 4 * q + 4, :].bitcast(I32)
+                w_sc[first_row : first_row + ROWS, :].bitcast(I32).rearrange("p (a r) -> p a r", a=PASSES),
+                (ws_scales, wt_scales)[side][:, ROWS * q : ROWS * (q + 1), :].rearrange("a q r -> q a r").bitcast(I32),
             )
-        nc.sync.dma_start(bias[:], b.rearrange("(p t) -> p t", t=PACK))
-        nc.sync.dma_start(edge_w[:], wgo)
+
+        scale_loads = [(side, q) for side in (SOURCE, TARGET) for q in range(QUADRANTS)]
+        for side, q in scale_loads[:AHEAD_OF_TABLE]:
+            load_w_scales(side, q)
+        nc.sync.dma_start(tab_w[:], tab_words.rearrange("a p t i -> p a (t i)").bitcast(I32))
+        for side, q in scale_loads[AHEAD_OF_TABLE:]:
+            load_w_scales(side, q)
+        for a in range(PASSES):
+            nc.sync.dma_start(ws_w[a][:].bitcast(I32), ws_words[a].bitcast(I32))
+            nc.sync.dma_start(wt_w[a][:], wt_words[a].rearrange("p r i -> p (r i)").bitcast(I32))
+        bias = placed(loads, "bias", [P, load_words["bias"]], F32, load_at["bias"])
+        nc.sync.dma_start(bias[:, :PACK], b.rearrange("(p t) -> p t", t=PACK))
+        ident = placed(loads, "ident", [P, P], F32, load_at["ident"])
+        make_identity(nc, ident[:])
 
         pages = []
-        def clear(page):
-            for first in range(0, T, BANK):
-                nc.gpsimd.memset(page[:, first : first + BANK], 0.0)
 
-        pages.append(sb("page0", [P, T], F32))
-        nc.vector.memset(pages[0][:], 0.0)
-        pages.append(landing("page1", 8, [P, T], F32))
-        clear(pages[1])
+        def add_page(page):
+            pages.append(page)
+            nc.vector.memset(page[:].bitcast(I32), 0)
+
+        for t in range(2):
+            add_page(sb(f"page{t}", [P, T], F32))
 
         src_sc = sb("src_sc", [P, J], U8)
         tgt_sc = sb("tgt_sc", [P, J], U8)
+        nc.vector.tensor_copy(src_sc[:], tab_sc[:].indirect(lists[SOURCE][:]))
+        nc.scalar.dma_start(src_sc1[0 : P - ROWS, :].bitcast(I32), src_sc[ROWS:P, :].bitcast(I32))
+        nc.vector.tensor_copy(tgt_sc[:], tab_sc[:].indirect(lists[TARGET][:]))
+
         picked = {}
+        picked_shape = [P, 2 * PASSES, CHUNK]
 
-        def gather_words(c, a, lst, side):
-            nc.vector.tensor_copy(
-                picked[c][:, 2 * a + side, :],
-                tab_w[:, a, :].bitcast(U32).indirect(entries(lst, c * CHUNK, CHUNK)),
-            )
-
-        def gather_chunk(c, tag=None):
-            picked[c] = sb(f"picked{c}", [P, 2 * PASSES, CHUNK], U32, tag)
+        def gather_chunk(c, dst):
+            picked[c] = dst
             for a in range(PASSES):
-                gather_words(c, a, src_list, 0)
-                gather_words(c, a, tgt_list, 1)
+                for side in (SOURCE, TARGET):
+                    nc.vector.tensor_copy(
+                        dst[:, 2 * a + side, :],
+                        tab_w[:, a, :].bitcast(U32).indirect(entries(lists[side], c * CHUNK, CHUNK)),
+                    )
 
-        nc.vector.tensor_copy(src_sc[:], tab_sc[:].indirect(src_list[:]))
-        nc.scalar.dma_start(src_sc1[0 : P - 4, :].bitcast(I32), src_sc[4:P, :].bitcast(I32))
-        picked[0] = sb("picked0", [P, 2 * PASSES, CHUNK], U32)
-        gather_words(0, 0, src_list, 0)
-        nc.vector.tensor_copy(tgt_sc[:, :CHUNK], tab_sc[:].indirect(entries(tgt_list, 0, CHUNK)))
-        gather_words(0, 0, tgt_list, 1)
-        gather_words(0, 1, src_list, 0)
-        gather_words(0, 1, tgt_list, 1)
-        nc.vector.tensor_copy(tgt_sc[:, CHUNK:], tab_sc[:].indirect(entries(tgt_list, CHUNK, J - CHUNK)))
-        gather_chunk(1)
+        gather_chunk(0, placed(dealt, "picked0", picked_shape, U32, 2 * N))
 
-        wd_w = sb("wd_w", [P, PASSES, N], I32)
-        nc.vector.tensor_copy(
-            wd_w[:].rearrange("p a (t c i) -> p a c t i", t=PACK, i=4),
-            wd_raw[:].rearrange("p a (c i t) -> p a c t i", t=PACK, i=4),
-        )
-        wd_sc = sb("wd_sc", [P, N], U8)
-        nc.vector.tensor_copy(
-            wd_sc[:].rearrange("p (t m) -> p t m", t=PACK), w_sc[:, PASSES * R :].rearrange("p (m t) -> p t m", t=PACK)
-        )
-        gather_chunk(2)
+        wd_raw = placed(late, "wd_raw", [P, PASSES, N], I32, 0)
+        wd_sc_raw = placed(late, "wd_sc_raw", [P, N], U8, wd_bytes)
+        edge_w = placed(late, "edge_w", [P, J], F32, wd_bytes + N)
+        nc.vector.memset(wd_sc_raw[:].bitcast(I32), 0)
+        nc.sync.dma_start(wd_raw[:], wd_words.rearrange("a p n i -> p a (n i)").bitcast(I32))
+        load_two_planes(wd_sc_raw, wd_scales)
+        nc.sync.dma_start(edge_w[:], wgo)
 
-        def first_pass(acc, blk, half, a, side):
-            c, cols = blk // 2, slice(P * (blk % 2), P * (blk % 2 + 1))
-            edges = slice(P * blk, P * (blk + 1))
-            r_cols = slice(a * R + half * BANK, a * R + (half + 1) * BANK)
-            if side == 0:
+        for c in range(1, CHUNKS - 1):
+            gather_chunk(c, sb(f"picked{c}", picked_shape, U32))
+
+        def first_banks(group):
+            return [
+                psum.tile([P, BANK], F32, name=f"a{group}_{half}", tag=f"first{2 * (group % 2) + half}")
+                for half in range(2)
+            ]
+
+        def first_pass(acc, group, half, a, side):
+            in_chunk = slice(P * (group % 2), P * (group % 2 + 1))
+            edges = slice(P * group, P * (group + 1))
+            plane_cols = slice(a * R + half * BANK, a * R + (half + 1) * BANK)
+            if side == SOURCE:
                 v_scale = (src_sc, src_sc1)[a][:, edges]
                 w = ws_w[a][:, 2 * half * BANK : 2 * (half + 1) * BANK].bitcast(FP4X4)
-                w_scale = w_sc[:, r_cols]
+                w_scale = w_sc[:, plane_cols]
             else:
-                v_scale = tgt_sc[4 * a : P, edges]
+                v_scale = tgt_sc[ROWS * a : P, edges]
                 w = wt_w[a][:, half * BANK : (half + 1) * BANK].bitcast(FP8X4)
-                w_scale = w_sc[4:P, r_cols]
+                w_scale = w_sc[ROWS:P, plane_cols]
             nc.tensor.matmul_mx(
-                out=acc[:], lhsT=picked[c][:, 2 * a + side, cols].bitcast(FP8X4), lhsT_scale=v_scale,
-                rhs=w, rhs_scale=w_scale, start=(a == 0 and side == 0), stop=(a == 1 and side == 1),
+                out=acc[:], lhsT=picked[group // 2][:, 2 * a + side, in_chunk].bitcast(FP8X4), lhsT_scale=v_scale,
+                rhs=w, rhs_scale=w_scale,
+                start=(a == 0 and side == SOURCE), stop=(a == PASSES - 1 and side == TARGET),
             )
 
-        order = [(a, side) for a in range(PASSES) for side in range(2)]
-
-        def first_banks(blk):
-            return [psum.tile([P, BANK], F32, name=f"a{blk}_{h}", tag=f"first{2 * (blk % 2) + h}") for h in range(2)]
-
-        def turn(blk, banks, h_in):
-            h_t = ring.tile([P, R], BF16, name=f"h_t{blk}", tag="h_t", align_bytes=64)
+        def turn(group, banks, h_in):
+            h_t = ring.tile([P, R], BF16, name=f"h_t{group}", tag="h_t", align_bytes=ALIGN)
             for half in range(2):
                 nc.scalar.activation(
                     h_t[:, half * BANK : (half + 1) * BANK].rearrange("j (u p e) -> j u p e", u=2, e=2),
                     banks[half][:].rearrange("j (p u e) -> j u p e", u=2, e=2),
                     ACT.Relu,
                 )
-            turned = psum.tile([P, BANK], F32, name=f"turned{blk}", tag=f"turn{blk % 2}")
-            for s in range(4):
+            turned = psum.tile([P, BANK], F32, name=f"turned{group}", tag=f"turn{group % 2}")
+            for s in range(2 * PASSES):
                 nc.tensor.transpose(turned[:, P * s : P * (s + 1)], h_t[:].bitcast(F32)[:, P * s : P * (s + 1)], ident[:])
+            h_words = h_in[:].bitcast(F32).rearrange("p (a j u) -> p a j u", a=PASSES, u=2)
             nc.scalar.copy(
-                h_in[:].bitcast(F32).rearrange("p (a j u) -> p a j u", a=PASSES, u=2)[:, :, P * (blk % 2) : P * (blk % 2 + 1), :],
+                h_words[:, :, P * (group % 2) : P * (group % 2 + 1), :],
                 turned[:].rearrange("p (a u j) -> p a j u", a=PASSES, u=2),
             )
 
@@ -197,7 +198,7 @@ def tile_list_msg_relu_biasP_kernel(
             for a in range(PASSES):
                 nc.tensor.matmul_mx(
                     out=acc, lhsT=wd_w[:, a, P * t : P * (t + 1)].bitcast(FP8X4),
-                    lhsT_scale=wd_sc[4 * a : P, P * t : P * (t + 1)],
+                    lhsT_scale=wd_sc[ROWS * a : P, P * t : P * (t + 1)],
                     rhs=h_w[c][:, a * CHUNK : (a + 1) * CHUNK].bitcast(FP8X4),
                     rhs_scale=h_sc[c][:, a * CHUNK : (a + 1) * CHUNK],
                     start=(a == 0), stop=(a == PASSES - 1),
@@ -208,85 +209,112 @@ def tile_list_msg_relu_biasP_kernel(
 
         def scatter(t, first, count):
             nc.vector.tensor_tensor(
-                pages[t][:].indirect(entries(tgt_list, first, count)),
+                pages[t][:].indirect(entries(lists[TARGET], first, count)),
                 msg[t][:, first : first + count], edge_w[:, first : first + count], MULT,
             )
 
-        def late_slice(c):
-            acc = psum.tile([P, BANK], F32, name=f"late{c}", tag="turn1")
-            second(acc[:, :CHUNK], c, 2)
-            add_bias(acc[:, :CHUNK], 2, c * CHUNK, CHUNK)
-            scatter(2, c * CHUNK, CHUNK)
-
-        for c in range(CHUNKS):
-            h_in = sb(f"h_in{c}", [P, PASSES * CHUNK * PACK], BF16)
-            blocks = (2 * c, 2 * c + 1)
-            if c == 0:
-                banks = {blk: first_banks(blk) for blk in blocks}
-                for side in range(2):
-                    for blk in blocks:
-                        for half in range(2):
-                            first_pass(banks[blk][half], blk, half, 0, side)
-                for blk in blocks:
-                    for half in range(2):
-                        for side in range(2):
-                            first_pass(banks[blk][half], blk, half, 1, side)
-                    turn(blk, banks[blk], h_in)
-            else:
-                for blk in blocks:
-                    pair = first_banks(blk)
-                    for half in range(2):
-                        for a, side in order:
-                            first_pass(pair[half], blk, half, a, side)
-                    turn(blk, pair, h_in)
-            h_w[c] = sb(f"h_w{c}", [P, PASSES * CHUNK], U32)
-            h_sc[c] = sb(f"h_sc{c}", [P, PASSES * CHUNK], U8)
-            nc.vector.quantize_mx(out=h_w[c][:].bitcast(FP8X4), scales=h_sc[c][:], in_=h_in[:])
-            if c == 0:
-                gather_chunk(CHUNKS - 1, "h_in0")
-                for t in range(2, PACK):
-                    pages.append(loads.tile([P, T], F32, name=f"page{t}", offset=4 * T * (t - 2), align_bytes=64))
-                    clear(pages[t])
-            else:
-                late_slice(c - 1)
+        def pages_0_and_1(c):
             acc = psum.tile([P, BANK], F32, name=f"early{c}", tag="second0")
             for t in range(2):
                 second(acc[:, t * CHUNK : (t + 1) * CHUNK], c, t)
             for t in range(2):
                 add_bias(acc[:, t * CHUNK : (t + 1) * CHUNK], t, c * CHUNK, CHUNK)
                 scatter(t, c * CHUNK, CHUNK)
-        late_slice(CHUNKS - 1)
-        for c in range(0, CHUNKS, 2):
-            acc = psum.tile([P, BANK], F32, name=f"last{c}", tag="second1")
+
+        def page_2(c):
+            acc = psum.tile([P, BANK], F32, name=f"y{c}_2", tag="turn1")
+            second(acc[:, :CHUNK], c, 2)
+            add_bias(acc[:, :CHUNK], 2, c * CHUNK, CHUNK)
+            scatter(2, c * CHUNK, CHUNK)
+
+        for c in range(CHUNKS):
+            h_in = sb(f"h_in{c}", [P, PASSES * CHUNK * PACK], BF16)
+            groups = (2 * c, 2 * c + 1)
+            if c == 0:
+                banks = {group: first_banks(group) for group in groups}
+                for side in (SOURCE, TARGET):
+                    for group in groups:
+                        for half in range(2):
+                            first_pass(banks[group][half], group, half, 0, side)
+                for group in groups:
+                    for half in range(2):
+                        for side in (SOURCE, TARGET):
+                            first_pass(banks[group][half], group, half, 1, side)
+                    turn(group, banks[group], h_in)
+                wd_w = placed(dealt, "wd_w", [P, PASSES, N], I32, 0)
+                nc.vector.tensor_copy(
+                    wd_w[:].rearrange("p a (t g i) -> p a g t i", t=PACK, i=4),
+                    wd_raw[:].rearrange("p a (g i t) -> p a g t i", t=PACK, i=4),
+                )
+                wd_sc = placed(dealt, "wd_sc", [P, N], U8, wd_bytes)
+                nc.vector.tensor_copy(
+                    wd_sc[:].rearrange("p (t m) -> p t m", t=PACK), wd_sc_raw[:].rearrange("p (m t) -> p t m", t=PACK)
+                )
+                add_page(placed(dealt, "page2", [P, T], F32, wd_bytes + N))
+            else:
+                for group in groups:
+                    group_banks = first_banks(group)
+                    for half in range(2):
+                        for a in range(PASSES):
+                            for side in (SOURCE, TARGET):
+                                first_pass(group_banks[half], group, half, a, side)
+                    turn(group, group_banks, h_in)
+            h_w[c] = sb(f"h_w{c}", [P, PASSES * CHUNK], U32)
+            h_sc[c] = sb(f"h_sc{c}", [P, PASSES * CHUNK], U8)
+            nc.vector.quantize_mx(out=h_w[c][:].bitcast(FP8X4), scales=h_sc[c][:], in_=h_in[:])
+            if c == 0:
+                gather_chunk(CHUNKS - 1, sb(f"picked{CHUNKS - 1}", picked_shape, U32, "h_in0"))
+            else:
+                if c == 1:
+                    add_page(sb("page3", [P, T], F32, "h_in1"))
+                page_2(c - 1)
+            pages_0_and_1(c)
+        page_2(CHUNKS - 1)
+
+        for half in range(2):
+            acc = psum.tile([P, BANK], F32, name=f"last{2 * half}", tag=f"first{2 + half}")
             for i in range(2):
-                second(acc[:, i * CHUNK : (i + 1) * CHUNK], c + i, 3)
-            add_bias(acc[:], 3, c * CHUNK, 2 * CHUNK)
+                second(acc[:, i * CHUNK : (i + 1) * CHUNK], 2 * half + i, 3)
+            add_bias(acc[:], 3, half * BANK, BANK)
         scatter(3, 0, J)
 
         out_rows = out_0.rearrange("(p t) c -> p t c", t=PACK)
         starts = [sum(OUT_WIDTHS[:i]) for i in range(len(OUT_WIDTHS))]
-        pairs = [sb(f"pairs{i}", [P, 2, w, 2], BF16) for i, w in enumerate(OUT_WIDTHS)]
+        pairs = [
+            placed(loads, f"pairs{i}", [P, 2, w, 2], BF16, load_at["bias"] + 2 * WORD * starts[i])
+            for i, w in enumerate(OUT_WIDTHS)
+        ]
         for t in range(PACK):
             nc.sync.dma_start(out_rows[:, t, :], pages[t][:])
             for i, w in enumerate(OUT_WIDTHS):
-                nc.scalar.copy(pairs[i][:, t // 2, :, t % 2], pages[t][:, starts[i] : starts[i] + w])
+                round_copy = nc.vector.tensor_copy if i == 0 and t >= 2 else nc.scalar.copy
+                round_copy(pairs[i][:, t // 2, :, t % 2], pages[t][:, starts[i] : starts[i] + w])
+
         out_sc = sb("out_sc", [P, T], U8)
         out_words = out_1[0].rearrange("p t i -> p (t i)").bitcast(I32)
+        last_piece = len(OUT_WIDTHS) - 1
         woven = []
-        for i in range(len(OUT_WIDTHS) + 1):
-            if i < len(OUT_WIDTHS):
-                w = OUT_WIDTHS[i]
-                woven.append(sb(f"woven{i}", [P, w * PACK], BF16))
-                nc.vector.tensor_copy(
-                    woven[i][:].bitcast(F32).rearrange("p (c u) -> p c u", u=2),
-                    pairs[i][:].rearrange("p u c e -> p u (c e)").bitcast(F32).rearrange("p u c -> p c u"),
-                )
-            if i > 0:
-                w, cols = OUT_WIDTHS[i - 1], slice(starts[i - 1], starts[i - 1] + OUT_WIDTHS[i - 1])
-                codes = sb(f"codes{i}", [P, w], I32)
-                nc.vector.quantize_mx(out=codes[:].bitcast(FP8X4), scales=out_sc[:, cols], in_=woven[i - 1][:])
-                nc.sync.dma_start(out_words[:, cols], codes[:])
-        for q in range(4):
+
+        def weave(i):
+            woven.append(sb(f"woven{i}", [P, OUT_WIDTHS[i] * PACK], BF16))
+            word_copy = nc.vector.tensor_copy if i < last_piece else nc.scalar.copy
+            word_copy(
+                woven[i][:].bitcast(F32).rearrange("p (c u) -> p c u", u=2),
+                pairs[i][:].rearrange("p u c e -> p u (c e)").bitcast(F32).rearrange("p u c -> p c u"),
+            )
+
+        def quantise_piece(i):
+            cols = slice(starts[i], starts[i] + OUT_WIDTHS[i])
+            codes = sb(f"codes{i + 1}", [P, OUT_WIDTHS[i]], I32)
+            nc.vector.quantize_mx(out=codes[:].bitcast(FP8X4), scales=out_sc[:, cols], in_=woven[i][:])
+            nc.sync.dma_start(out_words[:, cols], codes[:])
+
+        weave(0)
+        for i in range(last_piece):
+            weave(i + 1)
+            quantise_piece(i)
+        quantise_piece(last_piece)
+        for q in range(QUADRANTS):
             nc.scalar.dma_start(
-                out_2[0, 4 * q : 4 * q + 4, :].bitcast(I32), out_sc[32 * q : 32 * q + 4, :].bitcast(I32)
+                out_2[0, ROWS * q : ROWS * (q + 1), :].bitcast(I32), out_sc[QUAD * q : QUAD * q + ROWS, :].bitcast(I32)
             )

@@ -31,6 +31,7 @@ WORD = 4
 ALIGN = 64
 SOURCE, TARGET = 0, 1
 
+ORDER = ((0, SOURCE), (0, TARGET), (1, TARGET), (1, SOURCE))
 AHEAD_OF_TABLE = 3
 OUT_WIDTHS = (256, 512, 512, 512, 256)
 
@@ -46,7 +47,6 @@ def tile_list_msg_relu_biasP_kernel(
         loads = ctx.enter_context(tc.tile_pool(name="loads", bufs=1))
         late = ctx.enter_context(tc.tile_pool(name="late", bufs=1))
         dealt = ctx.enter_context(tc.tile_pool(name="dealt", bufs=1))
-        ring = ctx.enter_context(tc.tile_pool(name="ring", bufs=2))
         psum = ctx.enter_context(tc.psum_pool(name="psum", bufs=1))
 
         def sb(name, shape, dtype, tag=None):
@@ -80,8 +80,9 @@ def tile_list_msg_relu_biasP_kernel(
         w_sc_words = PASSES * R // WORD
         zeros = placed(loads, "zeros", [P, sum(load_words[n] for n in load_names)], I32, 0)
         nc.gpsimd.memset(zeros[:, :w_sc_words], 0)
-        w_sc = sb("w_sc", [P, PASSES * R], U8)
-        nc.vector.tensor_copy(w_sc[:].bitcast(I32), zeros[:, :w_sc_words])
+        w_sc = [sb(f"w_sc{side}", [P, PASSES * R], U8) for side in (SOURCE, TARGET)]
+        nc.vector.tensor_copy(w_sc[SOURCE][:].bitcast(I32), zeros[:, :w_sc_words])
+        nc.vector.memset(w_sc[TARGET][:].bitcast(I32), 0)
         src_sc1 = sb("src_sc1", [P, J], U8)
         nc.vector.memset(src_sc1[:].bitcast(I32), 0)
 
@@ -90,21 +91,28 @@ def tile_list_msg_relu_biasP_kernel(
         wt_w = [placed(loads, f"wt_w{a}", [P, R], I32, load_at[f"wt_w{a}"]) for a in range(PASSES)]
 
         def load_w_scales(side, q):
-            first_row = QUAD * q + ROWS * side
+            first_row = QUAD * q
             nc.sync.dma_start(
-                w_sc[first_row : first_row + ROWS, :].bitcast(I32).rearrange("p (a r) -> p a r", a=PASSES),
+                w_sc[side][first_row : first_row + ROWS, :].bitcast(I32).rearrange("p (a r) -> p a r", a=PASSES),
                 (ws_scales, wt_scales)[side][:, ROWS * q : ROWS * (q + 1), :].rearrange("a q r -> q a r").bitcast(I32),
             )
 
-        scale_loads = [(side, q) for side in (SOURCE, TARGET) for q in range(QUADRANTS)]
-        for side, q in scale_loads[:AHEAD_OF_TABLE]:
-            load_w_scales(side, q)
         nc.sync.dma_start(tab_w[:], tab_words.rearrange("a p t i -> p a (t i)").bitcast(I32))
-        for side, q in scale_loads[AHEAD_OF_TABLE:]:
-            load_w_scales(side, q)
-        for a in range(PASSES):
+        for q in range(QUADRANTS):
+            load_w_scales(SOURCE, q)
+
+        def load_ws(a):
             nc.sync.dma_start(ws_w[a][:].bitcast(I32), ws_words[a].bitcast(I32))
+
+        def load_wt(a):
             nc.sync.dma_start(wt_w[a][:], wt_words[a].rearrange("p r i -> p (r i)").bitcast(I32))
+
+        load_ws(0)
+        load_wt(0)
+        for q in range(QUADRANTS):
+            load_w_scales(TARGET, q)
+        load_wt(1)
+        load_ws(1)
         bias = placed(loads, "bias", [P, load_words["bias"]], F32, load_at["bias"])
         nc.sync.dma_start(bias[:, :PACK], b.rearrange("(p t) -> p t", t=PACK))
         ident = placed(loads, "ident", [P, P], F32, load_at["ident"])
@@ -113,8 +121,9 @@ def tile_list_msg_relu_biasP_kernel(
         pages = []
 
         def add_page(page):
+            engine = nc.vector if len(pages) < 2 else nc.gpsimd
             pages.append(page)
-            nc.vector.memset(page[:].bitcast(I32), 0)
+            engine.memset(page[:].bitcast(I32), 0)
 
         for t in range(2):
             add_page(sb(f"page{t}", [P, T], F32))
@@ -122,7 +131,11 @@ def tile_list_msg_relu_biasP_kernel(
         src_sc = sb("src_sc", [P, J], U8)
         tgt_sc = sb("tgt_sc", [P, J], U8)
         nc.vector.tensor_copy(src_sc[:], tab_sc[:].indirect(lists[SOURCE][:]))
-        nc.scalar.dma_start(src_sc1[0 : P - ROWS, :].bitcast(I32), src_sc[ROWS:P, :].bitcast(I32))
+        for q in range(QUADRANTS):
+            nc.sync.dma_start(
+                src_sc1[QUAD * q : QUAD * q + ROWS, :].bitcast(I32),
+                src_sc[QUAD * q + ROWS : QUAD * q + 2 * ROWS, :].bitcast(I32),
+            )
         nc.vector.tensor_copy(tgt_sc[:], tab_sc[:].indirect(lists[TARGET][:]))
 
         picked = {}
@@ -130,12 +143,11 @@ def tile_list_msg_relu_biasP_kernel(
 
         def gather_chunk(c, dst):
             picked[c] = dst
-            for a in range(PASSES):
-                for side in (SOURCE, TARGET):
-                    nc.vector.tensor_copy(
-                        dst[:, 2 * a + side, :],
-                        tab_w[:, a, :].bitcast(U32).indirect(entries(lists[side], c * CHUNK, CHUNK)),
-                    )
+            for a, side in ORDER:
+                nc.vector.tensor_copy(
+                    dst[:, 2 * a + side, :],
+                    tab_w[:, a, :].bitcast(U32).indirect(entries(lists[side], c * CHUNK, CHUNK)),
+                )
 
         gather_chunk(0, placed(dealt, "picked0", picked_shape, U32, 2 * N))
 
@@ -163,28 +175,38 @@ def tile_list_msg_relu_biasP_kernel(
             if side == SOURCE:
                 v_scale = (src_sc, src_sc1)[a][:, edges]
                 w = ws_w[a][:, 2 * half * BANK : 2 * (half + 1) * BANK].bitcast(FP4X4)
-                w_scale = w_sc[:, plane_cols]
+                w_scale = w_sc[SOURCE][:, plane_cols]
             else:
                 v_scale = tgt_sc[ROWS * a : P, edges]
                 w = wt_w[a][:, half * BANK : (half + 1) * BANK].bitcast(FP8X4)
-                w_scale = w_sc[ROWS:P, plane_cols]
+                w_scale = w_sc[TARGET][:, plane_cols]
             nc.tensor.matmul_mx(
                 out=acc[:], lhsT=picked[group // 2][:, 2 * a + side, in_chunk].bitcast(FP8X4), lhsT_scale=v_scale,
                 rhs=w, rhs_scale=w_scale,
-                start=(a == 0 and side == SOURCE), stop=(a == PASSES - 1 and side == TARGET),
+                start=((a, side) == ORDER[0]), stop=((a, side) == ORDER[-1]),
             )
 
-        def turn(group, banks, h_in):
-            h_t = ring.tile([P, R], BF16, name=f"h_t{group}", tag="h_t", align_bytes=ALIGN)
-            for half in range(2):
-                nc.scalar.activation(
-                    h_t[:, half * BANK : (half + 1) * BANK].rearrange("j (u p e) -> j u p e", u=2, e=2),
-                    banks[half][:].rearrange("j (p u e) -> j u p e", u=2, e=2),
-                    ACT.Relu,
-                )
+        h_ts = {}
+
+        def first_half(group, half, order):
+            acc = psum.tile([P, BANK], F32, name=f"a{group}_{half}", tag=f"first{2 * (group % 2) + half}")
+            for a, side in order:
+                first_pass(acc, group, half, a, side)
+            relu(group, half, acc)
+
+        def relu(group, half, acc):
+            if group not in h_ts:
+                h_ts[group] = sb(f"h_t{group}", [P, R], BF16)
+            nc.scalar.activation(
+                h_ts[group][:, half * BANK : (half + 1) * BANK].rearrange("j (u p e) -> j u p e", u=2, e=2),
+                acc[:].rearrange("j (p u e) -> j u p e", u=2, e=2),
+                ACT.Relu,
+            )
+
+        def turn(group, h_in):
             turned = psum.tile([P, BANK], F32, name=f"turned{group}", tag=f"turn{group % 2}")
             for s in range(2 * PASSES):
-                nc.tensor.transpose(turned[:, P * s : P * (s + 1)], h_t[:].bitcast(F32)[:, P * s : P * (s + 1)], ident[:])
+                nc.tensor.transpose(turned[:, P * s : P * (s + 1)], h_ts[group][:].bitcast(F32)[:, P * s : P * (s + 1)], ident[:])
             h_words = h_in[:].bitcast(F32).rearrange("p (a j u) -> p a j u", a=PASSES, u=2)
             nc.scalar.copy(
                 h_words[:, :, P * (group % 2) : P * (group % 2 + 1), :],
@@ -192,7 +214,6 @@ def tile_list_msg_relu_biasP_kernel(
             )
 
         h_w, h_sc = {}, {}
-        msg = [sb(f"msg{t}", [P, J], F32) for t in range(PACK)]
 
         def second(acc, c, t):
             for a in range(PASSES):
@@ -204,79 +225,88 @@ def tile_list_msg_relu_biasP_kernel(
                     start=(a == 0), stop=(a == PASSES - 1),
                 )
 
-        def add_bias(acc, t, first, count):
-            nc.scalar.activation(msg[t][:, first : first + count], acc, ACT.Identity, bias=bias[:, t : t + 1])
+        def add_bias(dst, acc, t):
+            nc.scalar.activation(dst, acc, ACT.Identity, bias=bias[:, t : t + 1])
 
-        def scatter(t, first, count):
+        def scatter(t, first, count, src):
             nc.vector.tensor_tensor(
-                pages[t][:].indirect(entries(lists[TARGET], first, count)),
-                msg[t][:, first : first + count], edge_w[:, first : first + count], MULT,
+                pages[t][:].indirect(entries(lists[TARGET], first, count)), src, edge_w[:, first : first + count], MULT,
             )
 
-        def pages_0_and_1(c):
+        msg3 = sb("msg3", [P, J], F32)
+        held = {}
+
+        def second_stage(c):
             acc = psum.tile([P, BANK], F32, name=f"early{c}", tag="second0")
+            acc2 = psum.tile([P, BANK], F32, name=f"lag{c}", tag="second1")
             for t in range(2):
                 second(acc[:, t * CHUNK : (t + 1) * CHUNK], c, t)
+            second(acc2[:, :CHUNK], c, 2)
+            if c == CHUNKS - 1:
+                second(acc2[:, CHUNK:], c, 3)
             for t in range(2):
-                add_bias(acc[:, t * CHUNK : (t + 1) * CHUNK], t, c * CHUNK, CHUNK)
-                scatter(t, c * CHUNK, CHUNK)
+                m = sb(f"msg{c}_{t}", [P, CHUNK], F32)
+                add_bias(m[:], acc[:, t * CHUNK : (t + 1) * CHUNK], t)
+                scatter(t, c * CHUNK, CHUNK, m[:])
+            held[c] = acc2
 
-        def page_2(c):
-            acc = psum.tile([P, BANK], F32, name=f"y{c}_2", tag="turn1")
-            second(acc[:, :CHUNK], c, 2)
-            add_bias(acc[:, :CHUNK], 2, c * CHUNK, CHUNK)
-            scatter(2, c * CHUNK, CHUNK)
+        def page_2(c, tag):
+            m = sb(f"msg{c}_2", [P, CHUNK], F32, tag)
+            add_bias(m[:], held[c][:, :CHUNK], 2)
+            scatter(2, c * CHUNK, CHUNK, m[:])
 
-        for c in range(CHUNKS):
+        def quantise_h(c):
             h_in = sb(f"h_in{c}", [P, PASSES * CHUNK * PACK], BF16)
-            groups = (2 * c, 2 * c + 1)
-            if c == 0:
-                banks = {group: first_banks(group) for group in groups}
-                for side in (SOURCE, TARGET):
-                    for group in groups:
-                        for half in range(2):
-                            first_pass(banks[group][half], group, half, 0, side)
-                for group in groups:
-                    for half in range(2):
-                        for side in (SOURCE, TARGET):
-                            first_pass(banks[group][half], group, half, 1, side)
-                    turn(group, banks[group], h_in)
-                wd_w = placed(dealt, "wd_w", [P, PASSES, N], I32, 0)
-                nc.vector.tensor_copy(
-                    wd_w[:].rearrange("p a (t g i) -> p a g t i", t=PACK, i=4),
-                    wd_raw[:].rearrange("p a (g i t) -> p a g t i", t=PACK, i=4),
-                )
-                wd_sc = placed(dealt, "wd_sc", [P, N], U8, wd_bytes)
-                nc.vector.tensor_copy(
-                    wd_sc[:].rearrange("p (t m) -> p t m", t=PACK), wd_sc_raw[:].rearrange("p (m t) -> p t m", t=PACK)
-                )
-                add_page(placed(dealt, "page2", [P, T], F32, wd_bytes + N))
-            else:
-                for group in groups:
-                    group_banks = first_banks(group)
-                    for half in range(2):
-                        for a in range(PASSES):
-                            for side in (SOURCE, TARGET):
-                                first_pass(group_banks[half], group, half, a, side)
-                    turn(group, group_banks, h_in)
+            for group in (2 * c, 2 * c + 1):
+                turn(group, h_in)
             h_w[c] = sb(f"h_w{c}", [P, PASSES * CHUNK], U32)
             h_sc[c] = sb(f"h_sc{c}", [P, PASSES * CHUNK], U8)
             nc.vector.quantize_mx(out=h_w[c][:].bitcast(FP8X4), scales=h_sc[c][:], in_=h_in[:])
+            if c > 0:
+                page_2(c - 1, f"h_t{2 * c + 1}")
             if c == 0:
                 gather_chunk(CHUNKS - 1, sb(f"picked{CHUNKS - 1}", picked_shape, U32, "h_in0"))
-            else:
-                if c == 1:
-                    add_page(sb("page3", [P, T], F32, "h_in1"))
-                page_2(c - 1)
-            pages_0_and_1(c)
-        page_2(CHUNKS - 1)
+                add_page(placed(loads, "page2", [P, T], F32, load_at["tab_w"]))
+            if c == 1:
+                add_page(sb("page3", [P, T], F32, "h_in1"))
 
-        for half in range(2):
-            acc = psum.tile([P, BANK], F32, name=f"last{2 * half}", tag=f"first{2 + half}")
-            for i in range(2):
-                second(acc[:, i * CHUNK : (i + 1) * CHUNK], 2 * half + i, 3)
-            add_bias(acc[:], 3, half * BANK, BANK)
-        scatter(3, 0, J)
+        order = ORDER
+        banks = {group: first_banks(group) for group in (0, 1)}
+        for a, side in ORDER[:2]:
+            for group in (0, 1):
+                for half in range(2):
+                    first_pass(banks[group][half], group, half, a, side)
+        for group in (0, 1):
+            for half in range(2):
+                for a, side in ORDER[2:]:
+                    first_pass(banks[group][half], group, half, a, side)
+                relu(group, half, banks[group][half])
+        wd_w = placed(dealt, "wd_w", [P, PASSES, N], I32, 0)
+        nc.vector.tensor_copy(
+            wd_w[:].rearrange("p a (t g i) -> p a g t i", t=PACK, i=4),
+            wd_raw[:].rearrange("p a (g i t) -> p a g t i", t=PACK, i=4),
+        )
+        wd_sc = placed(dealt, "wd_sc", [P, N], U8, wd_bytes)
+        nc.vector.tensor_copy(
+            wd_sc[:].rearrange("p (t m) -> p t m", t=PACK), wd_sc_raw[:].rearrange("p (m t) -> p t m", t=PACK)
+        )
+        for c in range(CHUNKS - 1):
+            first_half(2 * c + 2, 0, order)
+            quantise_h(c)
+            first_half(2 * c + 2, 1, order)
+            first_half(2 * c + 3, 0, order)
+            second_stage(c)
+            first_half(2 * c + 3, 1, order)
+        quantise_h(CHUNKS - 1)
+        for half, chunks in enumerate(((0, 1), (2,))):
+            acc = psum.tile([P, BANK], F32, name=f"last{half}", tag=f"first{half}")
+            for i, c in enumerate(chunks):
+                second(acc[:, i * CHUNK : (i + 1) * CHUNK], c, 3)
+            add_bias(msg3[:, half * BANK : half * BANK + CHUNK * len(chunks)], acc[:, : CHUNK * len(chunks)], 3)
+        second_stage(CHUNKS - 1)
+        page_2(CHUNKS - 1, None)
+        add_bias(msg3[:, J - CHUNK :], held[CHUNKS - 1][:, CHUNK:], 3)
+        scatter(3, 0, J, msg3[:])
 
         out_rows = out_0.rearrange("(p t) c -> p t c", t=PACK)
         starts = [sum(OUT_WIDTHS[:i]) for i in range(len(OUT_WIDTHS))]

@@ -33,7 +33,8 @@ SOURCE, TARGET = 0, 1
 
 ORDER = ((0, SOURCE), (0, TARGET), (1, TARGET), (1, SOURCE))
 AHEAD_OF_TABLE = 3
-OUT_WIDTHS = (256, 512, 512, 512, 256)
+OUT_WIDTHS = (256, 256, 512, 512, 256, 256)
+SCALAR_WEAVES = 2
 
 
 def tile_list_msg_relu_biasP_kernel(
@@ -45,7 +46,7 @@ def tile_list_msg_relu_biasP_kernel(
     with ExitStack() as ctx:
         keep = ctx.enter_context(tc.tile_pool(name="keep", bufs=1))
         loads = ctx.enter_context(tc.tile_pool(name="loads", bufs=1))
-        late = ctx.enter_context(tc.tile_pool(name="late", bufs=1))
+        second_half = ctx.enter_context(tc.tile_pool(name="second_half", bufs=1))
         dealt = ctx.enter_context(tc.tile_pool(name="dealt", bufs=1))
         psum = ctx.enter_context(tc.psum_pool(name="psum", bufs=1))
 
@@ -70,11 +71,11 @@ def tile_list_msg_relu_biasP_kernel(
         nc.sync.dma_start(lists[TARGET][:], offs2)
 
         wd_bytes = WORD * PASSES * N
-        tab_sc = placed(late, "tab_sc", [P, T], U8, wd_bytes - ALIGN)
+        tab_sc = sb("tab_sc", [P, T], U8)
         nc.vector.memset(tab_sc[:].bitcast(I32), 0)
         load_two_planes(tab_sc, tab_scales)
 
-        load_words = {"tab_w": PASSES * T, "ws_w0": R // 2, "wt_w0": R, "ws_w1": R // 2, "wt_w1": R, "ident": P, "bias": 2 * T}
+        load_words = {"tab_w0": T, "tab_w1": T, "ws_w0": R // 2, "wt_w0": R, "ws_w1": R // 2, "wt_w1": R, "ident": P, "wd_raw": PASSES * N, "wd_sc_raw": N // WORD, "edge_w": J, "bias": 2 * T}
         load_names = list(load_words)
         load_at = {name: WORD * sum(load_words[n] for n in load_names[:i]) for i, name in enumerate(load_names)}
         w_sc_words = PASSES * R // WORD
@@ -86,7 +87,7 @@ def tile_list_msg_relu_biasP_kernel(
         src_sc1 = sb("src_sc1", [P, J], U8)
         nc.vector.memset(src_sc1[:].bitcast(I32), 0)
 
-        tab_w = placed(loads, "tab_w", [P, PASSES, T], I32, load_at["tab_w"])
+        tab_w = [placed(loads, f"tab_w{a}", [P, T], I32, load_at[f"tab_w{a}"]) for a in range(PASSES)]
         ws_w = [placed(loads, f"ws_w{a}", [P, 2 * R], U8, load_at[f"ws_w{a}"]) for a in range(PASSES)]
         wt_w = [placed(loads, f"wt_w{a}", [P, R], I32, load_at[f"wt_w{a}"]) for a in range(PASSES)]
 
@@ -97,7 +98,10 @@ def tile_list_msg_relu_biasP_kernel(
                 (ws_scales, wt_scales)[side][:, ROWS * q : ROWS * (q + 1), :].rearrange("a q r -> q a r").bitcast(I32),
             )
 
-        nc.sync.dma_start(tab_w[:], tab_words.rearrange("a p t i -> p a (t i)").bitcast(I32))
+        def load_tab(a):
+            nc.sync.dma_start(tab_w[a][:], tab_words[a].rearrange("p t i -> p (t i)").bitcast(I32))
+
+        load_tab(0)
         for q in range(QUADRANTS):
             load_w_scales(SOURCE, q)
 
@@ -111,6 +115,7 @@ def tile_list_msg_relu_biasP_kernel(
         load_wt(0)
         for q in range(QUADRANTS):
             load_w_scales(TARGET, q)
+        load_tab(1)
         load_wt(1)
         load_ws(1)
         bias = placed(loads, "bias", [P, load_words["bias"]], F32, load_at["bias"])
@@ -129,38 +134,49 @@ def tile_list_msg_relu_biasP_kernel(
             add_page(sb(f"page{t}", [P, T], F32))
 
         src_sc = sb("src_sc", [P, J], U8)
-        tgt_sc = sb("tgt_sc", [P, J], U8)
         nc.vector.tensor_copy(src_sc[:], tab_sc[:].indirect(lists[SOURCE][:]))
         for q in range(QUADRANTS):
             nc.sync.dma_start(
                 src_sc1[QUAD * q : QUAD * q + ROWS, :].bitcast(I32),
                 src_sc[QUAD * q + ROWS : QUAD * q + 2 * ROWS, :].bitcast(I32),
             )
-        nc.vector.tensor_copy(tgt_sc[:], tab_sc[:].indirect(lists[TARGET][:]))
+        HALF = J // 2
+        part_bytes = WORD * CHUNK
+        tgt_sc = [sb("tgt_sc0", [P, HALF], U8)]
+        nc.vector.tensor_copy(tgt_sc[0][:], tab_sc[:].indirect(entries(lists[TARGET], 0, HALF)))
 
         picked = {}
-        picked_shape = [P, 2 * PASSES, CHUNK]
+
+        def gather(c, a, side, dst):
+            picked[c, a, side] = dst
+            nc.vector.tensor_copy(dst, tab_w[a][:].bitcast(U32).indirect(entries(lists[side], c * CHUNK, CHUNK)))
 
         def gather_chunk(c, dst):
-            picked[c] = dst
-            for a, side in ORDER:
-                nc.vector.tensor_copy(
-                    dst[:, 2 * a + side, :],
-                    tab_w[:, a, :].bitcast(U32).indirect(entries(lists[side], c * CHUNK, CHUNK)),
-                )
+            for i, (a, side) in enumerate(ORDER):
+                gather(c, a, side, dst[:, i, :])
 
-        gather_chunk(0, placed(dealt, "picked0", picked_shape, U32, 2 * N))
+        picked_shape = [P, 2 * PASSES, CHUNK]
+        early = {
+            (0, 1, TARGET): placed(second_half, "picked0_1t", [P, CHUNK], U32, 4 * part_bytes - HALF),
+            (0, 1, SOURCE): placed(dealt, "picked0_1s", [P, CHUNK], U32, wd_bytes - N),
+        }
+        for a in range(PASSES):
+            for c in range(2):
+                for key in [(c, a, side) for b, side in ORDER if b == a]:
+                    dst = early[key] if key in early else sb(f"picked{c}_{a}_{key[2]}", [P, CHUNK], U32)
+                    gather(*key, dst[:])
+        tgt_sc.append(placed(second_half, "tgt_sc1", [P, HALF], U8, 4 * part_bytes))
+        nc.vector.tensor_copy(tgt_sc[1][:], tab_sc[:].indirect(entries(lists[TARGET], HALF, HALF)))
+        gather_chunk(2, placed(second_half, "picked2", picked_shape, U32, 0))
 
-        wd_raw = placed(late, "wd_raw", [P, PASSES, N], I32, 0)
-        wd_sc_raw = placed(late, "wd_sc_raw", [P, N], U8, wd_bytes)
-        edge_w = placed(late, "edge_w", [P, J], F32, wd_bytes + N)
+        wd_raw = placed(loads, "wd_raw", [P, PASSES, N], I32, load_at["wd_raw"])
+        wd_sc_raw = placed(loads, "wd_sc_raw", [P, N], U8, load_at["wd_sc_raw"])
+        edge_w = placed(loads, "edge_w", [P, J], F32, load_at["edge_w"])
         nc.vector.memset(wd_sc_raw[:].bitcast(I32), 0)
         nc.sync.dma_start(wd_raw[:], wd_words.rearrange("a p n i -> p a (n i)").bitcast(I32))
         load_two_planes(wd_sc_raw, wd_scales)
         nc.sync.dma_start(edge_w[:], wgo)
 
-        for c in range(1, CHUNKS - 1):
-            gather_chunk(c, sb(f"picked{c}", picked_shape, U32))
 
         def first_banks(group):
             return [
@@ -177,11 +193,11 @@ def tile_list_msg_relu_biasP_kernel(
                 w = ws_w[a][:, 2 * half * BANK : 2 * (half + 1) * BANK].bitcast(FP4X4)
                 w_scale = w_sc[SOURCE][:, plane_cols]
             else:
-                v_scale = tgt_sc[ROWS * a : P, edges]
+                v_scale = tgt_sc[group // 4][ROWS * a : P, P * (group % 4) : P * (group % 4 + 1)]
                 w = wt_w[a][:, half * BANK : (half + 1) * BANK].bitcast(FP8X4)
                 w_scale = w_sc[TARGET][:, plane_cols]
             nc.tensor.matmul_mx(
-                out=acc[:], lhsT=picked[group // 2][:, 2 * a + side, in_chunk].bitcast(FP8X4), lhsT_scale=v_scale,
+                out=acc[:], lhsT=picked[group // 2, a, side][:, in_chunk].bitcast(FP8X4), lhsT_scale=v_scale,
                 rhs=w, rhs_scale=w_scale,
                 start=((a, side) == ORDER[0]), stop=((a, side) == ORDER[-1]),
             )
@@ -266,7 +282,7 @@ def tile_list_msg_relu_biasP_kernel(
                 page_2(c - 1, f"h_t{2 * c + 1}")
             if c == 0:
                 gather_chunk(CHUNKS - 1, sb(f"picked{CHUNKS - 1}", picked_shape, U32, "h_in0"))
-                add_page(placed(loads, "page2", [P, T], F32, load_at["tab_w"]))
+                add_page(placed(loads, "page2", [P, T], F32, load_at["tab_w1"]))
             if c == 1:
                 add_page(sb("page3", [P, T], F32, "h_in1"))
 
@@ -276,10 +292,12 @@ def tile_list_msg_relu_biasP_kernel(
             for group in (0, 1):
                 for half in range(2):
                     first_pass(banks[group][half], group, half, a, side)
-        for group in (0, 1):
-            for half in range(2):
-                for a, side in ORDER[2:]:
-                    first_pass(banks[group][half], group, half, a, side)
+        for group, half, side in (
+            (0, 0, TARGET), (0, 1, TARGET), (0, 0, SOURCE), (1, 0, TARGET), (1, 1, TARGET),
+            (0, 1, SOURCE), (1, 0, SOURCE), (1, 1, SOURCE),
+        ):
+            first_pass(banks[group][half], group, half, 1, side)
+            if side == SOURCE:
                 relu(group, half, banks[group][half])
         wd_w = placed(dealt, "wd_w", [P, PASSES, N], I32, 0)
         nc.vector.tensor_copy(
@@ -320,31 +338,39 @@ def tile_list_msg_relu_biasP_kernel(
                 round_copy = nc.vector.tensor_copy if i == 0 and t >= 2 else nc.scalar.copy
                 round_copy(pairs[i][:, t // 2, :, t % 2], pages[t][:, starts[i] : starts[i] + w])
 
-        out_sc = sb("out_sc", [P, T], U8)
+        out_sc = sb("out_sc", [P, BANK], U8)
         out_words = out_1[0].rearrange("p t i -> p (t i)").bitcast(I32)
-        last_piece = len(OUT_WIDTHS) - 1
+        pieces = len(OUT_WIDTHS)
         woven = []
+        codes = [sb(f"codes{i}", [P, BANK], I32) for i in range(T // BANK)]
 
         def weave(i):
             woven.append(sb(f"woven{i}", [P, OUT_WIDTHS[i] * PACK], BF16))
-            word_copy = nc.vector.tensor_copy if i < last_piece else nc.scalar.copy
+            word_copy = nc.vector.tensor_copy if i < pieces - SCALAR_WEAVES else nc.scalar.copy
             word_copy(
                 woven[i][:].bitcast(F32).rearrange("p (c u) -> p c u", u=2),
                 pairs[i][:].rearrange("p u c e -> p u (c e)").bitcast(F32).rearrange("p u c -> p c u"),
             )
 
         def quantise_piece(i):
-            cols = slice(starts[i], starts[i] + OUT_WIDTHS[i])
-            codes = sb(f"codes{i + 1}", [P, OUT_WIDTHS[i]], I32)
-            nc.vector.quantize_mx(out=codes[:].bitcast(FP8X4), scales=out_sc[:, cols], in_=woven[i][:])
-            nc.sync.dma_start(out_words[:, cols], codes[:])
+            block, first = divmod(starts[i], BANK)
+            cols = slice(first, first + OUT_WIDTHS[i])
+            nc.vector.quantize_mx(
+                out=codes[block][:, cols].bitcast(FP8X4), scales=out_sc[ROWS * block : P, cols], in_=woven[i][:]
+            )
+            if block == len(codes) - 1:
+                nc.sync.dma_start(out_words[:, starts[i] : starts[i] + OUT_WIDTHS[i]], codes[block][:, cols])
+            elif cols.stop == BANK:
+                nc.sync.dma_start(out_words[:, block * BANK : (block + 1) * BANK], codes[block][:])
 
         weave(0)
-        for i in range(last_piece):
-            weave(i + 1)
+        weave(1)
+        for i in range(pieces):
             quantise_piece(i)
-        quantise_piece(last_piece)
+            if i + 2 < pieces:
+                weave(i + 2)
         for q in range(QUADRANTS):
-            nc.scalar.dma_start(
-                out_2[0, ROWS * q : ROWS * (q + 1), :].bitcast(I32), out_sc[QUAD * q : QUAD * q + ROWS, :].bitcast(I32)
+            (nc.scalar, nc.sync)[q % 2].dma_start(
+                out_2[0, ROWS * q : ROWS * (q + 1), :].rearrange("s (i c) -> i s c", c=BANK).bitcast(I32),
+                out_sc[QUAD * q : QUAD * q + ROWS * ROWS, :].bitcast(I32),
             )

@@ -47,6 +47,7 @@ def tile_list_msg_relu_biasP_kernel(
         keep = ctx.enter_context(tc.tile_pool(name="keep", bufs=1))
         loads = ctx.enter_context(tc.tile_pool(name="loads", bufs=1))
         second_half = ctx.enter_context(tc.tile_pool(name="second_half", bufs=1))
+        aside = ctx.enter_context(tc.tile_pool(name="aside", bufs=1))
         dealt = ctx.enter_context(tc.tile_pool(name="dealt", bufs=1))
         psum = ctx.enter_context(tc.psum_pool(name="psum", bufs=1))
 
@@ -72,20 +73,21 @@ def tile_list_msg_relu_biasP_kernel(
 
         wd_bytes = WORD * PASSES * N
         tab_sc = sb("tab_sc", [P, T], U8)
-        nc.vector.memset(tab_sc[:].bitcast(I32), 0)
+        nc.gpsimd.memset(tab_sc[:].bitcast(I32), 0)
         load_two_planes(tab_sc, tab_scales)
 
-        load_words = {"tab_w0": T, "tab_w1": T, "ws_w0": R // 2, "wt_w0": R, "ws_w1": R // 2, "wt_w1": R, "ident": P, "wd_raw": PASSES * N, "wd_sc_raw": N // WORD, "edge_w": J, "bias": 2 * T}
+        load_words = {"tab_w0": T, "tab_w1": T, "ws_w0": R // 2, "wt_w0": R, "ws_w1": R // 2, "wt_w1": R, "wd_raw": PASSES * N, "edge_w": J, "bias": 2 * T}
         load_names = list(load_words)
         load_at = {name: WORD * sum(load_words[n] for n in load_names[:i]) for i, name in enumerate(load_names)}
-        w_sc_words = PASSES * R // WORD
         zeros = placed(loads, "zeros", [P, sum(load_words[n] for n in load_names)], I32, 0)
-        nc.gpsimd.memset(zeros[:, :w_sc_words], 0)
-        w_sc = [sb(f"w_sc{side}", [P, PASSES * R], U8) for side in (SOURCE, TARGET)]
-        nc.vector.tensor_copy(w_sc[SOURCE][:].bitcast(I32), zeros[:, :w_sc_words])
-        nc.vector.memset(w_sc[TARGET][:].bitcast(I32), 0)
+        nc.gpsimd.memset(zeros[:, : J // WORD], 0)
+        head_end = placed(aside, "head_end", [P, T + P], I32, 0)
+        nc.gpsimd.memset(head_end[:, : N // WORD], 0)
         src_sc1 = sb("src_sc1", [P, J], U8)
-        nc.vector.memset(src_sc1[:].bitcast(I32), 0)
+        nc.vector.tensor_copy(src_sc1[:].bitcast(I32), zeros[:, : J // WORD])
+        w_sc = [sb(f"w_sc{side}", [P, PASSES * R], U8) for side in (SOURCE, TARGET)]
+        for side in (SOURCE, TARGET):
+            nc.vector.memset(w_sc[side][:].bitcast(I32), 0)
 
         tab_w = [placed(loads, f"tab_w{a}", [P, T], I32, load_at[f"tab_w{a}"]) for a in range(PASSES)]
         ws_w = [placed(loads, f"ws_w{a}", [P, 2 * R], U8, load_at[f"ws_w{a}"]) for a in range(PASSES)]
@@ -120,18 +122,20 @@ def tile_list_msg_relu_biasP_kernel(
         load_ws(1)
         bias = placed(loads, "bias", [P, load_words["bias"]], F32, load_at["bias"])
         nc.sync.dma_start(bias[:, :PACK], b.rearrange("(p t) -> p t", t=PACK))
-        ident = placed(loads, "ident", [P, P], F32, load_at["ident"])
-        make_identity(nc, ident[:])
 
         pages = []
 
         def add_page(page):
-            engine = nc.vector if len(pages) < 2 else nc.gpsimd
+            engine = nc.gpsimd if pages else nc.vector
             pages.append(page)
             engine.memset(page[:].bitcast(I32), 0)
 
-        for t in range(2):
-            add_page(sb(f"page{t}", [P, T], F32))
+        add_page(sb("page0", [P, T], F32))
+        wd_sc_raw = sb("wd_sc_raw", [P, N], U8)
+        nc.vector.tensor_copy(wd_sc_raw[:].bitcast(I32), head_end[:, : N // WORD])
+        add_page(placed(aside, "page1", [P, T], F32, 0))
+        ident = placed(aside, "ident", [P, P], F32, WORD * T)
+        make_identity(nc, ident[:])
 
         src_sc = sb("src_sc", [P, J], U8)
         nc.vector.tensor_copy(src_sc[:], tab_sc[:].indirect(lists[SOURCE][:]))
@@ -170,9 +174,7 @@ def tile_list_msg_relu_biasP_kernel(
         gather_chunk(2, placed(second_half, "picked2", picked_shape, U32, 0))
 
         wd_raw = placed(loads, "wd_raw", [P, PASSES, N], I32, load_at["wd_raw"])
-        wd_sc_raw = placed(loads, "wd_sc_raw", [P, N], U8, load_at["wd_sc_raw"])
         edge_w = placed(loads, "edge_w", [P, J], F32, load_at["edge_w"])
-        nc.vector.memset(wd_sc_raw[:].bitcast(I32), 0)
         nc.sync.dma_start(wd_raw[:], wd_words.rearrange("a p n i -> p a (n i)").bitcast(I32))
         load_two_planes(wd_sc_raw, wd_scales)
         nc.sync.dma_start(edge_w[:], wgo)

@@ -49,6 +49,7 @@ def tile_list_msg_relu_biasP_kernel(
         second_half = ctx.enter_context(tc.tile_pool(name="second_half", bufs=1))
         aside = ctx.enter_context(tc.tile_pool(name="aside", bufs=1))
         dealt = ctx.enter_context(tc.tile_pool(name="dealt", bufs=1))
+        head_h = ctx.enter_context(tc.tile_pool(name="head_h", bufs=1))
         psum = ctx.enter_context(tc.psum_pool(name="psum", bufs=1))
 
         def sb(name, shape, dtype, tag=None):
@@ -60,161 +61,187 @@ def tile_list_msg_relu_biasP_kernel(
         def entries(list_tile, first, count):
             return list_tile[:, first // PER_COLUMN : (first + count) // PER_COLUMN]
 
-        def load_two_planes(plane, scales):
+        def load_two_planes(plane, scales, queue=nc.sync, shift=0):
             for q in range(QUADRANTS):
-                nc.sync.dma_start(
-                    plane[QUAD * q : QUAD * q + PASSES * ROWS, :].bitcast(I32),
+                queue.dma_start(
+                    plane[QUAD * q + shift : QUAD * q + shift + PASSES * ROWS, :].bitcast(I32),
                     scales[:, ROWS * q : ROWS * (q + 1), :].bitcast(I32),
                 )
 
         lists = [keep.tile([P, J // PER_COLUMN], U16, name=name) for name in ("src_list", "tgt_list")]
-        nc.sync.dma_start(lists[SOURCE][:], offs)
-        nc.sync.dma_start(lists[TARGET][:], offs2)
-
-        wd_bytes = WORD * PASSES * N
-        tab_sc = sb("tab_sc", [P, T], U8)
-        nc.gpsimd.memset(tab_sc[:].bitcast(I32), 0)
-        load_two_planes(tab_sc, tab_scales)
-
-        load_words = {"tab_w0": T, "tab_w1": T, "ws_w0": R // 2, "wt_w0": R, "ws_w1": R // 2, "wt_w1": R, "wd_raw": PASSES * N, "edge_w": J, "bias": 2 * T}
-        load_names = list(load_words)
-        load_at = {name: WORD * sum(load_words[n] for n in load_names[:i]) for i, name in enumerate(load_names)}
-        zeros = placed(loads, "zeros", [P, sum(load_words[n] for n in load_names)], I32, 0)
-        nc.gpsimd.memset(zeros[:, : J // WORD], 0)
-        head_end = placed(aside, "head_end", [P, T + P], I32, 0)
-        nc.gpsimd.memset(head_end[:, : N // WORD], 0)
-        src_sc1 = sb("src_sc1", [P, J], U8)
-        nc.vector.tensor_copy(src_sc1[:].bitcast(I32), zeros[:, : J // WORD])
-        w_sc = [sb(f"w_sc{side}", [P, PASSES * R], U8) for side in (SOURCE, TARGET)]
-        for side in (SOURCE, TARGET):
-            nc.vector.memset(w_sc[side][:].bitcast(I32), 0)
-
-        tab_w = [placed(loads, f"tab_w{a}", [P, T], I32, load_at[f"tab_w{a}"]) for a in range(PASSES)]
-        ws_w = [placed(loads, f"ws_w{a}", [P, 2 * R], U8, load_at[f"ws_w{a}"]) for a in range(PASSES)]
-        wt_w = [placed(loads, f"wt_w{a}", [P, R], I32, load_at[f"wt_w{a}"]) for a in range(PASSES)]
-
-        def load_w_scales(side, q):
-            first_row = QUAD * q
-            nc.sync.dma_start(
-                w_sc[side][first_row : first_row + ROWS, :].bitcast(I32).rearrange("p (a r) -> p a r", a=PASSES),
-                (ws_scales, wt_scales)[side][:, ROWS * q : ROWS * (q + 1), :].rearrange("a q r -> q a r").bitcast(I32),
-            )
-
-        def load_tab(a):
-            nc.sync.dma_start(tab_w[a][:], tab_words[a].rearrange("p t i -> p (t i)").bitcast(I32))
-
-        load_tab(0)
-        for q in range(QUADRANTS):
-            load_w_scales(SOURCE, q)
+        ws_w = [sb("ws_w0", [P, 2 * R], U8)]
 
         def load_ws(a):
             nc.sync.dma_start(ws_w[a][:].bitcast(I32), ws_words[a].bitcast(I32))
 
+        nc.sync.dma_start(lists[SOURCE][:], offs)
+        load_ws(0)
+        nc.sync.dma_start(lists[TARGET][:], offs2)
+
+        wd_bytes = WORD * PASSES * N
+        load_words = {
+            "tab_w1": T, "wt_w0": R, "ws_w1": R // 2, "wt_w1": R, "wd_raw": PASSES * N, "edge_w": J,
+            "wt_sc": PASSES * R // WORD, "ident": P, "page0": T, "page1": T, "page2": T, "bias": 2 * T,
+        }
+        load_names = list(load_words)
+        load_at = {name: WORD * sum(load_words[n] for n in load_names[:i]) for i, name in enumerate(load_names)}
+        first_zeros = placed(aside, "first_zeros", [P, N // WORD], I32, 0)
+        nc.gpsimd.memset(first_zeros[:], 0)
+        tab_sc = sb("tab_sc", [P, T], U8)
+        nc.gpsimd.memset(tab_sc[:].bitcast(I32), 0)
+        zeros = placed(loads, "zeros", [P, sum(load_words[n] for n in load_names)], I32, 0)
+        nc.vector.memset(zeros[:, : J // WORD], 0)
+        ws_sc = sb("ws_sc", [P, PASSES * R], U8)
+        nc.vector.memset(ws_sc[:].bitcast(I32), 0)
+        wd_sc_raw = sb("wd_sc_raw", [P, N], U8)
+        nc.gpsimd.tensor_copy(wd_sc_raw[:].bitcast(I32), first_zeros[:])
+        src_sc1 = sb("src_sc1", [P, J], U8)
+        nc.vector.tensor_copy(src_sc1[:].bitcast(I32), zeros[:, : J // WORD])
+        load_two_planes(tab_sc, tab_scales)
+
+        tab_w = [placed(aside, "tab_w0", [P, T], I32, 0), placed(loads, "tab_w1", [P, T], I32, load_at["tab_w1"])]
+        ws_w.append(placed(loads, "ws_w1", [P, 2 * R], U8, load_at["ws_w1"]))
+        wt_w = [placed(loads, f"wt_w{a}", [P, R], I32, load_at[f"wt_w{a}"]) for a in range(PASSES)]
+        wt_sc = placed(loads, "wt_sc", [P, PASSES * R], U8, load_at["wt_sc"])
+        nc.gpsimd.memset(wt_sc[:].bitcast(I32), 0)
+
+        def load_w_scales(queue, plane, scales, shift):
+            for q in range(QUADRANTS):
+                first_row = QUAD * q + shift
+                queue.dma_start(
+                    plane[first_row : first_row + ROWS, :].bitcast(I32).rearrange("p (a r) -> p a r", a=PASSES),
+                    scales[:, ROWS * q : ROWS * (q + 1), :].rearrange("a q r -> q a r").bitcast(I32),
+                )
+
+        def load_tab(a):
+            nc.sync.dma_start(tab_w[a][:], tab_words[a].rearrange("p t i -> p (t i)").bitcast(I32))
+
         def load_wt(a):
             nc.sync.dma_start(wt_w[a][:], wt_words[a].rearrange("p r i -> p (r i)").bitcast(I32))
 
-        load_ws(0)
-        load_wt(0)
-        for q in range(QUADRANTS):
-            load_w_scales(TARGET, q)
+        load_tab(0)
+        load_w_scales(nc.sync, ws_sc, ws_scales, 0)
         load_tab(1)
+        load_wt(0)
+        load_w_scales(nc.sync, wt_sc, wt_scales, ROWS)
         load_wt(1)
         load_ws(1)
+        wd_raw = placed(loads, "wd_raw", [P, PASSES, N], I32, load_at["wd_raw"])
+        edge_w = placed(loads, "edge_w", [P, J], F32, load_at["edge_w"])
         bias = placed(loads, "bias", [P, load_words["bias"]], F32, load_at["bias"])
-        nc.sync.dma_start(bias[:, :PACK], b.rearrange("(p t) -> p t", t=PACK))
 
+        ident = placed(loads, "ident", [P, P], F32, load_at["ident"])
+        make_identity(nc, ident[:])
         pages = []
 
         def add_page(page):
-            engine = nc.gpsimd if pages else nc.vector
             pages.append(page)
-            engine.memset(page[:].bitcast(I32), 0)
+            nc.gpsimd.memset(page[:].bitcast(I32), 0)
 
-        add_page(sb("page0", [P, T], F32))
-        wd_sc_raw = sb("wd_sc_raw", [P, N], U8)
-        nc.vector.tensor_copy(wd_sc_raw[:].bitcast(I32), head_end[:, : N // WORD])
-        add_page(placed(aside, "page1", [P, T], F32, 0))
-        ident = placed(aside, "ident", [P, P], F32, WORD * T)
-        make_identity(nc, ident[:])
+        for t in range(PACK - 1):
+            add_page(placed(loads, f"page{t}", [P, T], F32, load_at[f"page{t}"]))
 
-        src_sc = sb("src_sc", [P, J], U8)
-        nc.vector.tensor_copy(src_sc[:], tab_sc[:].indirect(lists[SOURCE][:]))
-        for q in range(QUADRANTS):
-            nc.sync.dma_start(
-                src_sc1[QUAD * q : QUAD * q + ROWS, :].bitcast(I32),
-                src_sc[QUAD * q + ROWS : QUAD * q + 2 * ROWS, :].bitcast(I32),
-            )
         HALF = J // 2
         part_bytes = WORD * CHUNK
-        tgt_sc = [sb("tgt_sc0", [P, HALF], U8)]
-        nc.vector.tensor_copy(tgt_sc[0][:], tab_sc[:].indirect(entries(lists[TARGET], 0, HALF)))
+        v_sc = {}
+
+        def gather_scales(side, half, dst):
+            v_sc[side, half] = dst
+            nc.vector.tensor_copy(dst[:], tab_sc[:].indirect(entries(lists[side], half * HALF, HALF)))
+
+        def shift_scales(queue, half):
+            for q in range(QUADRANTS):
+                queue.dma_start(
+                    src_sc1[QUAD * q : QUAD * q + ROWS, half * HALF : (half + 1) * HALF].bitcast(I32),
+                    v_sc[SOURCE, half][QUAD * q + ROWS : QUAD * q + 2 * ROWS, :].bitcast(I32),
+                )
 
         picked = {}
 
-        def gather(c, a, side, dst):
+        def gather(c, a, side, dst=None):
+            if dst is None:
+                dst = sb(f"picked{c}_{a}_{side}", [P, CHUNK], U32)[:]
             picked[c, a, side] = dst
             nc.vector.tensor_copy(dst, tab_w[a][:].bitcast(U32).indirect(entries(lists[side], c * CHUNK, CHUNK)))
 
-        def gather_chunk(c, dst):
-            for i, (a, side) in enumerate(ORDER):
-                gather(c, a, side, dst[:, i, :])
+        gather_scales(SOURCE, 0, sb("src_sc_a", [P, HALF], U8))
+        shift_scales(nc.sync, 0)
+        gather_scales(TARGET, 0, sb("tgt_sc_a", [P, HALF], U8))
+        gather(0, 0, SOURCE)
+        gather(1, 0, SOURCE)
+        gather(0, 0, TARGET)
+        gather(1, 0, TARGET)
+        gather(2, 0, SOURCE)
+        gather(2, 0, TARGET)
+        gather(0, 1, TARGET, placed(second_half, "picked0_1t", [P, CHUNK], U32, HALF - ALIGN)[:])
+        gather(0, 1, SOURCE, placed(dealt, "picked0_1s", [P, CHUNK], U32, wd_bytes - ALIGN)[:])
+        gather(1, 1, SOURCE)
+        gather(1, 1, TARGET)
+        gather(2, 1, TARGET)
+        gather(2, 1, SOURCE)
 
-        picked_shape = [P, 2 * PASSES, CHUNK]
-        early = {
-            (0, 1, TARGET): placed(second_half, "picked0_1t", [P, CHUNK], U32, 4 * part_bytes - HALF),
-            (0, 1, SOURCE): placed(dealt, "picked0_1s", [P, CHUNK], U32, wd_bytes - N),
-        }
-        for a in range(PASSES):
-            for c in range(2):
-                for key in [(c, a, side) for b, side in ORDER if b == a]:
-                    dst = early[key] if key in early else sb(f"picked{c}_{a}_{key[2]}", [P, CHUNK], U32)
-                    gather(*key, dst[:])
-        tgt_sc.append(placed(second_half, "tgt_sc1", [P, HALF], U8, 4 * part_bytes))
-        nc.vector.tensor_copy(tgt_sc[1][:], tab_sc[:].indirect(entries(lists[TARGET], HALF, HALF)))
-        gather_chunk(2, placed(second_half, "picked2", picked_shape, U32, 0))
-
-        wd_raw = placed(loads, "wd_raw", [P, PASSES, N], I32, load_at["wd_raw"])
-        edge_w = placed(loads, "edge_w", [P, J], F32, load_at["edge_w"])
         nc.sync.dma_start(wd_raw[:], wd_words.rearrange("a p n i -> p a (n i)").bitcast(I32))
         load_two_planes(wd_sc_raw, wd_scales)
         nc.sync.dma_start(edge_w[:], wgo)
+        nc.sync.dma_start(bias[:, :PACK], b.rearrange("(p t) -> p t", t=PACK))
 
+        gather_scales(SOURCE, 1, placed(second_half, "src_sc_b", [P, HALF], U8, 0))
+        shift_scales(nc.sync, 1)
+        gather_scales(TARGET, 1, placed(second_half, "tgt_sc_b", [P, HALF], U8, HALF + part_bytes - 2 * ALIGN))
+        wd_w = placed(dealt, "wd_w", [P, PASSES, N], I32, 0)
+        nc.vector.tensor_copy(
+            wd_w[:].rearrange("p a (t g i) -> p a g t i", t=PACK, i=4),
+            wd_raw[:].rearrange("p a (g i t) -> p a g t i", t=PACK, i=4),
+        )
+        wd_sc = placed(dealt, "wd_sc", [P, N], U8, wd_bytes)
+        nc.vector.tensor_copy(
+            wd_sc[:].rearrange("p (t m) -> p t m", t=PACK), wd_sc_raw[:].rearrange("p (m t) -> p t m", t=PACK)
+        )
+        last0 = placed(dealt, "picked3_0", [P, 2, CHUNK], U32, wd_bytes + part_bytes - 2 * ALIGN)
+        gather(3, 0, SOURCE, last0[:, 0, :])
+        gather(3, 0, TARGET, last0[:, 1, :])
 
-        def first_banks(group):
-            return [
-                psum.tile([P, BANK], F32, name=f"a{group}_{half}", tag=f"first{2 * (group % 2) + half}")
-                for half in range(2)
-            ]
+        FIRST_BANKS = ((0, 1), (2, 3), (4, 5), (3, 6), (7, 4), (5, 3), (7, 4), (5, 3))
+        TURN_BANKS = ((6, 7), (2, 6), (2, 6), (2, 6))
 
-        def first_pass(acc, group, half, a, side):
+        def bank(name, i):
+            return psum.tile([P, BANK], F32, name=name, tag=f"bank{i}")
+
+        def first_pass(acc, group, half, a, side, order=ORDER):
             in_chunk = slice(P * (group % 2), P * (group % 2 + 1))
             edges = slice(P * group, P * (group + 1))
+            in_half = slice(P * (group % 4), P * (group % 4 + 1))
             plane_cols = slice(a * R + half * BANK, a * R + (half + 1) * BANK)
             if side == SOURCE:
-                v_scale = (src_sc, src_sc1)[a][:, edges]
+                v_scale = src_sc1[:, edges] if a else v_sc[SOURCE, group // 4][:, in_half]
                 w = ws_w[a][:, 2 * half * BANK : 2 * (half + 1) * BANK].bitcast(FP4X4)
-                w_scale = w_sc[SOURCE][:, plane_cols]
+                w_scale = ws_sc[:, plane_cols]
             else:
-                v_scale = tgt_sc[group // 4][ROWS * a : P, P * (group % 4) : P * (group % 4 + 1)]
+                v_scale = v_sc[TARGET, group // 4][ROWS * a : P, in_half]
                 w = wt_w[a][:, half * BANK : (half + 1) * BANK].bitcast(FP8X4)
-                w_scale = w_sc[TARGET][:, plane_cols]
+                w_scale = wt_sc[ROWS:P, plane_cols]
             nc.tensor.matmul_mx(
                 out=acc[:], lhsT=picked[group // 2, a, side][:, in_chunk].bitcast(FP8X4), lhsT_scale=v_scale,
                 rhs=w, rhs_scale=w_scale,
-                start=((a, side) == ORDER[0]), stop=((a, side) == ORDER[-1]),
+                start=((a, side) == order[0]), stop=((a, side) == order[-1]),
             )
 
         h_ts = {}
 
-        def first_half(group, half, order):
-            acc = psum.tile([P, BANK], F32, name=f"a{group}_{half}", tag=f"first{2 * (group % 2) + half}")
+        def first_half(group, half, order, later=False):
+            acc = bank(f"a{group}_{half}", FIRST_BANKS[group][half])
             for a, side in order:
                 first_pass(acc, group, half, a, side)
+            if later:
+                return acc
             relu(group, half, acc)
 
         def relu(group, half, acc):
             if group not in h_ts:
-                h_ts[group] = sb(f"h_t{group}", [P, R], BF16)
+                if group in (1, 2, 3):
+                    h_ts[group] = placed(head_h, f"h_t{group}", [P, R], BF16, {2: 0, 1: R, 3: 2 * R}[group])
+                else:
+                    h_ts[group] = sb(f"h_t{group}", [P, R], BF16)
             nc.scalar.activation(
                 h_ts[group][:, half * BANK : (half + 1) * BANK].rearrange("j (u p e) -> j u p e", u=2, e=2),
                 acc[:].rearrange("j (p u e) -> j u p e", u=2, e=2),
@@ -222,7 +249,7 @@ def tile_list_msg_relu_biasP_kernel(
             )
 
         def turn(group, h_in):
-            turned = psum.tile([P, BANK], F32, name=f"turned{group}", tag=f"turn{group % 2}")
+            turned = bank(f"turned{group}", TURN_BANKS[group // 2][group % 2])
             for s in range(2 * PASSES):
                 nc.tensor.transpose(turned[:, P * s : P * (s + 1)], h_ts[group][:].bitcast(F32)[:, P * s : P * (s + 1)], ident[:])
             h_words = h_in[:].bitcast(F32).rearrange("p (a j u) -> p a j u", a=PASSES, u=2)
@@ -255,8 +282,8 @@ def tile_list_msg_relu_biasP_kernel(
         held = {}
 
         def second_stage(c):
-            acc = psum.tile([P, BANK], F32, name=f"early{c}", tag="second0")
-            acc2 = psum.tile([P, BANK], F32, name=f"lag{c}", tag="second1")
+            acc = bank(f"early{c}", 0)
+            acc2 = bank(f"lag{c}", 1)
             for t in range(2):
                 second(acc[:, t * CHUNK : (t + 1) * CHUNK], c, t)
             second(acc2[:, :CHUNK], c, 2)
@@ -269,7 +296,10 @@ def tile_list_msg_relu_biasP_kernel(
             held[c] = acc2
 
         def page_2(c, tag):
-            m = sb(f"msg{c}_2", [P, CHUNK], F32, tag)
+            if c == 0:
+                m = placed(head_h, "msg0_2", [P, CHUNK], F32, 3 * R)
+            else:
+                m = sb(f"msg{c}_2", [P, CHUNK], F32, tag)
             add_bias(m[:], held[c][:, :CHUNK], 2)
             scatter(2, c * CHUNK, CHUNK, m[:])
 
@@ -283,34 +313,37 @@ def tile_list_msg_relu_biasP_kernel(
             if c > 0:
                 page_2(c - 1, f"h_t{2 * c + 1}")
             if c == 0:
-                gather_chunk(CHUNKS - 1, sb(f"picked{CHUNKS - 1}", picked_shape, U32, "h_in0"))
-                add_page(placed(loads, "page2", [P, T], F32, load_at["tab_w1"]))
+                last1 = sb("picked3_1", [P, 2, CHUNK], U32, "h_in0")
+                gather(3, 1, TARGET, last1[:, 0, :])
+                gather(3, 1, SOURCE, last1[:, 1, :])
             if c == 1:
                 add_page(sb("page3", [P, T], F32, "h_in1"))
 
         order = ORDER
-        banks = {group: first_banks(group) for group in (0, 1)}
-        for a, side in ORDER[:2]:
-            for group in (0, 1):
+        banks = {(g, half): bank(f"a{g}_{half}", FIRST_BANKS[g][half]) for g in range(3) for half in range(2)}
+        for g, half in banks:
+            first_pass(banks[g, half], g, half, *ORDER[0])
+        SOURCE_FIRST = ((0, SOURCE), (1, SOURCE), (0, TARGET), (1, TARGET))
+
+        def finish(g, half):
+            for a, side in SOURCE_FIRST[1:]:
+                first_pass(banks[g, half], g, half, a, side, SOURCE_FIRST)
+
+        for a, side in ORDER[1:]:
+            for g in range(2):
                 for half in range(2):
-                    first_pass(banks[group][half], group, half, a, side)
-        for group, half, side in (
-            (0, 0, TARGET), (0, 1, TARGET), (0, 0, SOURCE), (1, 0, TARGET), (1, 1, TARGET),
-            (0, 1, SOURCE), (1, 0, SOURCE), (1, 1, SOURCE),
-        ):
-            first_pass(banks[group][half], group, half, 1, side)
-            if side == SOURCE:
-                relu(group, half, banks[group][half])
-        wd_w = placed(dealt, "wd_w", [P, PASSES, N], I32, 0)
-        nc.vector.tensor_copy(
-            wd_w[:].rearrange("p a (t g i) -> p a g t i", t=PACK, i=4),
-            wd_raw[:].rearrange("p a (g i t) -> p a g t i", t=PACK, i=4),
-        )
-        wd_sc = placed(dealt, "wd_sc", [P, N], U8, wd_bytes)
-        nc.vector.tensor_copy(
-            wd_sc[:].rearrange("p (t m) -> p t m", t=PACK), wd_sc_raw[:].rearrange("p (m t) -> p t m", t=PACK)
-        )
-        for c in range(CHUNKS - 1):
+                    first_pass(banks[g, half], g, half, a, side)
+                    if (a, side) == ORDER[-1]:
+                        relu(g, half, banks[g, half])
+        finish(2, 0)
+        finish(2, 1)
+        quantise_h(0)
+        relu(2, 0, banks[2, 0])
+        relu(2, 1, banks[2, 1])
+        first_half(3, 0, order)
+        first_half(3, 1, order)
+        second_stage(0)
+        for c in range(1, CHUNKS - 1):
             first_half(2 * c + 2, 0, order)
             quantise_h(c)
             first_half(2 * c + 2, 1, order)
@@ -319,7 +352,7 @@ def tile_list_msg_relu_biasP_kernel(
             first_half(2 * c + 3, 1, order)
         quantise_h(CHUNKS - 1)
         for half, chunks in enumerate(((0, 1), (2,))):
-            acc = psum.tile([P, BANK], F32, name=f"last{half}", tag=f"first{half}")
+            acc = bank(f"last{half}", FIRST_BANKS[-1][half])
             for i, c in enumerate(chunks):
                 second(acc[:, i * CHUNK : (i + 1) * CHUNK], c, 3)
             add_bias(msg3[:, half * BANK : half * BANK + CHUNK * len(chunks)], acc[:, : CHUNK * len(chunks)], 3)

@@ -81,20 +81,22 @@ def tile_list_msg_relu_biasP_kernel(
         wd_bytes = WORD * PASSES * N
         load_words = {
             "tab_w1": T, "wt_w0": R, "ws_w1": R // 2, "wt_w1": R, "wd_raw": PASSES * N, "edge_w": J,
-            "wt_sc": PASSES * R // WORD, "ident": P, "page0": T, "page1": T, "page2": T, "bias": 2 * T,
+            "wt_sc": PASSES * R // WORD, "ident": P, "page1": T, "bias": 2 * T,
         }
         load_names = list(load_words)
         load_at = {name: WORD * sum(load_words[n] for n in load_names[:i]) for i, name in enumerate(load_names)}
-        first_zeros = placed(aside, "first_zeros", [P, N // WORD], I32, 0)
-        nc.gpsimd.memset(first_zeros[:], 0)
         tab_sc = sb("tab_sc", [P, T], U8)
         nc.gpsimd.memset(tab_sc[:].bitcast(I32), 0)
+        first_zeros = placed(aside, "first_zeros", [P, N // WORD], I32, 0)
+        nc.gpsimd.memset(first_zeros[:], 0)
         zeros = placed(loads, "zeros", [P, sum(load_words[n] for n in load_names)], I32, 0)
         nc.vector.memset(zeros[:, : J // WORD], 0)
         ws_sc = sb("ws_sc", [P, PASSES * R], U8)
         nc.vector.memset(ws_sc[:].bitcast(I32), 0)
         wd_sc_raw = sb("wd_sc_raw", [P, N], U8)
         nc.gpsimd.tensor_copy(wd_sc_raw[:].bitcast(I32), first_zeros[:])
+        pages = [sb("page0", [P, T], F32)]
+        nc.vector.memset(pages[0][:].bitcast(I32), 0)
         src_sc1 = sb("src_sc1", [P, J], U8)
         nc.vector.tensor_copy(src_sc1[:].bitcast(I32), zeros[:, : J // WORD])
         load_two_planes(tab_sc, tab_scales)
@@ -132,14 +134,12 @@ def tile_list_msg_relu_biasP_kernel(
 
         ident = placed(loads, "ident", [P, P], F32, load_at["ident"])
         make_identity(nc, ident[:])
-        pages = []
 
         def add_page(page):
             pages.append(page)
             nc.gpsimd.memset(page[:].bitcast(I32), 0)
 
-        for t in range(PACK - 1):
-            add_page(placed(loads, f"page{t}", [P, T], F32, load_at[f"page{t}"]))
+        add_page(placed(loads, "page1", [P, T], F32, load_at["page1"]))
 
         HALF = J // 2
         part_bytes = WORD * CHUNK
@@ -316,6 +316,7 @@ def tile_list_msg_relu_biasP_kernel(
                 last1 = sb("picked3_1", [P, 2, CHUNK], U32, "h_in0")
                 gather(3, 1, TARGET, last1[:, 0, :])
                 gather(3, 1, SOURCE, last1[:, 1, :])
+                add_page(placed(loads, "page2", [P, T], F32, load_at["tab_w1"]))
             if c == 1:
                 add_page(sb("page3", [P, T], F32, "h_in1"))
 
@@ -343,13 +344,18 @@ def tile_list_msg_relu_biasP_kernel(
         first_half(3, 0, order)
         first_half(3, 1, order)
         second_stage(0)
-        for c in range(1, CHUNKS - 1):
-            first_half(2 * c + 2, 0, order)
-            quantise_h(c)
-            first_half(2 * c + 2, 1, order)
-            first_half(2 * c + 3, 0, order)
-            second_stage(c)
-            first_half(2 * c + 3, 1, order)
+        first_half(4, 0, order)
+        quantise_h(1)
+        first_half(4, 1, order)
+        first_half(5, 0, order)
+        first_half(5, 1, order)
+        second_stage(1)
+        quantise_h(2)
+        first_half(6, 0, order)
+        first_half(6, 1, order)
+        first_half(7, 0, order)
+        second_stage(2)
+        first_half(7, 1, order)
         quantise_h(CHUNKS - 1)
         for half, chunks in enumerate(((0, 1), (2,))):
             acc = bank(f"last{half}", FIRST_BANKS[-1][half])

@@ -164,21 +164,23 @@ def tile_list_msg_relu_biasP_kernel(
             picked[c, a, side] = dst
             nc.vector.tensor_copy(dst, tab_w[a][:].bitcast(U32).indirect(entries(lists[side], c * CHUNK, CHUNK)))
 
+        def gather_two(a, side):
+            dst = sb(f"picked12_{a}_{side}", [P, 2 * CHUNK], U32)
+            for i in range(2):
+                picked[1 + i, a, side] = dst[:, i * CHUNK : (i + 1) * CHUNK]
+            nc.vector.tensor_copy(dst[:], tab_w[a][:].bitcast(U32).indirect(entries(lists[side], CHUNK, 2 * CHUNK)))
+
         gather_scales(SOURCE, 0, sb("src_sc_a", [P, HALF], U8))
         shift_scales(nc.sync, 0)
         gather_scales(TARGET, 0, sb("tgt_sc_a", [P, HALF], U8))
         gather(0, 0, SOURCE)
-        gather(1, 0, SOURCE)
+        gather_two(0, SOURCE)
         gather(0, 0, TARGET)
-        gather(1, 0, TARGET)
-        gather(2, 0, SOURCE)
-        gather(2, 0, TARGET)
+        gather_two(0, TARGET)
         gather(0, 1, TARGET, placed(second_half, "picked0_1t", [P, CHUNK], U32, HALF - ALIGN)[:])
         gather(0, 1, SOURCE, placed(dealt, "picked0_1s", [P, CHUNK], U32, wd_bytes - ALIGN)[:])
-        gather(1, 1, SOURCE)
-        gather(1, 1, TARGET)
-        gather(2, 1, TARGET)
-        gather(2, 1, SOURCE)
+        gather_two(1, SOURCE)
+        gather_two(1, TARGET)
 
         nc.sync.dma_start(wd_raw[:], wd_words.rearrange("a p n i -> p a (n i)").bitcast(I32))
         load_two_planes(wd_sc_raw, wd_scales)

@@ -81,7 +81,7 @@ def tile_list_msg_relu_biasP_kernel(
         wd_bytes = WORD * PASSES * N
         load_words = {
             "tab_w1": T, "wt_w0": R, "ws_w1": R // 2, "wt_w1": R, "wd_raw": PASSES * N, "edge_w": J,
-            "wt_sc": PASSES * R // WORD, "ident": P, "page1": T, "bias": 2 * T,
+            "wt_sc": PASSES * R // WORD, "ident": P, "page0": T, "page1": T, "bias": 2 * T,
         }
         load_names = list(load_words)
         load_at = {name: WORD * sum(load_words[n] for n in load_names[:i]) for i, name in enumerate(load_names)}
@@ -95,8 +95,7 @@ def tile_list_msg_relu_biasP_kernel(
         nc.vector.memset(ws_sc[:].bitcast(I32), 0)
         wd_sc_raw = sb("wd_sc_raw", [P, N], U8)
         nc.gpsimd.tensor_copy(wd_sc_raw[:].bitcast(I32), first_zeros[:])
-        pages = [sb("page0", [P, T], F32)]
-        nc.vector.memset(pages[0][:].bitcast(I32), 0)
+        pages = []
         src_sc1 = sb("src_sc1", [P, J], U8)
         nc.vector.tensor_copy(src_sc1[:].bitcast(I32), zeros[:, : J // WORD])
         load_two_planes(tab_sc, tab_scales)
@@ -139,6 +138,7 @@ def tile_list_msg_relu_biasP_kernel(
             pages.append(page)
             nc.gpsimd.memset(page[:].bitcast(I32), 0)
 
+        add_page(placed(loads, "page0", [P, T], F32, load_at["page0"]))
         add_page(placed(loads, "page1", [P, T], F32, load_at["page1"]))
 
         HALF = J // 2

@@ -190,13 +190,12 @@ def tile_list_msg_relu_biasP_kernel(
         gather_scales(SOURCE, 1, placed(second_half, "src_sc_b", [P, HALF], U8, 0))
         shift_scales(nc.sync, 1)
         gather_scales(TARGET, 1, placed(second_half, "tgt_sc_b", [P, HALF], U8, HALF + part_bytes - 2 * ALIGN))
-        wd_w = placed(dealt, "wd_w", [P, PASSES, N], I32, 0)
-        nc.vector.tensor_copy(
-            wd_w[:].rearrange("p a (t g i) -> p a g t i", t=PACK, i=4),
-            wd_raw[:].rearrange("p a (g i t) -> p a g t i", t=PACK, i=4),
+        wd_w = sb("wd_w", [P, PASSES, N], I32)
+        nc.gpsimd.tensor_copy(
+            wd_w[:].rearrange("p a (t m) -> p a t m", t=PACK), wd_raw[:].rearrange("p a (m t) -> p a t m", t=PACK)
         )
-        wd_sc = placed(dealt, "wd_sc", [P, N], U8, wd_bytes)
-        nc.vector.tensor_copy(
+        wd_sc = sb("wd_sc", [P, N], U8)
+        nc.gpsimd.tensor_copy(
             wd_sc[:].rearrange("p (t m) -> p t m", t=PACK), wd_sc_raw[:].rearrange("p (m t) -> p t m", t=PACK)
         )
         last0 = placed(dealt, "picked3_0", [P, 2, CHUNK], U32, wd_bytes + part_bytes - 2 * ALIGN)

@@ -49,6 +49,7 @@ def tile_list_msg_relu_biasP_kernel(
         second_half = ctx.enter_context(tc.tile_pool(name="second_half", bufs=1))
         aside = ctx.enter_context(tc.tile_pool(name="aside", bufs=1))
         dealt = ctx.enter_context(tc.tile_pool(name="dealt", bufs=1))
+        mid_h = ctx.enter_context(tc.tile_pool(name="mid_h", bufs=1))
         head_h = ctx.enter_context(tc.tile_pool(name="head_h", bufs=1))
         psum = ctx.enter_context(tc.psum_pool(name="psum", bufs=1))
 
@@ -81,7 +82,7 @@ def tile_list_msg_relu_biasP_kernel(
         wd_bytes = WORD * PASSES * N
         load_words = {
             "tab_w1": T, "wt_w0": R, "ws_w1": R // 2, "wt_w1": R, "wd_raw": PASSES * N, "edge_w": J,
-            "wt_sc": PASSES * R // WORD, "ident": P, "page0": T, "page1": T, "bias": 2 * T,
+            "wt_sc": PASSES * R // WORD, "ident": P, "page0": T, "page1": T, "page2": T, "bias": 2 * T,
         }
         load_names = list(load_words)
         load_at = {name: WORD * sum(load_words[n] for n in load_names[:i]) for i, name in enumerate(load_names)}
@@ -107,11 +108,10 @@ def tile_list_msg_relu_biasP_kernel(
         nc.gpsimd.memset(wt_sc[:].bitcast(I32), 0)
 
         def load_w_scales(queue, plane, scales, shift):
-            for q in range(QUADRANTS):
-                first_row = QUAD * q + shift
+            for s in range(ROWS):
                 queue.dma_start(
-                    plane[first_row : first_row + ROWS, :].bitcast(I32).rearrange("p (a r) -> p a r", a=PASSES),
-                    scales[:, ROWS * q : ROWS * (q + 1), :].rearrange("a q r -> q a r").bitcast(I32),
+                    plane[shift + s : P : QUAD, :].bitcast(I32).rearrange("p (a r) -> p a r", a=PASSES),
+                    scales[:, s : ROWS * QUADRANTS : ROWS, :].rearrange("a q r -> q a r").bitcast(I32),
                 )
 
         def load_tab(a):
@@ -140,6 +140,7 @@ def tile_list_msg_relu_biasP_kernel(
 
         add_page(placed(loads, "page0", [P, T], F32, load_at["page0"]))
         add_page(placed(loads, "page1", [P, T], F32, load_at["page1"]))
+        add_page(placed(loads, "page2", [P, T], F32, load_at["page2"]))
 
         HALF = J // 2
         part_bytes = WORD * CHUNK
@@ -241,6 +242,8 @@ def tile_list_msg_relu_biasP_kernel(
             if group not in h_ts:
                 if group in (1, 2, 3):
                     h_ts[group] = placed(head_h, f"h_t{group}", [P, R], BF16, {2: 0, 1: R, 3: 2 * R}[group])
+                elif group == 5:
+                    h_ts[group] = placed(mid_h, "h_t5", [P, R], BF16, 0)
                 else:
                     h_ts[group] = sb(f"h_t{group}", [P, R], BF16)
             nc.scalar.activation(
@@ -279,7 +282,6 @@ def tile_list_msg_relu_biasP_kernel(
                 pages[t][:].indirect(entries(lists[TARGET], first, count)), src, edge_w[:, first : first + count], MULT,
             )
 
-        msg3 = sb("msg3", [P, J], F32)
         held = {}
 
         def second_stage(c):
@@ -287,22 +289,22 @@ def tile_list_msg_relu_biasP_kernel(
             acc2 = bank(f"lag{c}", 1)
             for t in range(2):
                 second(acc[:, t * CHUNK : (t + 1) * CHUNK], c, t)
-            second(acc2[:, :CHUNK], c, 2)
-            if c == CHUNKS - 1:
-                second(acc2[:, CHUNK:], c, 3)
+            for t in range(2):
+                second(acc2[:, t * CHUNK : (t + 1) * CHUNK], c, 2 + t)
             for t in range(2):
                 m = sb(f"msg{c}_{t}", [P, CHUNK], F32)
                 add_bias(m[:], acc[:, t * CHUNK : (t + 1) * CHUNK], t)
                 scatter(t, c * CHUNK, CHUNK, m[:])
             held[c] = acc2
 
-        def page_2(c, tag):
-            if c == 0:
-                m = placed(head_h, "msg0_2", [P, CHUNK], F32, 3 * R)
-            else:
-                m = sb(f"msg{c}_2", [P, CHUNK], F32, tag)
-            add_bias(m[:], held[c][:, :CHUNK], 2)
-            scatter(2, c * CHUNK, CHUNK, m[:])
+        def lagging_pages(c):
+            for t in range(2):
+                if c == 0:
+                    m = placed(head_h, f"msg0_{2 + t}", [P, CHUNK], F32, (3 - t) * R)
+                else:
+                    m = placed(mid_h, f"msg1_{2 + t}", [P, CHUNK], F32, t * R)
+                add_bias(m[:], held[c][:, t * CHUNK : (t + 1) * CHUNK], 2 + t)
+                scatter(2 + t, c * CHUNK, CHUNK, m[:])
 
         def quantise_h(c):
             h_in = sb(f"h_in{c}", [P, PASSES * CHUNK * PACK], BF16)
@@ -311,15 +313,13 @@ def tile_list_msg_relu_biasP_kernel(
             h_w[c] = sb(f"h_w{c}", [P, PASSES * CHUNK], U32)
             h_sc[c] = sb(f"h_sc{c}", [P, PASSES * CHUNK], U8)
             nc.vector.quantize_mx(out=h_w[c][:].bitcast(FP8X4), scales=h_sc[c][:], in_=h_in[:])
-            if c > 0:
-                page_2(c - 1, f"h_t{2 * c + 1}")
+            if c in (1, 2):
+                lagging_pages(c - 1)
             if c == 0:
                 last1 = sb("picked3_1", [P, 2, CHUNK], U32, "h_in0")
                 gather(3, 1, TARGET, last1[:, 0, :])
                 gather(3, 1, SOURCE, last1[:, 1, :])
-                add_page(placed(loads, "page2", [P, T], F32, load_at["tab_w1"]))
-            if c == 1:
-                add_page(sb("page3", [P, T], F32, "h_in1"))
+                add_page(placed(loads, "page3", [P, T], F32, load_at["tab_w1"]))
 
         order = ORDER
         banks = {(g, half): bank(f"a{g}_{half}", FIRST_BANKS[g][half]) for g in range(3) for half in range(2)}
@@ -355,18 +355,28 @@ def tile_list_msg_relu_biasP_kernel(
         first_half(6, 0, order)
         first_half(6, 1, order)
         first_half(7, 0, order)
-        second_stage(2)
         first_half(7, 1, order)
         quantise_h(CHUNKS - 1)
-        for half, chunks in enumerate(((0, 1), (2,))):
-            acc = bank(f"last{half}", FIRST_BANKS[-1][half])
-            for i, c in enumerate(chunks):
-                second(acc[:, i * CHUNK : (i + 1) * CHUNK], c, 3)
-            add_bias(msg3[:, half * BANK : half * BANK + CHUNK * len(chunks)], acc[:, : CHUNK * len(chunks)], 3)
-        second_stage(CHUNKS - 1)
-        page_2(CHUNKS - 1, None)
-        add_bias(msg3[:, J - CHUNK :], held[CHUNKS - 1][:, CHUNK:], 3)
-        scatter(3, 0, J, msg3[:])
+        LAST_BANKS = (3, 2, 6, 3)
+        last = [bank(f"last{t}", LAST_BANKS[t]) for t in range(PACK - 1)]
+        msgs = [sb(f"msg_last{t}", [P, 2 * CHUNK], F32) for t in range(PACK)]
+        second(last[0][:, :CHUNK], 2, 0)
+        add_bias(msgs[0][:, :CHUNK], last[0][:, :CHUNK], 0)
+        scatter(0, 2 * CHUNK, CHUNK, msgs[0][:, :CHUNK])
+        for t in (1, 2):
+            second(last[t][:, :CHUNK], 2, t)
+        second(last[0][:, CHUNK:], 3, 0)
+        add_bias(msgs[0][:, CHUNK:], last[0][:, CHUNK:], 0)
+        scatter(0, 3 * CHUNK, CHUNK, msgs[0][:, CHUNK:])
+        for t in (1, 2):
+            second(last[t][:, CHUNK:], 3, t)
+            add_bias(msgs[t][:], last[t][:], t)
+            scatter(t, 2 * CHUNK, 2 * CHUNK, msgs[t][:])
+        last.append(bank("last3", LAST_BANKS[3]))
+        for i in range(2):
+            second(last[3][:, i * CHUNK : (i + 1) * CHUNK], 2 + i, 3)
+        add_bias(msgs[3][:], last[3][:], 3)
+        scatter(3, 2 * CHUNK, 2 * CHUNK, msgs[3][:])
 
         out_rows = out_0.rearrange("(p t) c -> p t c", t=PACK)
         starts = [sum(OUT_WIDTHS[:i]) for i in range(len(OUT_WIDTHS))]

@@ -63,7 +63,7 @@ def tile_list_msg_relu_biasP_kernel(
             return list_tile[:, first // PER_COLUMN : (first + count) // PER_COLUMN]
 
         def load_two_planes(plane, scales, queue=nc.sync, shift=0):
-            for q in range(QUADRANTS):
+            for q in (0, 2, 1, 3):
                 queue.dma_start(
                     plane[QUAD * q + shift : QUAD * q + shift + PASSES * ROWS, :].bitcast(I32),
                     scales[:, ROWS * q : ROWS * (q + 1), :].bitcast(I32),
@@ -242,8 +242,8 @@ def tile_list_msg_relu_biasP_kernel(
             if group not in h_ts:
                 if group in (1, 2, 3):
                     h_ts[group] = placed(head_h, f"h_t{group}", [P, R], BF16, {2: 0, 1: R, 3: 2 * R}[group])
-                elif group == 5:
-                    h_ts[group] = placed(mid_h, "h_t5", [P, R], BF16, 0)
+                elif group in (5, 7):
+                    h_ts[group] = placed(mid_h, f"h_t{group}", [P, R], BF16, (group - 5) * R)
                 else:
                     h_ts[group] = sb(f"h_t{group}", [P, R], BF16)
             nc.scalar.activation(
@@ -297,12 +297,12 @@ def tile_list_msg_relu_biasP_kernel(
                 scatter(t, c * CHUNK, CHUNK, m[:])
             held[c] = acc2
 
-        def lagging_pages(c):
-            for t in range(2):
+        def lagging_pages(c, which):
+            for t in which:
                 if c == 0:
                     m = placed(head_h, f"msg0_{2 + t}", [P, CHUNK], F32, (3 - t) * R)
                 else:
-                    m = placed(mid_h, f"msg1_{2 + t}", [P, CHUNK], F32, t * R)
+                    m = placed(mid_h, f"msg1_{2 + t}", [P, CHUNK], F32, t * 2 * R)
                 add_bias(m[:], held[c][:, t * CHUNK : (t + 1) * CHUNK], 2 + t)
                 scatter(2 + t, c * CHUNK, CHUNK, m[:])
 
@@ -313,8 +313,8 @@ def tile_list_msg_relu_biasP_kernel(
             h_w[c] = sb(f"h_w{c}", [P, PASSES * CHUNK], U32)
             h_sc[c] = sb(f"h_sc{c}", [P, PASSES * CHUNK], U8)
             nc.vector.quantize_mx(out=h_w[c][:].bitcast(FP8X4), scales=h_sc[c][:], in_=h_in[:])
-            if c in (1, 2):
-                lagging_pages(c - 1)
+            if c > 0:
+                lagging_pages(*((0, (0, 1)), (1, (0,)), (1, (1,)))[c - 1])
             if c == 0:
                 last1 = sb("picked3_1", [P, 2, CHUNK], U32, "h_in0")
                 gather(3, 1, TARGET, last1[:, 0, :])
@@ -356,27 +356,23 @@ def tile_list_msg_relu_biasP_kernel(
         first_half(6, 1, order)
         first_half(7, 0, order)
         first_half(7, 1, order)
-        quantise_h(CHUNKS - 1)
-        LAST_BANKS = (3, 2, 6, 3)
-        last = [bank(f"last{t}", LAST_BANKS[t]) for t in range(PACK - 1)]
+        LAST_BANKS = (0, 3, 2, 6)
+        last = [bank("last0", LAST_BANKS[0])]
         msgs = [sb(f"msg_last{t}", [P, 2 * CHUNK], F32) for t in range(PACK)]
         second(last[0][:, :CHUNK], 2, 0)
         add_bias(msgs[0][:, :CHUNK], last[0][:, :CHUNK], 0)
         scatter(0, 2 * CHUNK, CHUNK, msgs[0][:, :CHUNK])
-        for t in (1, 2):
+        quantise_h(CHUNKS - 1)
+        last.extend(bank(f"last{t}", LAST_BANKS[t]) for t in range(1, PACK))
+        for t in (1, 2, 3):
             second(last[t][:, :CHUNK], 2, t)
         second(last[0][:, CHUNK:], 3, 0)
         add_bias(msgs[0][:, CHUNK:], last[0][:, CHUNK:], 0)
         scatter(0, 3 * CHUNK, CHUNK, msgs[0][:, CHUNK:])
-        for t in (1, 2):
+        for t in (1, 2, 3):
             second(last[t][:, CHUNK:], 3, t)
             add_bias(msgs[t][:], last[t][:], t)
             scatter(t, 2 * CHUNK, 2 * CHUNK, msgs[t][:])
-        last.append(bank("last3", LAST_BANKS[3]))
-        for i in range(2):
-            second(last[3][:, i * CHUNK : (i + 1) * CHUNK], 2 + i, 3)
-        add_bias(msgs[3][:], last[3][:], 3)
-        scatter(3, 2 * CHUNK, 2 * CHUNK, msgs[3][:])
 
         out_rows = out_0.rearrange("(p t) c -> p t c", t=PACK)
         starts = [sum(OUT_WIDTHS[:i]) for i in range(len(OUT_WIDTHS))]

@@ -33,8 +33,10 @@ SOURCE, TARGET = 0, 1
 
 ORDER = ((0, SOURCE), (0, TARGET), (1, TARGET), (1, SOURCE))
 AHEAD_OF_TABLE = 3
-OUT_WIDTHS = (256, 256, 512, 512, 256, 256)
+OUT_WIDTHS = (512, 512, 256, 256, 256, 256)
+VECTOR_ROUNDS = 256
 SCALAR_WEAVES = 2
+FEW = 8
 
 
 def tile_list_msg_relu_biasP_kernel(
@@ -62,9 +64,9 @@ def tile_list_msg_relu_biasP_kernel(
         def entries(list_tile, first, count):
             return list_tile[:, first // PER_COLUMN : (first + count) // PER_COLUMN]
 
-        def load_two_planes(plane, scales, queue=nc.sync, shift=0):
+        def load_two_planes(plane, scales, queue=(nc.sync, nc.sync), shift=0):
             for q in (0, 2, 1, 3):
-                queue.dma_start(
+                queue[q // 2].dma_start(
                     plane[QUAD * q + shift : QUAD * q + shift + PASSES * ROWS, :].bitcast(I32),
                     scales[:, ROWS * q : ROWS * (q + 1), :].bitcast(I32),
                 )
@@ -87,19 +89,20 @@ def tile_list_msg_relu_biasP_kernel(
         load_names = list(load_words)
         load_at = {name: WORD * sum(load_words[n] for n in load_names[:i]) for i, name in enumerate(load_names)}
         tab_sc = sb("tab_sc", [P, T], U8)
-        nc.gpsimd.memset(tab_sc[:].bitcast(I32), 0)
-        first_zeros = placed(aside, "first_zeros", [P, N // WORD], I32, 0)
+        first_zeros = placed(aside, "first_zeros", [P, FEW], I32, 0)
         nc.gpsimd.memset(first_zeros[:], 0)
+        nc.gpsimd.memset(tab_sc[:].bitcast(I32), 0)
         zeros = placed(loads, "zeros", [P, sum(load_words[n] for n in load_names)], I32, 0)
         nc.vector.memset(zeros[:, : J // WORD], 0)
         ws_sc = sb("ws_sc", [P, PASSES * R], U8)
         nc.vector.memset(ws_sc[:].bitcast(I32), 0)
         wd_sc_raw = sb("wd_sc_raw", [P, N], U8)
-        nc.gpsimd.tensor_copy(wd_sc_raw[:].bitcast(I32), first_zeros[:])
+        nc.gpsimd.tensor_copy(wd_sc_raw[:].bitcast(I32)[:, :FEW], first_zeros[:])
+        nc.gpsimd.memset(wd_sc_raw[:].bitcast(I32)[:, FEW:], 0)
         pages = []
         src_sc1 = sb("src_sc1", [P, J], U8)
         nc.vector.tensor_copy(src_sc1[:].bitcast(I32), zeros[:, : J // WORD])
-        load_two_planes(tab_sc, tab_scales)
+        load_two_planes(tab_sc, tab_scales, (nc.sync, nc.scalar))
 
         tab_w = [placed(aside, "tab_w0", [P, T], I32, 0), placed(loads, "tab_w1", [P, T], I32, load_at["tab_w1"])]
         ws_w.append(placed(loads, "ws_w1", [P, 2 * R], U8, load_at["ws_w1"]))
@@ -383,8 +386,10 @@ def tile_list_msg_relu_biasP_kernel(
         for t in range(PACK):
             nc.sync.dma_start(out_rows[:, t, :], pages[t][:])
             for i, w in enumerate(OUT_WIDTHS):
-                round_copy = nc.vector.tensor_copy if i == 0 and t >= 2 else nc.scalar.copy
-                round_copy(pairs[i][:, t // 2, :, t % 2], pages[t][:, starts[i] : starts[i] + w])
+                first = VECTOR_ROUNDS if i == 0 and t >= 2 else 0
+                if first:
+                    nc.vector.tensor_copy(pairs[i][:, t // 2, :first, t % 2], pages[t][:, :first])
+                nc.scalar.copy(pairs[i][:, t // 2, first:, t % 2], pages[t][:, starts[i] + first : starts[i] + w])
 
         out_sc = sb("out_sc", [P, BANK], U8)
         out_words = out_1[0].rearrange("p t i -> p (t i)").bitcast(I32)
@@ -395,10 +400,12 @@ def tile_list_msg_relu_biasP_kernel(
         def weave(i):
             woven.append(sb(f"woven{i}", [P, OUT_WIDTHS[i] * PACK], BF16))
             word_copy = nc.vector.tensor_copy if i < pieces - SCALAR_WEAVES else nc.scalar.copy
-            word_copy(
-                woven[i][:].bitcast(F32).rearrange("p (c u) -> p c u", u=2),
-                pairs[i][:].rearrange("p u c e -> p u (c e)").bitcast(F32).rearrange("p u c -> p c u"),
-            )
+            parts = (slice(VECTOR_ROUNDS, None), slice(0, VECTOR_ROUNDS)) if i == 0 else (slice(None),)
+            for part in parts:
+                word_copy(
+                    woven[i][:].bitcast(F32).rearrange("p (c u) -> p c u", u=2)[:, part],
+                    pairs[i][:].rearrange("p u c e -> p u (c e)").bitcast(F32).rearrange("p u c -> p c u")[:, part],
+                )
 
         def quantise_piece(i):
             block, first = divmod(starts[i], BANK)

@@ -33,9 +33,9 @@ SOURCE, TARGET = 0, 1
 
 ORDER = ((0, SOURCE), (0, TARGET), (1, TARGET), (1, SOURCE))
 AHEAD_OF_TABLE = 3
-OUT_WIDTHS = (512, 512, 256, 256, 256, 256)
+OUT_WIDTHS = (512, 512, 256, 256, 256, 128, 128)
 VECTOR_ROUNDS = 256
-SCALAR_WEAVES = 2
+SCALAR_WEAVES = 4
 FEW = 8
 
 
@@ -413,8 +413,10 @@ def tile_list_msg_relu_biasP_kernel(
             nc.vector.quantize_mx(
                 out=codes[block][:, cols].bitcast(FP8X4), scales=out_sc[ROWS * block : P, cols], in_=woven[i][:]
             )
-            if block == len(codes) - 1:
-                nc.sync.dma_start(out_words[:, starts[i] : starts[i] + OUT_WIDTHS[i]], codes[block][:, cols])
+            if i == pieces - 2:
+                nc.sync.dma_start(out_words[:, block * BANK : starts[-1]], codes[block][:, : cols.stop])
+            elif i == pieces - 1:
+                nc.sync.dma_start(out_words[:, starts[i] :], codes[block][:, cols])
             elif cols.stop == BANK:
                 nc.sync.dma_start(out_words[:, block * BANK : (block + 1) * BANK], codes[block][:])
 

@@ -26,17 +26,24 @@ ROWS = 4
 BANK = 512
 CHUNK = 2 * P
 CHUNKS = J // CHUNK
+RUN = J // 2
 PER_COLUMN = 16
 WORD = 4
 ALIGN = 64
+FEW_WORDS = 8
 SOURCE, TARGET = 0, 1
 
 ORDER = ((0, SOURCE), (0, TARGET), (1, TARGET), (1, SOURCE))
-AHEAD_OF_TABLE = 3
-OUT_WIDTHS = (512, 512, 256, 256, 256, 128, 128)
+SOURCE_FIRST = ((0, SOURCE), (1, SOURCE), (0, TARGET), (1, TARGET))
+
+FIRST_BANKS = ((0, 1), (2, 3), (4, 5), (3, 6), (7, 4), (5, 3), (7, 4), (5, 3))
+TURN_BANKS = ((6, 7), (2, 6), (2, 6), (2, 6))
+EARLY_BANK, LAG_BANK = 0, 1
+LAST_BANKS = (EARLY_BANK, FIRST_BANKS[-1][1]) + TURN_BANKS[-1]
+
+OUT_WIDTHS = (512, 256, 256, 256, 256, 256, 128, 128)
 VECTOR_ROUNDS = 256
-SCALAR_WEAVES = 4
-FEW = 8
+SCALAR_WEAVES = 3
 
 
 def tile_list_msg_relu_biasP_kernel(
@@ -48,11 +55,11 @@ def tile_list_msg_relu_biasP_kernel(
     with ExitStack() as ctx:
         keep = ctx.enter_context(tc.tile_pool(name="keep", bufs=1))
         loads = ctx.enter_context(tc.tile_pool(name="loads", bufs=1))
-        second_half = ctx.enter_context(tc.tile_pool(name="second_half", bufs=1))
-        aside = ctx.enter_context(tc.tile_pool(name="aside", bufs=1))
-        dealt = ctx.enter_context(tc.tile_pool(name="dealt", bufs=1))
-        mid_h = ctx.enter_context(tc.tile_pool(name="mid_h", bufs=1))
-        head_h = ctx.enter_context(tc.tile_pool(name="head_h", bufs=1))
+        after_target = ctx.enter_context(tc.tile_pool(name="after_target", bufs=1))
+        first_table = ctx.enter_context(tc.tile_pool(name="first_table", bufs=1))
+        after_source = ctx.enter_context(tc.tile_pool(name="after_source", bufs=1))
+        late_h = ctx.enter_context(tc.tile_pool(name="late_h", bufs=1))
+        early_h = ctx.enter_context(tc.tile_pool(name="early_h", bufs=1))
         psum = ctx.enter_context(tc.psum_pool(name="psum", bufs=1))
 
         def sb(name, shape, dtype, tag=None):
@@ -61,14 +68,24 @@ def tile_list_msg_relu_biasP_kernel(
         def placed(pool, name, shape, dtype, offset):
             return pool.tile(shape, dtype, name=name, offset=offset, align_bytes=ALIGN)
 
+        def bank(name, index):
+            return psum.tile([P, BANK], F32, name=name, tag=f"bank{index}")
+
         def entries(list_tile, first, count):
             return list_tile[:, first // PER_COLUMN : (first + count) // PER_COLUMN]
 
-        def load_two_planes(plane, scales, queue=(nc.sync, nc.sync), shift=0):
+        def load_two_planes(plane, scales, upper_queue):
             for q in (0, 2, 1, 3):
-                queue[q // 2].dma_start(
-                    plane[QUAD * q + shift : QUAD * q + shift + PASSES * ROWS, :].bitcast(I32),
+                (nc.sync, upper_queue)[q // 2].dma_start(
+                    plane[QUAD * q : QUAD * q + PASSES * ROWS, :].bitcast(I32),
                     scales[:, ROWS * q : ROWS * (q + 1), :].bitcast(I32),
+                )
+
+        def load_side_by_side(plane, scales, shift):
+            for s in range(ROWS):
+                nc.sync.dma_start(
+                    plane[shift + s : P : QUAD, :].bitcast(I32).rearrange("p (a r) -> p a r", a=PASSES),
+                    scales[:, s : ROWS * QUADRANTS : ROWS, :].rearrange("a q r -> q a r").bitcast(I32),
                 )
 
         lists = [keep.tile([P, J // PER_COLUMN], U16, name=name) for name in ("src_list", "tgt_list")]
@@ -81,41 +98,36 @@ def tile_list_msg_relu_biasP_kernel(
         load_ws(0)
         nc.sync.dma_start(lists[TARGET][:], offs2)
 
-        wd_bytes = WORD * PASSES * N
         load_words = {
             "tab_w1": T, "wt_w0": R, "ws_w1": R // 2, "wt_w1": R, "wd_raw": PASSES * N, "edge_w": J,
             "wt_sc": PASSES * R // WORD, "ident": P, "page0": T, "page1": T, "page2": T, "bias": 2 * T,
         }
         load_names = list(load_words)
         load_at = {name: WORD * sum(load_words[n] for n in load_names[:i]) for i, name in enumerate(load_names)}
+
         tab_sc = sb("tab_sc", [P, T], U8)
-        first_zeros = placed(aside, "first_zeros", [P, FEW], I32, 0)
-        nc.gpsimd.memset(first_zeros[:], 0)
+        few_zeros = placed(first_table, "few_zeros", [P, FEW_WORDS], I32, 0)
+        nc.gpsimd.memset(few_zeros[:], 0)
         nc.gpsimd.memset(tab_sc[:].bitcast(I32), 0)
         zeros = placed(loads, "zeros", [P, sum(load_words[n] for n in load_names)], I32, 0)
         nc.vector.memset(zeros[:, : J // WORD], 0)
         ws_sc = sb("ws_sc", [P, PASSES * R], U8)
         nc.vector.memset(ws_sc[:].bitcast(I32), 0)
         wd_sc_raw = sb("wd_sc_raw", [P, N], U8)
-        nc.gpsimd.tensor_copy(wd_sc_raw[:].bitcast(I32)[:, :FEW], first_zeros[:])
-        nc.gpsimd.memset(wd_sc_raw[:].bitcast(I32)[:, FEW:], 0)
-        pages = []
+        nc.gpsimd.tensor_copy(wd_sc_raw[:].bitcast(I32)[:, :FEW_WORDS], few_zeros[:])
+        nc.gpsimd.memset(wd_sc_raw[:].bitcast(I32)[:, FEW_WORDS:], 0)
         src_sc1 = sb("src_sc1", [P, J], U8)
         nc.vector.tensor_copy(src_sc1[:].bitcast(I32), zeros[:, : J // WORD])
-        load_two_planes(tab_sc, tab_scales, (nc.sync, nc.scalar))
+        load_two_planes(tab_sc, tab_scales, nc.scalar)
 
-        tab_w = [placed(aside, "tab_w0", [P, T], I32, 0), placed(loads, "tab_w1", [P, T], I32, load_at["tab_w1"])]
+        tab_w = [
+            placed(first_table, "tab_w0", [P, T], I32, 0),
+            placed(loads, "tab_w1", [P, T], I32, load_at["tab_w1"]),
+        ]
         ws_w.append(placed(loads, "ws_w1", [P, 2 * R], U8, load_at["ws_w1"]))
         wt_w = [placed(loads, f"wt_w{a}", [P, R], I32, load_at[f"wt_w{a}"]) for a in range(PASSES)]
         wt_sc = placed(loads, "wt_sc", [P, PASSES * R], U8, load_at["wt_sc"])
         nc.gpsimd.memset(wt_sc[:].bitcast(I32), 0)
-
-        def load_w_scales(queue, plane, scales, shift):
-            for s in range(ROWS):
-                queue.dma_start(
-                    plane[shift + s : P : QUAD, :].bitcast(I32).rearrange("p (a r) -> p a r", a=PASSES),
-                    scales[:, s : ROWS * QUADRANTS : ROWS, :].rearrange("a q r -> q a r").bitcast(I32),
-                )
 
         def load_tab(a):
             nc.sync.dma_start(tab_w[a][:], tab_words[a].rearrange("p t i -> p (t i)").bitcast(I32))
@@ -124,10 +136,10 @@ def tile_list_msg_relu_biasP_kernel(
             nc.sync.dma_start(wt_w[a][:], wt_words[a].rearrange("p r i -> p (r i)").bitcast(I32))
 
         load_tab(0)
-        load_w_scales(nc.sync, ws_sc, ws_scales, 0)
+        load_side_by_side(ws_sc, ws_scales, 0)
         load_tab(1)
         load_wt(0)
-        load_w_scales(nc.sync, wt_sc, wt_scales, ROWS)
+        load_side_by_side(wt_sc, wt_scales, ROWS)
         load_wt(1)
         load_ws(1)
         wd_raw = placed(loads, "wd_raw", [P, PASSES, N], I32, load_at["wd_raw"])
@@ -137,63 +149,60 @@ def tile_list_msg_relu_biasP_kernel(
         ident = placed(loads, "ident", [P, P], F32, load_at["ident"])
         make_identity(nc, ident[:])
 
-        def add_page(page):
+        pages = []
+
+        def add_page(offset):
+            page = placed(loads, f"page{len(pages)}", [P, T], F32, offset)
             pages.append(page)
             nc.gpsimd.memset(page[:].bitcast(I32), 0)
 
-        add_page(placed(loads, "page0", [P, T], F32, load_at["page0"]))
-        add_page(placed(loads, "page1", [P, T], F32, load_at["page1"]))
-        add_page(placed(loads, "page2", [P, T], F32, load_at["page2"]))
+        for t in range(PACK - 1):
+            add_page(load_at[f"page{t}"])
 
-        HALF = J // 2
-        part_bytes = WORD * CHUNK
+        chunk_bytes = WORD * CHUNK
         v_sc = {}
-
-        def gather_scales(side, half, dst):
-            v_sc[side, half] = dst
-            nc.vector.tensor_copy(dst[:], tab_sc[:].indirect(entries(lists[side], half * HALF, HALF)))
-
-        def shift_scales(queue, half):
-            for q in range(QUADRANTS):
-                queue.dma_start(
-                    src_sc1[QUAD * q : QUAD * q + ROWS, half * HALF : (half + 1) * HALF].bitcast(I32),
-                    v_sc[SOURCE, half][QUAD * q + ROWS : QUAD * q + 2 * ROWS, :].bitcast(I32),
-                )
-
         picked = {}
 
-        def gather(c, a, side, dst=None):
-            if dst is None:
-                dst = sb(f"picked{c}_{a}_{side}", [P, CHUNK], U32)[:]
-            picked[c, a, side] = dst
-            nc.vector.tensor_copy(dst, tab_w[a][:].bitcast(U32).indirect(entries(lists[side], c * CHUNK, CHUNK)))
+        def gather_scales(side, run, dst):
+            v_sc[side, run] = dst
+            nc.vector.tensor_copy(dst[:], tab_sc[:].indirect(entries(lists[side], run * RUN, RUN)))
 
-        def gather_two(a, side):
-            dst = sb(f"picked12_{a}_{side}", [P, 2 * CHUNK], U32)
-            for i in range(2):
-                picked[1 + i, a, side] = dst[:, i * CHUNK : (i + 1) * CHUNK]
-            nc.vector.tensor_copy(dst[:], tab_w[a][:].bitcast(U32).indirect(entries(lists[side], CHUNK, 2 * CHUNK)))
+        def shift_scales(run):
+            for q in range(QUADRANTS):
+                nc.sync.dma_start(
+                    src_sc1[QUAD * q : QUAD * q + ROWS, run * RUN : (run + 1) * RUN].bitcast(I32),
+                    v_sc[SOURCE, run][QUAD * q + ROWS : QUAD * q + 2 * ROWS, :].bitcast(I32),
+                )
 
-        gather_scales(SOURCE, 0, sb("src_sc_a", [P, HALF], U8))
-        shift_scales(nc.sync, 0)
-        gather_scales(TARGET, 0, sb("tgt_sc_a", [P, HALF], U8))
-        gather(0, 0, SOURCE)
-        gather_two(0, SOURCE)
-        gather(0, 0, TARGET)
-        gather_two(0, TARGET)
-        gather(0, 1, TARGET, placed(second_half, "picked0_1t", [P, CHUNK], U32, HALF - ALIGN)[:])
-        gather(0, 1, SOURCE, placed(dealt, "picked0_1s", [P, CHUNK], U32, wd_bytes - ALIGN)[:])
-        gather_two(1, SOURCE)
-        gather_two(1, TARGET)
+        def gather(first_chunk, count, a, side, dst):
+            for i in range(count):
+                picked[first_chunk + i, a, side] = dst[:, i * CHUNK : (i + 1) * CHUNK]
+            window = tab_w[a][:].bitcast(U32)
+            nc.vector.tensor_copy(dst, window.indirect(entries(lists[side], first_chunk * CHUNK, count * CHUNK)))
+
+        def gather_middle(a, side):
+            gather(1, 2, a, side, sb(f"picked12_{a}_{side}", [P, 2 * CHUNK], U32)[:])
+
+        gather_scales(SOURCE, 0, sb("src_sc_a", [P, RUN], U8))
+        shift_scales(0)
+        gather_scales(TARGET, 0, sb("tgt_sc_a", [P, RUN], U8))
+        for side in (SOURCE, TARGET):
+            gather(0, 1, 0, side, sb(f"picked0_0_{side}", [P, CHUNK], U32)[:])
+            gather_middle(0, side)
+        gather(0, 1, 1, TARGET, placed(after_target, "picked0_1t", [P, CHUNK], U32, RUN - ALIGN)[:])
+        gather(0, 1, 1, SOURCE, placed(after_source, "picked0_1s", [P, CHUNK], U32, 0)[:])
+        gather_middle(1, SOURCE)
+        gather_middle(1, TARGET)
 
         nc.sync.dma_start(wd_raw[:], wd_words.rearrange("a p n i -> p a (n i)").bitcast(I32))
-        load_two_planes(wd_sc_raw, wd_scales)
+        load_two_planes(wd_sc_raw, wd_scales, nc.sync)
         nc.sync.dma_start(edge_w[:], wgo)
         nc.sync.dma_start(bias[:, :PACK], b.rearrange("(p t) -> p t", t=PACK))
 
-        gather_scales(SOURCE, 1, placed(second_half, "src_sc_b", [P, HALF], U8, 0))
-        shift_scales(nc.sync, 1)
-        gather_scales(TARGET, 1, placed(second_half, "tgt_sc_b", [P, HALF], U8, HALF + part_bytes - 2 * ALIGN))
+        gather_scales(SOURCE, 1, placed(after_target, "src_sc_b", [P, RUN], U8, 0))
+        shift_scales(1)
+        gather_scales(TARGET, 1, placed(after_target, "tgt_sc_b", [P, RUN], U8, RUN + chunk_bytes - 2 * ALIGN))
+
         wd_w = sb("wd_w", [P, PASSES, N], I32)
         nc.gpsimd.tensor_copy(
             wd_w[:].rearrange("p a (t m) -> p a t m", t=PACK), wd_raw[:].rearrange("p a (m t) -> p a t m", t=PACK)
@@ -202,27 +211,21 @@ def tile_list_msg_relu_biasP_kernel(
         nc.gpsimd.tensor_copy(
             wd_sc[:].rearrange("p (t m) -> p t m", t=PACK), wd_sc_raw[:].rearrange("p (m t) -> p t m", t=PACK)
         )
-        last0 = placed(dealt, "picked3_0", [P, 2, CHUNK], U32, wd_bytes + part_bytes - 2 * ALIGN)
-        gather(3, 0, SOURCE, last0[:, 0, :])
-        gather(3, 0, TARGET, last0[:, 1, :])
+        picked3_0 = placed(after_source, "picked3_0", [P, 2, CHUNK], U32, chunk_bytes - ALIGN)
+        for side in (SOURCE, TARGET):
+            gather(CHUNKS - 1, 1, 0, side, picked3_0[:, side, :])
 
-        FIRST_BANKS = ((0, 1), (2, 3), (4, 5), (3, 6), (7, 4), (5, 3), (7, 4), (5, 3))
-        TURN_BANKS = ((6, 7), (2, 6), (2, 6), (2, 6))
-
-        def bank(name, i):
-            return psum.tile([P, BANK], F32, name=name, tag=f"bank{i}")
-
-        def first_pass(acc, group, half, a, side, order=ORDER):
+        def first_pass(acc, group, half, a, side, order):
             in_chunk = slice(P * (group % 2), P * (group % 2 + 1))
-            edges = slice(P * group, P * (group + 1))
-            in_half = slice(P * (group % 4), P * (group % 4 + 1))
+            run, first = divmod(P * group, RUN)
+            in_run = slice(first, first + P)
             plane_cols = slice(a * R + half * BANK, a * R + (half + 1) * BANK)
             if side == SOURCE:
-                v_scale = src_sc1[:, edges] if a else v_sc[SOURCE, group // 4][:, in_half]
+                v_scale = src_sc1[:, P * group : P * (group + 1)] if a else v_sc[SOURCE, run][:, in_run]
                 w = ws_w[a][:, 2 * half * BANK : 2 * (half + 1) * BANK].bitcast(FP4X4)
                 w_scale = ws_sc[:, plane_cols]
             else:
-                v_scale = v_sc[TARGET, group // 4][ROWS * a : P, in_half]
+                v_scale = v_sc[TARGET, run][ROWS * a : P, in_run]
                 w = wt_w[a][:, half * BANK : (half + 1) * BANK].bitcast(FP8X4)
                 w_scale = wt_sc[ROWS:P, plane_cols]
             nc.tensor.matmul_mx(
@@ -231,34 +234,33 @@ def tile_list_msg_relu_biasP_kernel(
                 start=((a, side) == order[0]), stop=((a, side) == order[-1]),
             )
 
-        h_ts = {}
-
-        def first_half(group, half, order, later=False):
-            acc = bank(f"a{group}_{half}", FIRST_BANKS[group][half])
-            for a, side in order:
-                first_pass(acc, group, half, a, side)
-            if later:
-                return acc
-            relu(group, half, acc)
+        h_edge = {}
+        h_edge_at = {2: (early_h, 0), 1: (early_h, R), 3: (early_h, 2 * R), 5: (late_h, 0), 7: (late_h, 2 * R)}
 
         def relu(group, half, acc):
-            if group not in h_ts:
-                if group in (1, 2, 3):
-                    h_ts[group] = placed(head_h, f"h_t{group}", [P, R], BF16, {2: 0, 1: R, 3: 2 * R}[group])
-                elif group in (5, 7):
-                    h_ts[group] = placed(mid_h, f"h_t{group}", [P, R], BF16, (group - 5) * R)
+            if group not in h_edge:
+                if group in h_edge_at:
+                    pool, offset = h_edge_at[group]
+                    h_edge[group] = placed(pool, f"h_edge{group}", [P, R], BF16, offset)
                 else:
-                    h_ts[group] = sb(f"h_t{group}", [P, R], BF16)
+                    h_edge[group] = sb(f"h_edge{group}", [P, R], BF16)
             nc.scalar.activation(
-                h_ts[group][:, half * BANK : (half + 1) * BANK].rearrange("j (u p e) -> j u p e", u=2, e=2),
+                h_edge[group][:, half * BANK : (half + 1) * BANK].rearrange("j (u p e) -> j u p e", u=2, e=2),
                 acc[:].rearrange("j (p u e) -> j u p e", u=2, e=2),
                 ACT.Relu,
             )
 
+        def first_half(group, half):
+            acc = bank(f"a{group}_{half}", FIRST_BANKS[group][half])
+            for a, side in ORDER:
+                first_pass(acc, group, half, a, side, ORDER)
+            relu(group, half, acc)
+
         def turn(group, h_in):
             turned = bank(f"turned{group}", TURN_BANKS[group // 2][group % 2])
+            pair_words = h_edge[group][:].bitcast(F32)
             for s in range(2 * PASSES):
-                nc.tensor.transpose(turned[:, P * s : P * (s + 1)], h_ts[group][:].bitcast(F32)[:, P * s : P * (s + 1)], ident[:])
+                nc.tensor.transpose(turned[:, P * s : P * (s + 1)], pair_words[:, P * s : P * (s + 1)], ident[:])
             h_words = h_in[:].bitcast(F32).rearrange("p (a j u) -> p a j u", a=PASSES, u=2)
             nc.scalar.copy(
                 h_words[:, :, P * (group % 2) : P * (group % 2 + 1), :],
@@ -266,6 +268,14 @@ def tile_list_msg_relu_biasP_kernel(
             )
 
         h_w, h_sc = {}, {}
+
+        def quantise_h(c):
+            h_in = sb(f"h_in{c}", [P, PASSES * CHUNK * PACK], BF16)
+            for group in (2 * c, 2 * c + 1):
+                turn(group, h_in)
+            h_w[c] = sb(f"h_w{c}", [P, PASSES * CHUNK], U32)
+            h_sc[c] = sb(f"h_sc{c}", [P, PASSES * CHUNK], U8)
+            nc.vector.quantize_mx(out=h_w[c][:].bitcast(FP8X4), scales=h_sc[c][:], in_=h_in[:])
 
         def second(acc, c, t):
             for a in range(PASSES):
@@ -277,108 +287,85 @@ def tile_list_msg_relu_biasP_kernel(
                     start=(a == 0), stop=(a == PASSES - 1),
                 )
 
-        def add_bias(dst, acc, t):
-            nc.scalar.activation(dst, acc, ACT.Identity, bias=bias[:, t : t + 1])
-
-        def scatter(t, first, count, src):
+        def put(t, first_chunk, count, msg, acc):
+            first, edges = first_chunk * CHUNK, count * CHUNK
+            nc.scalar.activation(msg, acc, ACT.Identity, bias=bias[:, t : t + 1])
             nc.vector.tensor_tensor(
-                pages[t][:].indirect(entries(lists[TARGET], first, count)), src, edge_w[:, first : first + count], MULT,
+                pages[t][:].indirect(entries(lists[TARGET], first, edges)), msg, edge_w[:, first : first + edges], MULT,
             )
 
-        held = {}
+        def part(acc, i):
+            return acc[:, i * CHUNK : (i + 1) * CHUNK]
+
+        lagging = {}
 
         def second_stage(c):
-            acc = bank(f"early{c}", 0)
-            acc2 = bank(f"lag{c}", 1)
+            early = bank(f"early{c}", EARLY_BANK)
+            lagging[c] = bank(f"lag{c}", LAG_BANK)
+            for t in range(PACK):
+                second(part((early, lagging[c])[t // 2], t % 2), c, t)
             for t in range(2):
-                second(acc[:, t * CHUNK : (t + 1) * CHUNK], c, t)
-            for t in range(2):
-                second(acc2[:, t * CHUNK : (t + 1) * CHUNK], c, 2 + t)
-            for t in range(2):
-                m = sb(f"msg{c}_{t}", [P, CHUNK], F32)
-                add_bias(m[:], acc[:, t * CHUNK : (t + 1) * CHUNK], t)
-                scatter(t, c * CHUNK, CHUNK, m[:])
-            held[c] = acc2
+                put(t, c, 1, sb(f"msg{c}_{t}", [P, CHUNK], F32)[:], part(early, t))
 
-        def lagging_pages(c, which):
-            for t in which:
-                if c == 0:
-                    m = placed(head_h, f"msg0_{2 + t}", [P, CHUNK], F32, (3 - t) * R)
-                else:
-                    m = placed(mid_h, f"msg1_{2 + t}", [P, CHUNK], F32, t * 2 * R)
-                add_bias(m[:], held[c][:, t * CHUNK : (t + 1) * CHUNK], 2 + t)
-                scatter(2 + t, c * CHUNK, CHUNK, m[:])
+        def lagging_page(c, t, pool, offset):
+            put(t, c, 1, placed(pool, f"msg{c}_{t}", [P, CHUNK], F32, offset)[:], part(lagging[c], t - 2))
 
-        def quantise_h(c):
-            h_in = sb(f"h_in{c}", [P, PASSES * CHUNK * PACK], BF16)
-            for group in (2 * c, 2 * c + 1):
-                turn(group, h_in)
-            h_w[c] = sb(f"h_w{c}", [P, PASSES * CHUNK], U32)
-            h_sc[c] = sb(f"h_sc{c}", [P, PASSES * CHUNK], U8)
-            nc.vector.quantize_mx(out=h_w[c][:].bitcast(FP8X4), scales=h_sc[c][:], in_=h_in[:])
-            if c > 0:
-                lagging_pages(*((0, (0, 1)), (1, (0,)), (1, (1,)))[c - 1])
-            if c == 0:
-                last1 = sb("picked3_1", [P, 2, CHUNK], U32, "h_in0")
-                gather(3, 1, TARGET, last1[:, 0, :])
-                gather(3, 1, SOURCE, last1[:, 1, :])
-                add_page(placed(loads, "page3", [P, T], F32, load_at["tab_w1"]))
-
-        order = ORDER
-        banks = {(g, half): bank(f"a{g}_{half}", FIRST_BANKS[g][half]) for g in range(3) for half in range(2)}
-        for g, half in banks:
-            first_pass(banks[g, half], g, half, *ORDER[0])
-        SOURCE_FIRST = ((0, SOURCE), (1, SOURCE), (0, TARGET), (1, TARGET))
-
-        def finish(g, half):
-            for a, side in SOURCE_FIRST[1:]:
-                first_pass(banks[g, half], g, half, a, side, SOURCE_FIRST)
-
+        opened = {(g, half): bank(f"a{g}_{half}", FIRST_BANKS[g][half]) for g in range(3) for half in range(2)}
+        for g, half in opened:
+            first_pass(opened[g, half], g, half, *ORDER[0], ORDER)
         for a, side in ORDER[1:]:
             for g in range(2):
                 for half in range(2):
-                    first_pass(banks[g, half], g, half, a, side)
+                    first_pass(opened[g, half], g, half, a, side, ORDER)
                     if (a, side) == ORDER[-1]:
-                        relu(g, half, banks[g, half])
-        finish(2, 0)
-        finish(2, 1)
+                        relu(g, half, opened[g, half])
+        for half in range(2):
+            for a, side in SOURCE_FIRST[1:]:
+                first_pass(opened[2, half], 2, half, a, side, SOURCE_FIRST)
+
         quantise_h(0)
-        relu(2, 0, banks[2, 0])
-        relu(2, 1, banks[2, 1])
-        first_half(3, 0, order)
-        first_half(3, 1, order)
+        picked3_1 = sb("picked3_1", [P, 2, CHUNK], U32, "h_in0")
+        for i, side in enumerate((TARGET, SOURCE)):
+            gather(CHUNKS - 1, 1, 1, side, picked3_1[:, i, :])
+        add_page(load_at["tab_w1"])
+
+        for half in range(2):
+            relu(2, half, opened[2, half])
+        first_half(3, 0)
+        first_half(3, 1)
         second_stage(0)
-        first_half(4, 0, order)
+        first_half(4, 0)
         quantise_h(1)
-        first_half(4, 1, order)
-        first_half(5, 0, order)
-        first_half(5, 1, order)
+        lagging_page(0, 2, early_h, 3 * R)
+        lagging_page(0, 3, early_h, 2 * R)
+        first_half(4, 1)
+        first_half(5, 0)
+        first_half(5, 1)
         second_stage(1)
         quantise_h(2)
-        first_half(6, 0, order)
-        first_half(6, 1, order)
-        first_half(7, 0, order)
-        first_half(7, 1, order)
-        LAST_BANKS = (0, 3, 2, 6)
+        lagging_page(1, 2, *h_edge_at[5])
+        for group in (6, 7):
+            for half in range(2):
+                first_half(group, half)
+
         last = [bank("last0", LAST_BANKS[0])]
         msgs = [sb(f"msg_last{t}", [P, 2 * CHUNK], F32) for t in range(PACK)]
-        second(last[0][:, :CHUNK], 2, 0)
-        add_bias(msgs[0][:, :CHUNK], last[0][:, :CHUNK], 0)
-        scatter(0, 2 * CHUNK, CHUNK, msgs[0][:, :CHUNK])
-        quantise_h(CHUNKS - 1)
+        second(part(last[0], 0), 2, 0)
+        put(0, 2, 1, part(msgs[0], 0), part(last[0], 0))
+        quantise_h(3)
+        lagging_page(1, 3, *h_edge_at[7])
         last.extend(bank(f"last{t}", LAST_BANKS[t]) for t in range(1, PACK))
-        for t in (1, 2, 3):
-            second(last[t][:, :CHUNK], 2, t)
-        second(last[0][:, CHUNK:], 3, 0)
-        add_bias(msgs[0][:, CHUNK:], last[0][:, CHUNK:], 0)
-        scatter(0, 3 * CHUNK, CHUNK, msgs[0][:, CHUNK:])
-        for t in (1, 2, 3):
-            second(last[t][:, CHUNK:], 3, t)
-            add_bias(msgs[t][:], last[t][:], t)
-            scatter(t, 2 * CHUNK, 2 * CHUNK, msgs[t][:])
+        for t in range(1, PACK):
+            second(part(last[t], 0), 2, t)
+        second(part(last[0], 1), 3, 0)
+        put(0, 3, 1, part(msgs[0], 1), part(last[0], 1))
+        for t in range(1, PACK):
+            second(part(last[t], 1), 3, t)
+            put(t, 2, 2, msgs[t][:], last[t][:])
 
         out_rows = out_0.rearrange("(p t) c -> p t c", t=PACK)
-        starts = [sum(OUT_WIDTHS[:i]) for i in range(len(OUT_WIDTHS))]
+        pieces = len(OUT_WIDTHS)
+        starts = [sum(OUT_WIDTHS[:i]) for i in range(pieces)]
         pairs = [
             placed(loads, f"pairs{i}", [P, 2, w, 2], BF16, load_at["bias"] + 2 * WORD * starts[i])
             for i, w in enumerate(OUT_WIDTHS)
@@ -393,18 +380,17 @@ def tile_list_msg_relu_biasP_kernel(
 
         out_sc = sb("out_sc", [P, BANK], U8)
         out_words = out_1[0].rearrange("p t i -> p (t i)").bitcast(I32)
-        pieces = len(OUT_WIDTHS)
-        woven = []
         codes = [sb(f"codes{i}", [P, BANK], I32) for i in range(T // BANK)]
+        woven = []
 
         def weave(i):
             woven.append(sb(f"woven{i}", [P, OUT_WIDTHS[i] * PACK], BF16))
             word_copy = nc.vector.tensor_copy if i < pieces - SCALAR_WEAVES else nc.scalar.copy
-            parts = (slice(VECTOR_ROUNDS, None), slice(0, VECTOR_ROUNDS)) if i == 0 else (slice(None),)
-            for part in parts:
+            shares = (slice(VECTOR_ROUNDS, None), slice(0, VECTOR_ROUNDS)) if i == 0 else (slice(None),)
+            for share in shares:
                 word_copy(
-                    woven[i][:].bitcast(F32).rearrange("p (c u) -> p c u", u=2)[:, part],
-                    pairs[i][:].rearrange("p u c e -> p u (c e)").bitcast(F32).rearrange("p u c -> p c u")[:, part],
+                    woven[i][:].bitcast(F32).rearrange("p (c u) -> p c u", u=2)[:, share],
+                    pairs[i][:].rearrange("p u c e -> p u (c e)").bitcast(F32).rearrange("p u c -> p c u")[:, share],
                 )
 
         def quantise_piece(i):
@@ -413,10 +399,10 @@ def tile_list_msg_relu_biasP_kernel(
             nc.vector.quantize_mx(
                 out=codes[block][:, cols].bitcast(FP8X4), scales=out_sc[ROWS * block : P, cols], in_=woven[i][:]
             )
-            if i == pieces - 2:
-                nc.sync.dma_start(out_words[:, block * BANK : starts[-1]], codes[block][:, : cols.stop])
-            elif i == pieces - 1:
+            if i == pieces - 1:
                 nc.sync.dma_start(out_words[:, starts[i] :], codes[block][:, cols])
+            elif i == pieces - 2:
+                nc.sync.dma_start(out_words[:, block * BANK : starts[-1]], codes[block][:, : cols.stop])
             elif cols.stop == BANK:
                 nc.sync.dma_start(out_words[:, block * BANK : (block + 1) * BANK], codes[block][:])
 

@@ -1,7 +1,6 @@
 from contextlib import ExitStack
 
 import concourse.mybir as mybir
-from concourse.masks import make_identity
 
 K, R, N, T, J = 1024, 1024, 512, 2048, 1024
 FLOPS = 2 * J * (2 * K * R + R * N)
@@ -32,14 +31,12 @@ WORD = 4
 ALIGN = 64
 FEW_WORDS = 8
 SOURCE, TARGET = 0, 1
+AS_THEY_LIE = P - PASSES * ROWS * QUADRANTS
 
-ORDER = ((0, SOURCE), (0, TARGET), (1, TARGET), (1, SOURCE))
-SOURCE_FIRST = ((0, SOURCE), (1, SOURCE), (0, TARGET), (1, TARGET))
-
-FIRST_BANKS = ((0, 1), (2, 3), (4, 5), (3, 6), (7, 4), (5, 3), (7, 4), (5, 3))
-TURN_BANKS = ((6, 7), (2, 6), (2, 6), (2, 6))
-EARLY_BANK, LAG_BANK = 0, 1
-LAST_BANKS = (EARLY_BANK, FIRST_BANKS[-1][1]) + TURN_BANKS[-1]
+FIRST_BANKS = ((0, 1, 2, 3), (0, 1, 2, 3), (4, 0, 1, 2), (3, 5, 4, 0))
+SECOND_BANKS = ((4, 5), (6, 7))
+LAST_BANKS = (6, 1, 2, 3)
+MOVING = (P, CHUNK, CHUNK, CHUNK)
 
 OUT_WIDTHS = (512, 256, 256, 256, 256, 256, 128, 128)
 VECTOR_ROUNDS = 256
@@ -54,12 +51,10 @@ def tile_list_msg_relu_biasP_kernel(
 
     with ExitStack() as ctx:
         keep = ctx.enter_context(tc.tile_pool(name="keep", bufs=1))
-        loads = ctx.enter_context(tc.tile_pool(name="loads", bufs=1))
-        after_target = ctx.enter_context(tc.tile_pool(name="after_target", bufs=1))
-        first_table = ctx.enter_context(tc.tile_pool(name="first_table", bufs=1))
-        after_source = ctx.enter_context(tc.tile_pool(name="after_source", bufs=1))
-        late_h = ctx.enter_context(tc.tile_pool(name="late_h", bufs=1))
-        early_h = ctx.enter_context(tc.tile_pool(name="early_h", bufs=1))
+        lag0 = ctx.enter_context(tc.tile_pool(name="lag0", bufs=1))
+        lag1 = ctx.enter_context(tc.tile_pool(name="lag1", bufs=1))
+        lag3 = ctx.enter_context(tc.tile_pool(name="lag3", bufs=1))
+        lag2 = ctx.enter_context(tc.tile_pool(name="lag2", bufs=1))
         psum = ctx.enter_context(tc.psum_pool(name="psum", bufs=1))
 
         def sb(name, shape, dtype, tag=None):
@@ -74,105 +69,150 @@ def tile_list_msg_relu_biasP_kernel(
         def entries(list_tile, first, count):
             return list_tile[:, first // PER_COLUMN : (first + count) // PER_COLUMN]
 
-        def load_two_planes(plane, scales, upper_queue):
+        def load_two_planes(queues, plane, scales, shift):
             for q in (0, 2, 1, 3):
-                (nc.sync, upper_queue)[q // 2].dma_start(
-                    plane[QUAD * q : QUAD * q + PASSES * ROWS, :].bitcast(I32),
+                queues[q // 2].dma_start(
+                    plane[QUAD * q + shift : QUAD * q + shift + PASSES * ROWS, :].bitcast(I32),
                     scales[:, ROWS * q : ROWS * (q + 1), :].bitcast(I32),
                 )
 
-        def load_side_by_side(plane, scales, shift):
+        def load_side_by_side(queue, plane, scales):
             for s in range(ROWS):
-                nc.sync.dma_start(
-                    plane[shift + s : P : QUAD, :].bitcast(I32).rearrange("p (a r) -> p a r", a=PASSES),
+                queue.dma_start(
+                    plane[s : P : QUAD, :].bitcast(I32).rearrange("p (a r) -> p a r", a=PASSES),
                     scales[:, s : ROWS * QUADRANTS : ROWS, :].rearrange("a q r -> q a r").bitcast(I32),
                 )
 
         lists = [keep.tile([P, J // PER_COLUMN], U16, name=name) for name in ("src_list", "tgt_list")]
-        ws_w = [sb("ws_w0", [P, 2 * R], U8)]
-
-        def load_ws(a):
-            nc.sync.dma_start(ws_w[a][:].bitcast(I32), ws_words[a].bitcast(I32))
-
         nc.sync.dma_start(lists[SOURCE][:], offs)
-        load_ws(0)
+        rows = sb("rows", [P, T], U8)
+        nc.scalar.dma_start(
+            rows[AS_THEY_LIE:P, :].bitcast(I32), tab_scales.rearrange("a q t -> (a q) t").bitcast(I32)
+        )
         nc.sync.dma_start(lists[TARGET][:], offs2)
 
-        load_words = {
-            "tab_w1": T, "wt_w0": R, "ws_w1": R // 2, "wt_w1": R, "wd_raw": PASSES * N, "edge_w": J,
-            "wt_sc": PASSES * R // WORD, "ident": P, "page0": T, "page1": T, "page2": T, "bias": 2 * T,
+        words = {
+            "first": {"tab_w0": T, "ws_raw": R},
+            "second": {"wt_raw": PASSES * R, "page0": T, "page1": T, "wt_sc_raw": T},
+            "third": {"tab_w1": T},
+            "fourth": {"wd_raw": PASSES * N, "edge_w": J, "bias": 2 * T},
         }
-        load_names = list(load_words)
-        load_at = {name: WORD * sum(load_words[n] for n in load_names[:i]) for i, name in enumerate(load_names)}
+        pools = {name: ctx.enter_context(tc.tile_pool(name=name, bufs=1)) for name in words}
+        at = {}
+        for name in words:
+            names = list(words[name])
+            for i, tile_name in enumerate(names):
+                at[tile_name] = (pools[name], WORD * sum(words[name][n] for n in names[:i]))
+
+        def held(name, shape, dtype, place=None):
+            pool, offset = at[place or name]
+            return placed(pool, name, shape, dtype, offset)
+
+        def zeros(name, engine, count):
+            tile = placed(pools[name], f"zeros_{name}", [P, sum(words[name].values())], I32, 0)
+            engine.memset(tile[:, :count], 0)
+            return tile[:, :count]
 
         tab_sc = sb("tab_sc", [P, T], U8)
-        few_zeros = placed(first_table, "few_zeros", [P, FEW_WORDS], I32, 0)
-        nc.gpsimd.memset(few_zeros[:], 0)
-        nc.gpsimd.memset(tab_sc[:].bitcast(I32), 0)
-        zeros = placed(loads, "zeros", [P, sum(load_words[n] for n in load_names)], I32, 0)
-        nc.vector.memset(zeros[:, : J // WORD], 0)
-        ws_sc = sb("ws_sc", [P, PASSES * R], U8)
-        nc.vector.memset(ws_sc[:].bitcast(I32), 0)
         wd_sc_raw = sb("wd_sc_raw", [P, N], U8)
-        nc.gpsimd.tensor_copy(wd_sc_raw[:].bitcast(I32)[:, :FEW_WORDS], few_zeros[:])
-        nc.gpsimd.memset(wd_sc_raw[:].bitcast(I32)[:, FEW_WORDS:], 0)
-        src_sc1 = sb("src_sc1", [P, J], U8)
-        nc.vector.tensor_copy(src_sc1[:].bitcast(I32), zeros[:, : J // WORD])
-        load_two_planes(tab_sc, tab_scales, nc.scalar)
-
-        tab_w = [
-            placed(first_table, "tab_w0", [P, T], I32, 0),
-            placed(loads, "tab_w1", [P, T], I32, load_at["tab_w1"]),
-        ]
-        ws_w.append(placed(loads, "ws_w1", [P, 2 * R], U8, load_at["ws_w1"]))
-        wt_w = [placed(loads, f"wt_w{a}", [P, R], I32, load_at[f"wt_w{a}"]) for a in range(PASSES)]
-        wt_sc = placed(loads, "wt_sc", [P, PASSES * R], U8, load_at["wt_sc"])
-        nc.gpsimd.memset(wt_sc[:].bitcast(I32), 0)
+        moved = sb("moved", [P, PASSES * RUN], U8)
+        shifted = placed(lag0, "shifted", [P, RUN], U8, WORD * CHUNK - RUN // 2)
+        ws_sc_raw = sb("ws_sc_raw", [P, PASSES * R], U8)
+        zeros1 = zeros("first", nc.gpsimd, FEW_WORDS)
+        nc.gpsimd.memset(tab_sc[:].bitcast(I32), 0)
+        nc.gpsimd.tensor_copy(wd_sc_raw[:].bitcast(I32)[:, :FEW_WORDS], zeros1)
+        zeros3 = zeros("third", nc.gpsimd, FEW_WORDS)
+        zeros4 = zeros("fourth", nc.gpsimd, PASSES * RUN // WORD - FEW_WORDS)
+        nc.vector.memset(rows[:AS_THEY_LIE, :].bitcast(I32), 0)
+        zeros2 = zeros("second", nc.vector, RUN // WORD)
+        nc.vector.memset(ws_sc_raw[:].bitcast(I32), 0)
+        nc.vector.tensor_copy(shifted[:].bitcast(I32), zeros2)
+        load_two_planes((nc.sync, nc.scalar), tab_sc, tab_scales, 0)
 
         def load_tab(a):
             nc.sync.dma_start(tab_w[a][:], tab_words[a].rearrange("p t i -> p (t i)").bitcast(I32))
 
-        def load_wt(a):
-            nc.sync.dma_start(wt_w[a][:], wt_words[a].rearrange("p r i -> p (r i)").bitcast(I32))
-
+        tab_w = [held("tab_w0", [P, T], I32), held("tab_w1", [P, T], I32)]
         load_tab(0)
-        load_side_by_side(ws_sc, ws_scales, 0)
+        ws_raw = held("ws_raw", [P, PASSES, 2 * R], U8)
+        nc.sync.dma_start(ws_raw[:].bitcast(I32), ws_words.rearrange("a p r -> p a r").bitcast(I32))
+        load_side_by_side(nc.sync, ws_sc_raw, ws_scales)
+        wt_raw = held("wt_raw", [P, PASSES, R], I32)
+        nc.sync.dma_start(wt_raw[:], wt_words.rearrange("a p r i -> p a (r i)").bitcast(I32))
+        wt_sc_raw = held("wt_sc_raw", [P, R], U8)
+        nc.gpsimd.memset(wt_sc_raw[:].bitcast(I32), 0)
+        load_two_planes((nc.sync, nc.sync), wt_sc_raw, wt_scales, ROWS)
+        nc.gpsimd.tensor_copy(moved[:].bitcast(I32)[:, :FEW_WORDS], zeros3)
         load_tab(1)
-        load_wt(0)
-        load_side_by_side(wt_sc, wt_scales, ROWS)
-        load_wt(1)
-        load_ws(1)
-        wd_raw = placed(loads, "wd_raw", [P, PASSES, N], I32, load_at["wd_raw"])
-        edge_w = placed(loads, "edge_w", [P, J], F32, load_at["edge_w"])
-        bias = placed(loads, "bias", [P, load_words["bias"]], F32, load_at["bias"])
-
-        ident = placed(loads, "ident", [P, P], F32, load_at["ident"])
-        make_identity(nc, ident[:])
 
         pages = []
 
-        def add_page(offset):
-            page = placed(loads, f"page{len(pages)}", [P, T], F32, offset)
-            pages.append(page)
-            nc.gpsimd.memset(page[:].bitcast(I32), 0)
+        def add_page(place):
+            pages.append(held(f"page{len(pages)}", [P, T], F32, place))
+            nc.gpsimd.memset(pages[-1][:].bitcast(I32), 0)
 
-        for t in range(PACK - 1):
-            add_page(load_at[f"page{t}"])
+        add_page("page0")
+        nc.gpsimd.tensor_copy(moved[:].bitcast(I32)[:, FEW_WORDS:], zeros4)
+        nc.gpsimd.memset(wd_sc_raw[:].bitcast(I32)[:, FEW_WORDS:], 0)
+        add_page("page1")
 
-        chunk_bytes = WORD * CHUNK
-        v_sc = {}
-        picked = {}
+        def gather_scales(name, window, side, first, count):
+            dst = sb(name, [P, count], U8)
+            nc.vector.tensor_copy(dst[:], window[:].indirect(entries(lists[side], first, count)))
+            return dst
 
-        def gather_scales(side, run, dst):
-            v_sc[side, run] = dst
-            nc.vector.tensor_copy(dst[:], tab_sc[:].indirect(entries(lists[side], run * RUN, RUN)))
+        src_rows = gather_scales("src_rows", rows, SOURCE, RUN, RUN)
+        src_sc = gather_scales("src_sc", tab_sc, SOURCE, 0, RUN)
+        tgt_sc = gather_scales("tgt_sc", tab_sc, TARGET, 0, J)
+        for q in range(QUADRANTS):
+            nc.sync.dma_start(
+                shifted[QUAD * q : QUAD * q + ROWS, :].bitcast(I32),
+                src_sc[QUAD * q + ROWS : QUAD * q + 2 * ROWS, :].bitcast(I32),
+            )
 
-        def shift_scales(run):
-            for q in range(QUADRANTS):
+        wd_raw = held("wd_raw", [P, PASSES, N], I32)
+        edge_w = held("edge_w", [P, J], F32)
+        bias = held("bias", [P, 2 * T], F32)
+        nc.sync.dma_start(wd_raw[:], wd_words.rearrange("a p n i -> p a (n i)").bitcast(I32))
+        load_two_planes((nc.sync, nc.sync), wd_sc_raw, wd_scales, 0)
+        nc.sync.dma_start(edge_w[:], wgo)
+        nc.sync.dma_start(bias[:, :PACK], b.rearrange("(p t) -> p t", t=PACK))
+
+        def deal_words(name, raw, dtype, width):
+            dealt = sb(name, [P, width], dtype)
+            nc.scalar.copy(
+                dealt[:].rearrange("p (h t m) -> p h m t", t=PACK, m=P),
+                raw.rearrange("p (h m t) -> p h m t", t=PACK, m=P),
+            )
+            return dealt
+
+        def deal_scales(name, raw):
+            dealt = sb(name, [P, BANK], U8)
+            nc.gpsimd.tensor_copy(
+                dealt[:].rearrange("p (t m) -> p t m", t=PACK), raw.rearrange("p (m t) -> p t m", t=PACK)
+            )
+            return dealt
+
+        ws_w = [deal_words(f"ws_w{a}", ws_raw[:, a, :].bitcast(U16), U16, R) for a in range(PASSES)]
+        wt_w = [deal_words(f"wt_w{a}", wt_raw[:, a, :].bitcast(U32), U32, R) for a in range(PASSES)]
+        ws_sc = [deal_scales(f"ws_sc{i}", ws_sc_raw[:, i * BANK : (i + 1) * BANK]) for i in range(2 * PASSES)]
+        wt_sc = [deal_scales(f"wt_sc{i}", wt_sc_raw[:, i * BANK : (i + 1) * BANK]) for i in range(2)]
+        for a in range(PASSES):
+            for s in range(ROWS):
+                first = AS_THEY_LIE + ROWS * QUADRANTS * a + s
                 nc.sync.dma_start(
-                    src_sc1[QUAD * q : QUAD * q + ROWS, run * RUN : (run + 1) * RUN].bitcast(I32),
-                    v_sc[SOURCE, run][QUAD * q + ROWS : QUAD * q + 2 * ROWS, :].bitcast(I32),
+                    moved[s : P : QUAD, a * RUN : (a + 1) * RUN].bitcast(I32),
+                    src_rows[first : first + ROWS * (QUADRANTS - 1) + 1 : ROWS, :].bitcast(I32),
                 )
+        add_page("wt_sc_raw")
+        wd_w = sb("wd_w", [P, PASSES * N], I32)
+        nc.gpsimd.tensor_copy(
+            wd_w[:].rearrange("p (a t m) -> p a t m", a=PASSES, t=PACK),
+            wd_raw[:].rearrange("p a (m t) -> p a t m", t=PACK),
+        )
+        wd_sc = deal_scales("wd_sc", wd_sc_raw[:])
+
+        picked = {}
 
         def gather(first_chunk, count, a, side, dst):
             for i in range(count):
@@ -180,128 +220,101 @@ def tile_list_msg_relu_biasP_kernel(
             window = tab_w[a][:].bitcast(U32)
             nc.vector.tensor_copy(dst, window.indirect(entries(lists[side], first_chunk * CHUNK, count * CHUNK)))
 
-        def gather_middle(a, side):
-            gather(1, 2, a, side, sb(f"picked12_{a}_{side}", [P, 2 * CHUNK], U32)[:])
+        for first_chunk, count, side in ((0, 1, SOURCE), (0, 1, TARGET), (1, 2, TARGET), (1, 3, SOURCE)):
+            gather(first_chunk, count, 0, side, sb(f"picked{first_chunk}_0_{side}", [P, count * CHUNK], U32)[:])
+        gather(0, 1, 1, TARGET, sb("picked0_1_t", [P, CHUNK], U32)[:])
+        gather(0, 1, 1, SOURCE, placed(lag3, "picked0_1_s", [P, CHUNK], U32, 0)[:])
+        gather(1, 2, 1, TARGET, sb("picked1_1_t", [P, 2 * CHUNK], U32)[:])
+        gather(1, 2, 1, SOURCE, placed(lag1, "picked1_1_s", [P, 2 * CHUNK], U32, 0)[:])
 
-        gather_scales(SOURCE, 0, sb("src_sc_a", [P, RUN], U8))
-        shift_scales(0)
-        gather_scales(TARGET, 0, sb("tgt_sc_a", [P, RUN], U8))
-        for side in (SOURCE, TARGET):
-            gather(0, 1, 0, side, sb(f"picked0_0_{side}", [P, CHUNK], U32)[:])
-            gather_middle(0, side)
-        gather(0, 1, 1, TARGET, placed(after_target, "picked0_1t", [P, CHUNK], U32, RUN - ALIGN)[:])
-        gather(0, 1, 1, SOURCE, placed(after_source, "picked0_1s", [P, CHUNK], U32, 0)[:])
-        gather_middle(1, SOURCE)
-        gather_middle(1, TARGET)
+        acc, h_in = {}, {}
+        no_bias = 0.0
+        zero_bias = placed(lag2, "zero_bias", [P, FEW_WORDS], F32, 0)
+        nc.vector.memset(zero_bias[:], 0.0)
 
-        nc.sync.dma_start(wd_raw[:], wd_words.rearrange("a p n i -> p a (n i)").bitcast(I32))
-        load_two_planes(wd_sc_raw, wd_scales, nc.sync)
-        nc.sync.dma_start(edge_w[:], wgo)
-        nc.sync.dma_start(bias[:, :PACK], b.rearrange("(p t) -> p t", t=PACK))
+        def slices(c, k):
+            n = MOVING[c]
+            per_bank = BANK // n
+            group, rest = divmod(k * per_bank, PASSES * PACK)
+            return [(slice(i * n, (i + 1) * n), P * (rest + i), slice(group * n, (group + 1) * n)) for i in range(per_bank)]
 
-        gather_scales(SOURCE, 1, placed(after_target, "src_sc_b", [P, RUN], U8, 0))
-        shift_scales(1)
-        gather_scales(TARGET, 1, placed(after_target, "tgt_sc_b", [P, RUN], U8, RUN + chunk_bytes - 2 * ALIGN))
-
-        wd_w = sb("wd_w", [P, PASSES, N], I32)
-        nc.gpsimd.tensor_copy(
-            wd_w[:].rearrange("p a (t m) -> p a t m", t=PACK), wd_raw[:].rearrange("p a (m t) -> p a t m", t=PACK)
-        )
-        wd_sc = sb("wd_sc", [P, N], U8)
-        nc.gpsimd.tensor_copy(
-            wd_sc[:].rearrange("p (t m) -> p t m", t=PACK), wd_sc_raw[:].rearrange("p (m t) -> p t m", t=PACK)
-        )
-        picked3_0 = placed(after_source, "picked3_0", [P, 2, CHUNK], U32, chunk_bytes - ALIGN)
-        for side in (SOURCE, TARGET):
-            gather(CHUNKS - 1, 1, 0, side, picked3_0[:, side, :])
-
-        def first_pass(acc, group, half, a, side, order):
-            in_chunk = slice(P * (group % 2), P * (group % 2 + 1))
-            run, first = divmod(P * group, RUN)
-            in_run = slice(first, first + P)
-            plane_cols = slice(a * R + half * BANK, a * R + (half + 1) * BANK)
-            if side == SOURCE:
-                v_scale = src_sc1[:, P * group : P * (group + 1)] if a else v_sc[SOURCE, run][:, in_run]
-                w = ws_w[a][:, 2 * half * BANK : 2 * (half + 1) * BANK].bitcast(FP4X4)
-                w_scale = ws_sc[:, plane_cols]
-            else:
-                v_scale = v_sc[TARGET, run][ROWS * a : P, in_run]
-                w = wt_w[a][:, half * BANK : (half + 1) * BANK].bitcast(FP8X4)
-                w_scale = wt_sc[ROWS:P, plane_cols]
-            nc.tensor.matmul_mx(
-                out=acc[:], lhsT=picked[group // 2, a, side][:, in_chunk].bitcast(FP8X4), lhsT_scale=v_scale,
-                rhs=w, rhs_scale=w_scale,
-                start=((a, side) == order[0]), stop=((a, side) == order[-1]),
-            )
-
-        h_edge = {}
-        h_edge_at = {2: (early_h, 0), 1: (early_h, R), 3: (early_h, 2 * R), 5: (late_h, 0), 7: (late_h, 2 * R)}
-
-        def relu(group, half, acc):
-            if group not in h_edge:
-                if group in h_edge_at:
-                    pool, offset = h_edge_at[group]
-                    h_edge[group] = placed(pool, f"h_edge{group}", [P, R], BF16, offset)
+        def first_pass(c, k, a, side, start=False, stop=False):
+            if start:
+                acc[c, k] = bank(f"a{c}_{k}", FIRST_BANKS[c][k])
+            parts = slices(c, k)
+            for i, (cols, col, edges) in enumerate(parts):
+                first, last = c * CHUNK + edges.start, c * CHUNK + edges.stop
+                if side == SOURCE:
+                    w = ws_w[a][:, col : col + P].bitcast(FP4X4)
+                    w_scale = ws_sc[2 * a + col // BANK][:, col % BANK : col % BANK + P]
+                    if first >= RUN:
+                        v_scale = moved[:, (a - 1) * RUN + first : (a - 1) * RUN + last]
+                    else:
+                        v_scale = (src_sc, shifted)[a][:, first:last]
                 else:
-                    h_edge[group] = sb(f"h_edge{group}", [P, R], BF16)
+                    w = wt_w[a][:, col : col + P].bitcast(FP8X4)
+                    w_scale = wt_sc[col // BANK][ROWS * (a + 1) : P, col % BANK : col % BANK + P]
+                    v_scale = tgt_sc[ROWS * a : P, first:last]
+                nc.tensor.matmul_mx(
+                    out=acc[c, k][:, cols], lhsT=w, lhsT_scale=w_scale,
+                    rhs=picked[c, a, side][:, edges].bitcast(FP8X4), rhs_scale=v_scale,
+                    start=start and i == 0, stop=stop and i == len(parts) - 1,
+                )
+
+        def relu(c, k):
+            if c not in h_in:
+                h_in[c] = sb(f"h_in{c}", [P, PASSES * CHUNK * PACK], BF16)
+            parts = slices(c, k)
+            half, t = divmod(parts[0][1] // P, PACK)
             nc.scalar.activation(
-                h_edge[group][:, half * BANK : (half + 1) * BANK].rearrange("j (u p e) -> j u p e", u=2, e=2),
-                acc[:].rearrange("j (p u e) -> j u p e", u=2, e=2),
+                h_in[c][:].rearrange("p (a j i) -> p a j i", a=PASSES, i=PACK)[:, half, parts[0][2], t : t + len(parts)],
+                acc[c, k][:].rearrange("p (i j) -> p j i", i=len(parts)),
                 ACT.Relu,
+                bias=(no_bias, zero_bias[:, :1])[c == 0],
             )
 
-        def first_half(group, half):
-            acc = bank(f"a{group}_{half}", FIRST_BANKS[group][half])
-            for a, side in ORDER:
-                first_pass(acc, group, half, a, side, ORDER)
-            relu(group, half, acc)
+        def finish_bank(c, k):
+            first_pass(c, k, 1, TARGET)
+            first_pass(c, k, 1, SOURCE, stop=True)
+            relu(c, k)
 
-        def turn(group, h_in):
-            turned = bank(f"turned{group}", TURN_BANKS[group // 2][group % 2])
-            pair_words = h_edge[group][:].bitcast(F32)
-            for s in range(2 * PASSES):
-                nc.tensor.transpose(turned[:, P * s : P * (s + 1)], pair_words[:, P * s : P * (s + 1)], ident[:])
-            h_words = h_in[:].bitcast(F32).rearrange("p (a j u) -> p a j u", a=PASSES, u=2)
-            nc.scalar.copy(
-                h_words[:, :, P * (group % 2) : P * (group % 2 + 1), :],
-                turned[:].rearrange("p (a u j) -> p a j u", a=PASSES, u=2),
-            )
+        def whole_bank(c, k):
+            first_pass(c, k, 0, SOURCE, start=True)
+            first_pass(c, k, 0, TARGET)
+            finish_bank(c, k)
 
         h_w, h_sc = {}, {}
 
         def quantise_h(c):
-            h_in = sb(f"h_in{c}", [P, PASSES * CHUNK * PACK], BF16)
-            for group in (2 * c, 2 * c + 1):
-                turn(group, h_in)
             h_w[c] = sb(f"h_w{c}", [P, PASSES * CHUNK], U32)
             h_sc[c] = sb(f"h_sc{c}", [P, PASSES * CHUNK], U8)
-            nc.vector.quantize_mx(out=h_w[c][:].bitcast(FP8X4), scales=h_sc[c][:], in_=h_in[:])
+            nc.vector.quantize_mx(out=h_w[c][:].bitcast(FP8X4), scales=h_sc[c][:], in_=h_in[c][:])
 
-        def second(acc, c, t):
+        def second(out, c, t):
             for a in range(PASSES):
                 nc.tensor.matmul_mx(
-                    out=acc, lhsT=wd_w[:, a, P * t : P * (t + 1)].bitcast(FP8X4),
+                    out=out, lhsT=wd_w[:, a * N + P * t : a * N + P * (t + 1)].bitcast(FP8X4),
                     lhsT_scale=wd_sc[ROWS * a : P, P * t : P * (t + 1)],
                     rhs=h_w[c][:, a * CHUNK : (a + 1) * CHUNK].bitcast(FP8X4),
                     rhs_scale=h_sc[c][:, a * CHUNK : (a + 1) * CHUNK],
                     start=(a == 0), stop=(a == PASSES - 1),
                 )
 
-        def put(t, first_chunk, count, msg, acc):
+        def put(t, first_chunk, count, msg, y):
             first, edges = first_chunk * CHUNK, count * CHUNK
-            nc.scalar.activation(msg, acc, ACT.Identity, bias=bias[:, t : t + 1])
+            nc.scalar.activation(msg, y, ACT.Identity, bias=bias[:, t : t + 1])
             nc.vector.tensor_tensor(
                 pages[t][:].indirect(entries(lists[TARGET], first, edges)), msg, edge_w[:, first : first + edges], MULT,
             )
 
-        def part(acc, i):
-            return acc[:, i * CHUNK : (i + 1) * CHUNK]
+        def part(tile, i):
+            return tile[:, i * CHUNK : (i + 1) * CHUNK]
 
         lagging = {}
 
         def second_stage(c):
-            early = bank(f"early{c}", EARLY_BANK)
-            lagging[c] = bank(f"lag{c}", LAG_BANK)
+            early = bank(f"early{c}", SECOND_BANKS[c][0])
+            lagging[c] = bank(f"lag{c}", SECOND_BANKS[c][1])
             for t in range(PACK):
                 second(part((early, lagging[c])[t // 2], t % 2), c, t)
             for t in range(2):
@@ -310,50 +323,49 @@ def tile_list_msg_relu_biasP_kernel(
         def lagging_page(c, t, pool, offset):
             put(t, c, 1, placed(pool, f"msg{c}_{t}", [P, CHUNK], F32, offset)[:], part(lagging[c], t - 2))
 
-        opened = {(g, half): bank(f"a{g}_{half}", FIRST_BANKS[g][half]) for g in range(3) for half in range(2)}
-        for g, half in opened:
-            first_pass(opened[g, half], g, half, *ORDER[0], ORDER)
-        for a, side in ORDER[1:]:
-            for g in range(2):
-                for half in range(2):
-                    first_pass(opened[g, half], g, half, a, side, ORDER)
-                    if (a, side) == ORDER[-1]:
-                        relu(g, half, opened[g, half])
-        for half in range(2):
-            for a, side in SOURCE_FIRST[1:]:
-                first_pass(opened[2, half], 2, half, a, side, SOURCE_FIRST)
-
+        for side in (SOURCE, TARGET):
+            for k in (0, 2, 1, 3):
+                first_pass(0, k, 0, side, start=(side == SOURCE))
+        for k in range(2):
+            first_pass(0, k, 1, TARGET)
+        for k in range(2):
+            first_pass(0, k, 1, SOURCE, stop=True)
+            relu(0, k)
+        for k in range(2, 4):
+            first_pass(0, k, 1, SOURCE)
+            first_pass(0, k, 1, TARGET, stop=True)
+            relu(0, k)
+        gather(CHUNKS - 1, 1, 0, TARGET, placed(lag3, "picked3_0_t", [P, CHUNK], U32, 0)[:])
         quantise_h(0)
-        picked3_1 = sb("picked3_1", [P, 2, CHUNK], U32, "h_in0")
+        picked3 = placed(lag2, "picked3", [P, 2, CHUNK], U32, 0)
         for i, side in enumerate((TARGET, SOURCE)):
-            gather(CHUNKS - 1, 1, 1, side, picked3_1[:, i, :])
-        add_page(load_at["tab_w1"])
-
-        for half in range(2):
-            relu(2, half, opened[2, half])
-        first_half(3, 0)
-        first_half(3, 1)
+            gather(CHUNKS - 1, 1, 1, side, picked3[:, i, :])
+        add_page("tab_w1")
+        whole_bank(1, 0)
         second_stage(0)
-        first_half(4, 0)
+        whole_bank(1, 1)
+        whole_bank(1, 2)
+        whole_bank(1, 3)
         quantise_h(1)
-        lagging_page(0, 2, early_h, 3 * R)
-        lagging_page(0, 3, early_h, 2 * R)
-        first_half(4, 1)
-        first_half(5, 0)
-        first_half(5, 1)
+        lagging_page(0, 2, lag0, 0)
+        lagging_page(0, 3, lag0, WORD * CHUNK)
+        whole_bank(2, 0)
+        whole_bank(2, 1)
         second_stage(1)
+        whole_bank(2, 2)
+        whole_bank(2, 3)
         quantise_h(2)
-        lagging_page(1, 2, *h_edge_at[5])
-        for group in (6, 7):
-            for half in range(2):
-                first_half(group, half)
-
+        lagging_page(1, 2, lag1, 0)
+        whole_bank(3, 0)
+        whole_bank(3, 1)
         last = [bank("last0", LAST_BANKS[0])]
         msgs = [sb(f"msg_last{t}", [P, 2 * CHUNK], F32) for t in range(PACK)]
         second(part(last[0], 0), 2, 0)
         put(0, 2, 1, part(msgs[0], 0), part(last[0], 0))
+        whole_bank(3, 2)
+        whole_bank(3, 3)
         quantise_h(3)
-        lagging_page(1, 3, *h_edge_at[7])
+        lagging_page(1, 3, lag2, 0)
         last.extend(bank(f"last{t}", LAST_BANKS[t]) for t in range(1, PACK))
         for t in range(1, PACK):
             second(part(last[t], 0), 2, t)
@@ -367,7 +379,7 @@ def tile_list_msg_relu_biasP_kernel(
         pieces = len(OUT_WIDTHS)
         starts = [sum(OUT_WIDTHS[:i]) for i in range(pieces)]
         pairs = [
-            placed(loads, f"pairs{i}", [P, 2, w, 2], BF16, load_at["bias"] + 2 * WORD * starts[i])
+            placed(at["bias"][0], f"pairs{i}", [P, 2, w, 2], BF16, at["bias"][1] + 2 * WORD * starts[i])
             for i, w in enumerate(OUT_WIDTHS)
         ]
         for t in range(PACK):

@@ -31,11 +31,10 @@ WORD = 4
 ALIGN = 64
 FEW_WORDS = 8
 SOURCE, TARGET = 0, 1
-AS_THEY_LIE = P - PASSES * ROWS * QUADRANTS
 
-FIRST_BANKS = ((0, 1, 2, 3), (0, 1, 2, 3), (4, 0, 1, 2), (3, 5, 4, 0))
-SECOND_BANKS = ((4, 5), (6, 7))
-LAST_BANKS = (6, 1, 2, 3)
+FIRST_BANKS = ((0, 1, 2, 3), (4, 5, 6, 7), (2, 3, 0, 4), (6, 7, 2, 0))
+SECOND_BANKS = ((0, 1), (3, 5))
+LAST_BANKS = (1, 4, 3, 6)
 MOVING = (P, CHUNK, CHUNK, CHUNK)
 
 OUT_WIDTHS = (512, 256, 256, 256, 256, 256, 128, 128)
@@ -54,6 +53,7 @@ def tile_list_msg_relu_biasP_kernel(
         lag0 = ctx.enter_context(tc.tile_pool(name="lag0", bufs=1))
         lag1 = ctx.enter_context(tc.tile_pool(name="lag1", bufs=1))
         lag3 = ctx.enter_context(tc.tile_pool(name="lag3", bufs=1))
+        lag4 = ctx.enter_context(tc.tile_pool(name="lag4", bufs=1))
         lag2 = ctx.enter_context(tc.tile_pool(name="lag2", bufs=1))
         psum = ctx.enter_context(tc.psum_pool(name="psum", bufs=1))
 
@@ -85,15 +85,17 @@ def tile_list_msg_relu_biasP_kernel(
 
         lists = [keep.tile([P, J // PER_COLUMN], U16, name=name) for name in ("src_list", "tgt_list")]
         nc.sync.dma_start(lists[SOURCE][:], offs)
-        rows = sb("rows", [P, T], U8)
-        nc.scalar.dma_start(
-            rows[AS_THEY_LIE:P, :].bitcast(I32), tab_scales.rearrange("a q t -> (a q) t").bitcast(I32)
-        )
+        ws_raw = [sb("ws_raw0", [P, 2 * R], U8)]
+
+        def load_ws(a):
+            nc.sync.dma_start(ws_raw[a][:].bitcast(I32), ws_words[a].bitcast(I32))
+
+        load_ws(0)
         nc.sync.dma_start(lists[TARGET][:], offs2)
 
         words = {
-            "first": {"tab_w0": T, "ws_raw": R},
-            "second": {"wt_raw": PASSES * R, "page0": T, "page1": T, "wt_sc_raw": T},
+            "first": {"tab_w0": T},
+            "second": {"wt_raw": PASSES * R, "ws_raw1": R // 2, "page0": T, "page1": T, "wt_sc_raw": T},
             "third": {"tab_w1": T},
             "fourth": {"wd_raw": PASSES * N, "edge_w": J, "bias": 2 * T},
         }
@@ -115,18 +117,16 @@ def tile_list_msg_relu_biasP_kernel(
 
         tab_sc = sb("tab_sc", [P, T], U8)
         wd_sc_raw = sb("wd_sc_raw", [P, N], U8)
-        moved = sb("moved", [P, PASSES * RUN], U8)
-        shifted = placed(lag0, "shifted", [P, RUN], U8, WORD * CHUNK - RUN // 2)
+        shifted = [placed(lag0, "shifted0", [P, RUN], U8, WORD * CHUNK - RUN // 2), sb("shifted1", [P, RUN], U8)]
         ws_sc_raw = sb("ws_sc_raw", [P, PASSES * R], U8)
         zeros1 = zeros("first", nc.gpsimd, FEW_WORDS)
         nc.gpsimd.memset(tab_sc[:].bitcast(I32), 0)
         nc.gpsimd.tensor_copy(wd_sc_raw[:].bitcast(I32)[:, :FEW_WORDS], zeros1)
         zeros3 = zeros("third", nc.gpsimd, FEW_WORDS)
-        zeros4 = zeros("fourth", nc.gpsimd, PASSES * RUN // WORD - FEW_WORDS)
-        nc.vector.memset(rows[:AS_THEY_LIE, :].bitcast(I32), 0)
+        zeros4 = zeros("fourth", nc.gpsimd, RUN // WORD - FEW_WORDS)
         zeros2 = zeros("second", nc.vector, RUN // WORD)
         nc.vector.memset(ws_sc_raw[:].bitcast(I32), 0)
-        nc.vector.tensor_copy(shifted[:].bitcast(I32), zeros2)
+        nc.vector.tensor_copy(shifted[0][:].bitcast(I32), zeros2)
         load_two_planes((nc.sync, nc.scalar), tab_sc, tab_scales, 0)
 
         def load_tab(a):
@@ -134,15 +134,15 @@ def tile_list_msg_relu_biasP_kernel(
 
         tab_w = [held("tab_w0", [P, T], I32), held("tab_w1", [P, T], I32)]
         load_tab(0)
-        ws_raw = held("ws_raw", [P, PASSES, 2 * R], U8)
-        nc.sync.dma_start(ws_raw[:].bitcast(I32), ws_words.rearrange("a p r -> p a r").bitcast(I32))
         load_side_by_side(nc.sync, ws_sc_raw, ws_scales)
         wt_raw = held("wt_raw", [P, PASSES, R], I32)
         nc.sync.dma_start(wt_raw[:], wt_words.rearrange("a p r i -> p a (r i)").bitcast(I32))
+        ws_raw.append(held("ws_raw1", [P, 2 * R], U8))
+        load_ws(1)
         wt_sc_raw = held("wt_sc_raw", [P, R], U8)
         nc.gpsimd.memset(wt_sc_raw[:].bitcast(I32), 0)
         load_two_planes((nc.sync, nc.sync), wt_sc_raw, wt_scales, ROWS)
-        nc.gpsimd.tensor_copy(moved[:].bitcast(I32)[:, :FEW_WORDS], zeros3)
+        nc.gpsimd.tensor_copy(shifted[1][:].bitcast(I32)[:, :FEW_WORDS], zeros3)
         load_tab(1)
 
         pages = []
@@ -152,23 +152,25 @@ def tile_list_msg_relu_biasP_kernel(
             nc.gpsimd.memset(pages[-1][:].bitcast(I32), 0)
 
         add_page("page0")
-        nc.gpsimd.tensor_copy(moved[:].bitcast(I32)[:, FEW_WORDS:], zeros4)
+        nc.gpsimd.tensor_copy(shifted[1][:].bitcast(I32)[:, FEW_WORDS:], zeros4)
         nc.gpsimd.memset(wd_sc_raw[:].bitcast(I32)[:, FEW_WORDS:], 0)
-        add_page("page1")
+        pages.append(held("page1", [P, T], F32))
+        nc.vector.memset(pages[1][:].bitcast(I32), 0)
 
-        def gather_scales(name, window, side, first, count):
-            dst = sb(name, [P, count], U8)
-            nc.vector.tensor_copy(dst[:], window[:].indirect(entries(lists[side], first, count)))
+        def gather_scales(dst, side, first, count):
+            nc.vector.tensor_copy(dst[:], tab_sc[:].indirect(entries(lists[side], first, count)))
             return dst
 
-        src_rows = gather_scales("src_rows", rows, SOURCE, RUN, RUN)
-        src_sc = gather_scales("src_sc", tab_sc, SOURCE, 0, RUN)
-        tgt_sc = gather_scales("tgt_sc", tab_sc, TARGET, 0, J)
-        for q in range(QUADRANTS):
-            nc.sync.dma_start(
-                shifted[QUAD * q : QUAD * q + ROWS, :].bitcast(I32),
-                src_sc[QUAD * q + ROWS : QUAD * q + 2 * ROWS, :].bitcast(I32),
-            )
+        def shift_scales(run):
+            for q in range(QUADRANTS):
+                nc.sync.dma_start(
+                    shifted[run][QUAD * q : QUAD * q + ROWS, :].bitcast(I32),
+                    src_sc[run][QUAD * q + ROWS : QUAD * q + 2 * ROWS, :].bitcast(I32),
+                )
+
+        src_sc = [gather_scales(sb("src_sc0", [P, RUN], U8), SOURCE, 0, RUN)]
+        tgt_sc = [gather_scales(sb("tgt_sc0", [P, RUN], U8), TARGET, 0, RUN)]
+        shift_scales(0)
 
         wd_raw = held("wd_raw", [P, PASSES, N], I32)
         edge_w = held("edge_w", [P, J], F32)
@@ -193,17 +195,11 @@ def tile_list_msg_relu_biasP_kernel(
             )
             return dealt
 
-        ws_w = [deal_words(f"ws_w{a}", ws_raw[:, a, :].bitcast(U16), U16, R) for a in range(PASSES)]
+        ws_w = [deal_words("ws_w0", ws_raw[0][:].bitcast(U16), U16, R)]
         wt_w = [deal_words(f"wt_w{a}", wt_raw[:, a, :].bitcast(U32), U32, R) for a in range(PASSES)]
+        ws_w.append(deal_words("ws_w1", ws_raw[1][:].bitcast(U16), U16, R))
         ws_sc = [deal_scales(f"ws_sc{i}", ws_sc_raw[:, i * BANK : (i + 1) * BANK]) for i in range(2 * PASSES)]
         wt_sc = [deal_scales(f"wt_sc{i}", wt_sc_raw[:, i * BANK : (i + 1) * BANK]) for i in range(2)]
-        for a in range(PASSES):
-            for s in range(ROWS):
-                first = AS_THEY_LIE + ROWS * QUADRANTS * a + s
-                nc.sync.dma_start(
-                    moved[s : P : QUAD, a * RUN : (a + 1) * RUN].bitcast(I32),
-                    src_rows[first : first + ROWS * (QUADRANTS - 1) + 1 : ROWS, :].bitcast(I32),
-                )
         add_page("wt_sc_raw")
         wd_w = sb("wd_w", [P, PASSES * N], I32)
         nc.gpsimd.tensor_copy(
@@ -220,10 +216,11 @@ def tile_list_msg_relu_biasP_kernel(
             window = tab_w[a][:].bitcast(U32)
             nc.vector.tensor_copy(dst, window.indirect(entries(lists[side], first_chunk * CHUNK, count * CHUNK)))
 
-        for first_chunk, count, side in ((0, 1, SOURCE), (0, 1, TARGET), (1, 2, TARGET), (1, 3, SOURCE)):
+        gather(0, 1, 0, SOURCE, placed(lag4, "picked0_0_s", [P, 2 * CHUNK], U32, 0)[:, :CHUNK])
+        for first_chunk, count, side in ((0, 1, TARGET), (1, 3, SOURCE), (1, 3, TARGET)):
             gather(first_chunk, count, 0, side, sb(f"picked{first_chunk}_0_{side}", [P, count * CHUNK], U32)[:])
         gather(0, 1, 1, TARGET, sb("picked0_1_t", [P, CHUNK], U32)[:])
-        gather(0, 1, 1, SOURCE, placed(lag3, "picked0_1_s", [P, CHUNK], U32, 0)[:])
+        gather(0, 1, 1, SOURCE, placed(lag3, "picked0_1_s", [P, 3 * CHUNK], U32, 0)[:, :CHUNK])
         gather(1, 2, 1, TARGET, sb("picked1_1_t", [P, 2 * CHUNK], U32)[:])
         gather(1, 2, 1, SOURCE, placed(lag1, "picked1_1_s", [P, 2 * CHUNK], U32, 0)[:])
 
@@ -238,23 +235,24 @@ def tile_list_msg_relu_biasP_kernel(
             group, rest = divmod(k * per_bank, PASSES * PACK)
             return [(slice(i * n, (i + 1) * n), P * (rest + i), slice(group * n, (group + 1) * n)) for i in range(per_bank)]
 
-        def first_pass(c, k, a, side, start=False, stop=False):
+        def first_pass(c, k, a, side, start=False, stop=False, only=None):
             if start:
                 acc[c, k] = bank(f"a{c}_{k}", FIRST_BANKS[c][k])
             parts = slices(c, k)
             for i, (cols, col, edges) in enumerate(parts):
+                if only is not None and i != only:
+                    continue
                 first, last = c * CHUNK + edges.start, c * CHUNK + edges.stop
                 if side == SOURCE:
                     w = ws_w[a][:, col : col + P].bitcast(FP4X4)
                     w_scale = ws_sc[2 * a + col // BANK][:, col % BANK : col % BANK + P]
-                    if first >= RUN:
-                        v_scale = moved[:, (a - 1) * RUN + first : (a - 1) * RUN + last]
-                    else:
-                        v_scale = (src_sc, shifted)[a][:, first:last]
+                    run = first // RUN
+                    v_scale = (src_sc, shifted)[a][run][:, first - run * RUN : last - run * RUN]
                 else:
                     w = wt_w[a][:, col : col + P].bitcast(FP8X4)
                     w_scale = wt_sc[col // BANK][ROWS * (a + 1) : P, col % BANK : col % BANK + P]
-                    v_scale = tgt_sc[ROWS * a : P, first:last]
+                    run = first // RUN
+                    v_scale = tgt_sc[run][ROWS * a : P, first - run * RUN : last - run * RUN]
                 nc.tensor.matmul_mx(
                     out=acc[c, k][:, cols], lhsT=w, lhsT_scale=w_scale,
                     rhs=picked[c, a, side][:, edges].bitcast(FP8X4), rhs_scale=v_scale,
@@ -323,9 +321,10 @@ def tile_list_msg_relu_biasP_kernel(
         def lagging_page(c, t, pool, offset):
             put(t, c, 1, placed(pool, f"msg{c}_{t}", [P, CHUNK], F32, offset)[:], part(lagging[c], t - 2))
 
-        for side in (SOURCE, TARGET):
-            for k in (0, 2, 1, 3):
-                first_pass(0, k, 0, side, start=(side == SOURCE))
+        for c, side in ((0, SOURCE), (0, TARGET), (1, SOURCE)):
+            for k in (0, 2, 1, 3) if c == 0 else range(4):
+                first_pass(c, k, 0, side, start=(side == SOURCE))
+        tgt_sc.append(gather_scales(placed(lag4, "tgt_sc1", [P, RUN], U8, WORD * CHUNK), TARGET, RUN, RUN))
         for k in range(2):
             first_pass(0, k, 1, TARGET)
         for k in range(2):
@@ -335,45 +334,40 @@ def tile_list_msg_relu_biasP_kernel(
             first_pass(0, k, 1, SOURCE)
             first_pass(0, k, 1, TARGET, stop=True)
             relu(0, k)
-        gather(CHUNKS - 1, 1, 0, TARGET, placed(lag3, "picked3_0_t", [P, CHUNK], U32, 0)[:])
+        src_sc.append(gather_scales(placed(lag3, "src_sc1", [P, RUN], U8, WORD * CHUNK), SOURCE, RUN, RUN))
+        shift_scales(1)
         quantise_h(0)
         picked3 = placed(lag2, "picked3", [P, 2, CHUNK], U32, 0)
         for i, side in enumerate((TARGET, SOURCE)):
             gather(CHUNKS - 1, 1, 1, side, picked3[:, i, :])
         add_page("tab_w1")
-        whole_bank(1, 0)
-        second_stage(0)
-        whole_bank(1, 1)
-        whole_bank(1, 2)
-        whole_bank(1, 3)
+        for k in range(4):
+            first_pass(1, k, 1, SOURCE, only=0)
+            first_pass(1, k, 0, TARGET)
+            first_pass(1, k, 1, TARGET)
+            first_pass(1, k, 1, SOURCE, stop=True, only=1)
+            relu(1, k)
+            if k == 0:
+                second_stage(0)
         quantise_h(1)
         lagging_page(0, 2, lag0, 0)
         lagging_page(0, 3, lag0, WORD * CHUNK)
-        whole_bank(2, 0)
-        whole_bank(2, 1)
+        for k in range(3):
+            whole_bank(2, k)
         second_stage(1)
-        whole_bank(2, 2)
         whole_bank(2, 3)
         quantise_h(2)
         lagging_page(1, 2, lag1, 0)
-        whole_bank(3, 0)
-        whole_bank(3, 1)
-        last = [bank("last0", LAST_BANKS[0])]
-        msgs = [sb(f"msg_last{t}", [P, 2 * CHUNK], F32) for t in range(PACK)]
-        second(part(last[0], 0), 2, 0)
-        put(0, 2, 1, part(msgs[0], 0), part(last[0], 0))
-        whole_bank(3, 2)
-        whole_bank(3, 3)
+        for k in range(4):
+            whole_bank(3, k)
         quantise_h(3)
         lagging_page(1, 3, lag2, 0)
-        last.extend(bank(f"last{t}", LAST_BANKS[t]) for t in range(1, PACK))
-        for t in range(1, PACK):
+        last = [bank(f"last{t}", LAST_BANKS[t]) for t in range(PACK)]
+        for t in range(PACK):
             second(part(last[t], 0), 2, t)
-        second(part(last[0], 1), 3, 0)
-        put(0, 3, 1, part(msgs[0], 1), part(last[0], 1))
-        for t in range(1, PACK):
+        for t in range(PACK):
             second(part(last[t], 1), 3, t)
-            put(t, 2, 2, msgs[t][:], last[t][:])
+            put(t, 2, 2, sb(f"msg_last{t}", [P, 2 * CHUNK], F32)[:], last[t][:])
 
         out_rows = out_0.rearrange("(p t) c -> p t c", t=PACK)
         pieces = len(OUT_WIDTHS)

@@ -52,8 +52,6 @@ def tile_list_msg_relu_biasP_kernel(
         keep = ctx.enter_context(tc.tile_pool(name="keep", bufs=1))
         lag0 = ctx.enter_context(tc.tile_pool(name="lag0", bufs=1))
         lag1 = ctx.enter_context(tc.tile_pool(name="lag1", bufs=1))
-        lag3 = ctx.enter_context(tc.tile_pool(name="lag3", bufs=1))
-        lag4 = ctx.enter_context(tc.tile_pool(name="lag4", bufs=1))
         lag2 = ctx.enter_context(tc.tile_pool(name="lag2", bufs=1))
         psum = ctx.enter_context(tc.psum_pool(name="psum", bufs=1))
 
@@ -95,8 +93,8 @@ def tile_list_msg_relu_biasP_kernel(
 
         words = {
             "first": {"tab_w0": T},
-            "second": {"wt_raw": PASSES * R, "ws_raw1": R // 2, "page0": T, "page1": T, "wt_sc_raw": T},
-            "third": {"tab_w1": T},
+            "second": {"wt_raw": PASSES * R, "page0": T, "page1": T, "wt_sc_raw": T},
+            "third": {"tab_w1": T, "ws_raw1": R // 2},
             "fourth": {"wd_raw": PASSES * N, "edge_w": J, "bias": 2 * T},
         }
         pools = {name: ctx.enter_context(tc.tile_pool(name=name, bufs=1)) for name in words}
@@ -119,8 +117,8 @@ def tile_list_msg_relu_biasP_kernel(
         wd_sc_raw = sb("wd_sc_raw", [P, N], U8)
         shifted = [placed(lag0, "shifted0", [P, RUN], U8, WORD * CHUNK - RUN // 2), sb("shifted1", [P, RUN], U8)]
         ws_sc_raw = sb("ws_sc_raw", [P, PASSES * R], U8)
-        zeros1 = zeros("first", nc.gpsimd, FEW_WORDS)
         nc.gpsimd.memset(tab_sc[:].bitcast(I32), 0)
+        zeros1 = zeros("first", nc.gpsimd, FEW_WORDS)
         nc.gpsimd.tensor_copy(wd_sc_raw[:].bitcast(I32)[:, :FEW_WORDS], zeros1)
         zeros3 = zeros("third", nc.gpsimd, FEW_WORDS)
         zeros4 = zeros("fourth", nc.gpsimd, RUN // WORD - FEW_WORDS)
@@ -137,13 +135,13 @@ def tile_list_msg_relu_biasP_kernel(
         load_side_by_side(nc.sync, ws_sc_raw, ws_scales)
         wt_raw = held("wt_raw", [P, PASSES, R], I32)
         nc.sync.dma_start(wt_raw[:], wt_words.rearrange("a p r i -> p a (r i)").bitcast(I32))
-        ws_raw.append(held("ws_raw1", [P, 2 * R], U8))
-        load_ws(1)
         wt_sc_raw = held("wt_sc_raw", [P, R], U8)
         nc.gpsimd.memset(wt_sc_raw[:].bitcast(I32), 0)
         load_two_planes((nc.sync, nc.sync), wt_sc_raw, wt_scales, ROWS)
         nc.gpsimd.tensor_copy(shifted[1][:].bitcast(I32)[:, :FEW_WORDS], zeros3)
         load_tab(1)
+        ws_raw.append(held("ws_raw1", [P, 2 * R], U8))
+        load_ws(1)
 
         pages = []
 
@@ -155,7 +153,8 @@ def tile_list_msg_relu_biasP_kernel(
         nc.gpsimd.tensor_copy(shifted[1][:].bitcast(I32)[:, FEW_WORDS:], zeros4)
         nc.gpsimd.memset(wd_sc_raw[:].bitcast(I32)[:, FEW_WORDS:], 0)
         pages.append(held("page1", [P, T], F32))
-        nc.vector.memset(pages[1][:].bitcast(I32), 0)
+        nc.vector.memset(pages[1][:, : T // 2].bitcast(I32), 0)
+        nc.gpsimd.memset(pages[1][:, T // 2 :].bitcast(I32), 0)
 
         def gather_scales(dst, side, first, count):
             nc.vector.tensor_copy(dst[:], tab_sc[:].indirect(entries(lists[side], first, count)))
@@ -195,9 +194,11 @@ def tile_list_msg_relu_biasP_kernel(
             )
             return dealt
 
-        ws_w = [deal_words("ws_w0", ws_raw[0][:].bitcast(U16), U16, R)]
+        ws_w = [deal_words("ws_w0", ws_raw[0][:].bitcast(U16), U16, R)[:]]
         wt_w = [deal_words(f"wt_w{a}", wt_raw[:, a, :].bitcast(U32), U32, R) for a in range(PASSES)]
-        ws_w.append(deal_words("ws_w1", ws_raw[1][:].bitcast(U16), U16, R))
+        ws_late = [
+            deal_words(f"ws_w1_{h}", ws_raw[1][:].bitcast(U16)[:, h * BANK : (h + 1) * BANK], U16, BANK) for h in range(2)
+        ]
         ws_sc = [deal_scales(f"ws_sc{i}", ws_sc_raw[:, i * BANK : (i + 1) * BANK]) for i in range(2 * PASSES)]
         wt_sc = [deal_scales(f"wt_sc{i}", wt_sc_raw[:, i * BANK : (i + 1) * BANK]) for i in range(2)]
         add_page("wt_sc_raw")
@@ -216,18 +217,18 @@ def tile_list_msg_relu_biasP_kernel(
             window = tab_w[a][:].bitcast(U32)
             nc.vector.tensor_copy(dst, window.indirect(entries(lists[side], first_chunk * CHUNK, count * CHUNK)))
 
-        gather(0, 1, 0, SOURCE, placed(lag4, "picked0_0_s", [P, 2 * CHUNK], U32, 0)[:, :CHUNK])
+        gather(0, 1, 0, SOURCE, sb("picked0_0_s", [P, CHUNK], U32)[:])
         for first_chunk, count, side in ((0, 1, TARGET), (1, 3, SOURCE), (1, 3, TARGET)):
             gather(first_chunk, count, 0, side, sb(f"picked{first_chunk}_0_{side}", [P, count * CHUNK], U32)[:])
         gather(0, 1, 1, TARGET, sb("picked0_1_t", [P, CHUNK], U32)[:])
-        gather(0, 1, 1, SOURCE, placed(lag3, "picked0_1_s", [P, 3 * CHUNK], U32, 0)[:, :CHUNK])
-        gather(1, 2, 1, TARGET, sb("picked1_1_t", [P, 2 * CHUNK], U32)[:])
+        gather(0, 1, 1, SOURCE, sb("picked0_1_s", [P, CHUNK], U32)[:])
         gather(1, 2, 1, SOURCE, placed(lag1, "picked1_1_s", [P, 2 * CHUNK], U32, 0)[:])
+        gather(1, 3, 1, TARGET, sb("picked1_1_t", [P, 3 * CHUNK], U32)[:])
 
         acc, h_in = {}, {}
         no_bias = 0.0
-        zero_bias = placed(lag2, "zero_bias", [P, FEW_WORDS], F32, 0)
-        nc.vector.memset(zero_bias[:], 0.0)
+        zero_bias = placed(lag2, "zero_bias", [P, 2 * CHUNK], F32, 0)
+        nc.vector.memset(zero_bias[:, :FEW_WORDS], 0.0)
 
         def slices(c, k):
             n = MOVING[c]
@@ -244,7 +245,7 @@ def tile_list_msg_relu_biasP_kernel(
                     continue
                 first, last = c * CHUNK + edges.start, c * CHUNK + edges.stop
                 if side == SOURCE:
-                    w = ws_w[a][:, col : col + P].bitcast(FP4X4)
+                    w = (ws_late[col // BANK][:, col % BANK : col % BANK + P] if a else ws_w[0][:, col : col + P]).bitcast(FP4X4)
                     w_scale = ws_sc[2 * a + col // BANK][:, col % BANK : col % BANK + P]
                     run = first // RUN
                     v_scale = (src_sc, shifted)[a][run][:, first - run * RUN : last - run * RUN]
@@ -324,22 +325,20 @@ def tile_list_msg_relu_biasP_kernel(
         for c, side in ((0, SOURCE), (0, TARGET), (1, SOURCE)):
             for k in (0, 2, 1, 3) if c == 0 else range(4):
                 first_pass(c, k, 0, side, start=(side == SOURCE))
-        tgt_sc.append(gather_scales(placed(lag4, "tgt_sc1", [P, RUN], U8, WORD * CHUNK), TARGET, RUN, RUN))
-        for k in range(2):
+        for k in (0, 2):
             first_pass(0, k, 1, TARGET)
-        for k in range(2):
+        for k in (0, 2):
             first_pass(0, k, 1, SOURCE, stop=True)
             relu(0, k)
-        for k in range(2, 4):
+        for k in (1, 3):
             first_pass(0, k, 1, SOURCE)
             first_pass(0, k, 1, TARGET, stop=True)
             relu(0, k)
-        src_sc.append(gather_scales(placed(lag3, "src_sc1", [P, RUN], U8, WORD * CHUNK), SOURCE, RUN, RUN))
+        src_sc.append(gather_scales(held("src_sc1", [P, RUN], U8, "ws_raw1"), SOURCE, RUN, RUN))
         shift_scales(1)
         quantise_h(0)
-        picked3 = placed(lag2, "picked3", [P, 2, CHUNK], U32, 0)
-        for i, side in enumerate((TARGET, SOURCE)):
-            gather(CHUNKS - 1, 1, 1, side, picked3[:, i, :])
+        tgt_sc.append(gather_scales(placed(lag2, "tgt_sc1", [P, RUN], U8, WORD * CHUNK), TARGET, RUN, RUN))
+        gather(CHUNKS - 1, 1, 1, SOURCE, placed(lag2, "picked3_1_s", [P, CHUNK], U32, 0)[:])
         add_page("tab_w1")
         for k in range(4):
             first_pass(1, k, 1, SOURCE, only=0)

@@ -34,7 +34,7 @@ SOURCE, TARGET = 0, 1
 
 FIRST_BANKS = ((0, 1, 2, 3), (4, 5, 6, 7), (2, 3, 0, 4), (6, 7, 2, 0))
 SECOND_BANKS = ((0, 1), (3, 5))
-LAST_BANKS = (1, 4, 3, 6)
+LAST_BANKS = (7, 4, 3, 6)
 MOVING = (P, CHUNK, CHUNK, CHUNK)
 
 OUT_WIDTHS = (512, 256, 256, 256, 256, 256, 128, 128)
@@ -357,16 +357,23 @@ def tile_list_msg_relu_biasP_kernel(
         whole_bank(2, 3)
         quantise_h(2)
         lagging_page(1, 2, lag1, 0)
-        for k in range(4):
+        for k in range(3):
             whole_bank(3, k)
+        last = [bank("last0", LAST_BANKS[0])]
+        msgs = [sb(f"msg_last{t}", [P, 2 * CHUNK], F32) for t in range(PACK)]
+        second(part(last[0], 0), 2, 0)
+        put(0, 2, 1, part(msgs[0], 0), part(last[0], 0))
+        whole_bank(3, 3)
         quantise_h(3)
         lagging_page(1, 3, lag2, 0)
-        last = [bank(f"last{t}", LAST_BANKS[t]) for t in range(PACK)]
-        for t in range(PACK):
+        last.extend(bank(f"last{t}", LAST_BANKS[t]) for t in range(1, PACK))
+        for t in range(1, PACK):
             second(part(last[t], 0), 2, t)
-        for t in range(PACK):
+        second(part(last[0], 1), 3, 0)
+        put(0, 3, 1, part(msgs[0], 1), part(last[0], 1))
+        for t in range(1, PACK):
             second(part(last[t], 1), 3, t)
-            put(t, 2, 2, sb(f"msg_last{t}", [P, 2 * CHUNK], F32)[:], last[t][:])
+            put(t, 2, 2, msgs[t][:], last[t][:])
 
         out_rows = out_0.rearrange("(p t) c -> p t c", t=PACK)
         pieces = len(OUT_WIDTHS)

@@ -52,6 +52,7 @@ def tile_list_msg_relu_biasP_kernel(
         keep = ctx.enter_context(tc.tile_pool(name="keep", bufs=1))
         lag0 = ctx.enter_context(tc.tile_pool(name="lag0", bufs=1))
         lag1 = ctx.enter_context(tc.tile_pool(name="lag1", bufs=1))
+        lag5 = ctx.enter_context(tc.tile_pool(name="lag5", bufs=1))
         lag2 = ctx.enter_context(tc.tile_pool(name="lag2", bufs=1))
         psum = ctx.enter_context(tc.psum_pool(name="psum", bufs=1))
 
@@ -226,9 +227,9 @@ def tile_list_msg_relu_biasP_kernel(
         gather(1, 3, 1, TARGET, sb("picked1_1_t", [P, 3 * CHUNK], U32)[:])
 
         acc, h_in = {}, {}
-        no_bias = 0.0
         zero_bias = placed(lag2, "zero_bias", [P, 2 * CHUNK], F32, 0)
         nc.vector.memset(zero_bias[:, :FEW_WORDS], 0.0)
+        relu_bias = {(0, k): zero_bias[:, :1] for k in range(4)}
 
         def slices(c, k):
             n = MOVING[c]
@@ -269,7 +270,7 @@ def tile_list_msg_relu_biasP_kernel(
                 h_in[c][:].rearrange("p (a j i) -> p a j i", a=PASSES, i=PACK)[:, half, parts[0][2], t : t + len(parts)],
                 acc[c, k][:].rearrange("p (i j) -> p j i", i=len(parts)),
                 ACT.Relu,
-                bias=(no_bias, zero_bias[:, :1])[c == 0],
+                bias=relu_bias.get((c, k), 0.0),
             )
 
         def finish_bank(c, k):
@@ -286,7 +287,8 @@ def tile_list_msg_relu_biasP_kernel(
 
         def quantise_h(c):
             h_w[c] = sb(f"h_w{c}", [P, PASSES * CHUNK], U32)
-            h_sc[c] = sb(f"h_sc{c}", [P, PASSES * CHUNK], U8)
+            shape = [P, PASSES * CHUNK]
+            h_sc[c] = sb(f"h_sc{c}", shape, U8) if c else placed(lag5, "h_sc0", shape, U8, 0)
             nc.vector.quantize_mx(out=h_w[c][:].bitcast(FP8X4), scales=h_sc[c][:], in_=h_in[c][:])
 
         def second(out, c, t):
@@ -339,7 +341,6 @@ def tile_list_msg_relu_biasP_kernel(
         quantise_h(0)
         tgt_sc.append(gather_scales(placed(lag2, "tgt_sc1", [P, RUN], U8, WORD * CHUNK), TARGET, RUN, RUN))
         gather(CHUNKS - 1, 1, 1, SOURCE, placed(lag2, "picked3_1_s", [P, CHUNK], U32, 0)[:])
-        add_page("tab_w1")
         for k in range(4):
             first_pass(1, k, 1, SOURCE, only=0)
             first_pass(1, k, 0, TARGET)
@@ -348,6 +349,11 @@ def tile_list_msg_relu_biasP_kernel(
             relu(1, k)
             if k == 0:
                 second_stage(0)
+                late_zero = placed(lag5, "late_zero", [P, FEW_WORDS], F32, 0)
+                nc.gpsimd.memset(late_zero[:], 0.0)
+                relu_bias[1, 1] = late_zero[:, :1]
+                pages.append(placed(lag5, "page3", [P, T], F32, ALIGN))
+                nc.gpsimd.memset(pages[3][:].bitcast(I32), 0)
         quantise_h(1)
         lagging_page(0, 2, lag0, 0)
         lagging_page(0, 3, lag0, WORD * CHUNK)

from contextlib import ExitStack

import concourse.mybir as mybir

K, R, N, T, J = 1024, 1024, 512, 2048, 1024
FLOPS = 2 * J * (2 * K * R + R * N)

F32 = mybir.dt.float32
BF16 = mybir.dt.bfloat16
I32 = mybir.dt.int32
U32 = mybir.dt.uint32
U16 = mybir.dt.uint16
U8 = mybir.dt.uint8
FP8X4 = mybir.dt.float8_e4m3fn_x4
FP4X4 = mybir.dt.float4_e2m1fn_x4
ACT = mybir.ActivationFunctionType
MULT = mybir.AluOpType.mult

P = 128
PACK = 4
PASSES = 2
QUADRANTS = 4
QUAD = P // QUADRANTS
ROWS = 4
BANK = 512
CHUNK = 2 * P
CHUNKS = J // CHUNK
RUN = J // 2
PER_COLUMN = 16
WORD = 4
ALIGN = 64
FEW_WORDS = 8
SOURCE, TARGET = 0, 1

FIRST_BANKS = ((0, 1, 2, 3), (4, 5, 6, 7), (2, 3, 0, 4), (6, 7, 2, 0))
SECOND_BANKS = ((0, 1), (3, 5))
LAST_BANKS = (7, 4, 3, 6)
MOVING = (P, CHUNK, CHUNK, CHUNK)

OUT_WIDTHS = (512, 256, 256, 256, 256, 256, 128, 128)
VECTOR_ROUNDS = 256
SCALAR_WEAVES = 3


def tile_list_msg_relu_biasP_kernel(
    tc, tab_words, tab_scales, ws_words, ws_scales, wt_words, wt_scales, wd_words, wd_scales,
    b, wgo, offs, offs2, out_0, out_1, out_2,
):
    nc = tc.nc

    with ExitStack() as ctx:
        keep = ctx.enter_context(tc.tile_pool(name="keep", bufs=1))
        lag0 = ctx.enter_context(tc.tile_pool(name="lag0", bufs=1))
        lag1 = ctx.enter_context(tc.tile_pool(name="lag1", bufs=1))
        lag5 = ctx.enter_context(tc.tile_pool(name="lag5", bufs=1))
        lag2 = ctx.enter_context(tc.tile_pool(name="lag2", bufs=1))
        psum = ctx.enter_context(tc.psum_pool(name="psum", bufs=1))

        def sb(name, shape, dtype, tag=None):
            return keep.tile(shape, dtype, name=name, tag=tag or name, align_bytes=ALIGN)

        def placed(pool, name, shape, dtype, offset):
            return pool.tile(shape, dtype, name=name, offset=offset, align_bytes=ALIGN)

        def bank(name, index):
            return psum.tile([P, BANK], F32, name=name, tag=f"bank{index}")

        def entries(list_tile, first, count):
            return list_tile[:, first // PER_COLUMN : (first + count) // PER_COLUMN]

        def load_two_planes(queues, plane, scales, shift):
            for q in (0, 2, 1, 3):
                queues[q // 2].dma_start(
                    plane[QUAD * q + shift : QUAD * q + shift + PASSES * ROWS, :].bitcast(I32),
                    scales[:, ROWS * q : ROWS * (q + 1), :].bitcast(I32),
                )

        def load_side_by_side(queue, plane, scales):
            for s in range(ROWS):
                queue.dma_start(
                    plane[s : P : QUAD, :].bitcast(I32).rearrange("p (a r) -> p a r", a=PASSES),
                    scales[:, s : ROWS * QUADRANTS : ROWS, :].rearrange("a q r -> q a r").bitcast(I32),
                )

        lists = [keep.tile([P, J // PER_COLUMN], U16, name=name) for name in ("src_list", "tgt_list")]
        nc.sync.dma_start(lists[SOURCE][:], offs)
        ws_raw = [sb("ws_raw0", [P, 2 * R], U8)]

        def load_ws(a):
            nc.sync.dma_start(ws_raw[a][:].bitcast(I32), ws_words[a].bitcast(I32))

        load_ws(0)
        nc.sync.dma_start(lists[TARGET][:], offs2)

        words = {
            "first": {"tab_w0": T},
            "second": {"wt_raw": PASSES * R, "page0": T, "page1": T, "wt_sc_raw": T},
            "third": {"tab_w1": T, "ws_raw1": R // 2},
            "fourth": {"wd_raw": PASSES * N, "edge_w": J, "bias": 2 * T},
        }
        pools = {name: ctx.enter_context(tc.tile_pool(name=name, bufs=1)) for name in words}
        at = {}
        for name in words:
            names = list(words[name])
            for i, tile_name in enumerate(names):
                at[tile_name] = (pools[name], WORD * sum(words[name][n] for n in names[:i]))

        def held(name, shape, dtype, place=None):
            pool, offset = at[place or name]
            return placed(pool, name, shape, dtype, offset)

        def zeros(name, engine, count):
            tile = placed(pools[name], f"zeros_{name}", [P, sum(words[name].values())], I32, 0)
            engine.memset(tile[:, :count], 0)
            return tile[:, :count]

        tab_sc = sb("tab_sc", [P, T], U8)
        wd_sc_raw = sb("wd_sc_raw", [P, N], U8)
        shifted = [placed(lag0, "shifted0", [P, RUN], U8, WORD * CHUNK - RUN // 2), sb("shifted1", [P, RUN], U8)]
        ws_sc_raw = sb("ws_sc_raw", [P, PASSES * R], U8)
        nc.gpsimd.memset(tab_sc[:].bitcast(I32), 0)
        zeros1 = zeros("first", nc.gpsimd, FEW_WORDS)
        nc.gpsimd.tensor_copy(wd_sc_raw[:].bitcast(I32)[:, :FEW_WORDS], zeros1)
        zeros3 = zeros("third", nc.gpsimd, FEW_WORDS)
        zeros4 = zeros("fourth", nc.gpsimd, RUN // WORD - FEW_WORDS)
        zeros2 = zeros("second", nc.vector, RUN // WORD)
        nc.vector.memset(ws_sc_raw[:].bitcast(I32), 0)
        nc.vector.tensor_copy(shifted[0][:].bitcast(I32), zeros2)
        load_two_planes((nc.sync, nc.scalar), tab_sc, tab_scales, 0)

        def load_tab(a):
            nc.sync.dma_start(tab_w[a][:], tab_words[a].rearrange("p t i -> p (t i)").bitcast(I32))

        tab_w = [held("tab_w0", [P, T], I32), held("tab_w1", [P, T], I32)]
        load_tab(0)
        load_side_by_side(nc.sync, ws_sc_raw, ws_scales)
        wt_raw = held("wt_raw", [P, PASSES, R], I32)
        nc.sync.dma_start(wt_raw[:], wt_words.rearrange("a p r i -> p a (r i)").bitcast(I32))
        wt_sc_raw = held("wt_sc_raw", [P, R], U8)
        nc.gpsimd.memset(wt_sc_raw[:].bitcast(I32), 0)
        load_two_planes((nc.sync, nc.sync), wt_sc_raw, wt_scales, ROWS)
        nc.gpsimd.tensor_copy(shifted[1][:].bitcast(I32)[:, :FEW_WORDS], zeros3)
        load_tab(1)
        ws_raw.append(held("ws_raw1", [P, 2 * R], U8))
        load_ws(1)

        pages = []

        def add_page(place):
            pages.append(held(f"page{len(pages)}", [P, T], F32, place))
            nc.gpsimd.memset(pages[-1][:].bitcast(I32), 0)

        add_page("page0")
        nc.gpsimd.tensor_copy(shifted[1][:].bitcast(I32)[:, FEW_WORDS:], zeros4)
        nc.gpsimd.memset(wd_sc_raw[:].bitcast(I32)[:, FEW_WORDS:], 0)
        pages.append(held("page1", [P, T], F32))
        nc.vector.memset(pages[1][:, : T // 2].bitcast(I32), 0)
        nc.gpsimd.memset(pages[1][:, T // 2 :].bitcast(I32), 0)

        def gather_scales(dst, side, first, count):
            nc.vector.tensor_copy(dst[:], tab_sc[:].indirect(entries(lists[side], first, count)))
            return dst

        def shift_scales(run):
            for q in range(QUADRANTS):
                nc.sync.dma_start(
                    shifted[run][QUAD * q : QUAD * q + ROWS, :].bitcast(I32),
                    src_sc[run][QUAD * q + ROWS : QUAD * q + 2 * ROWS, :].bitcast(I32),
                )

        src_sc = [gather_scales(sb("src_sc0", [P, RUN], U8), SOURCE, 0, RUN)]
        tgt_sc = [gather_scales(sb("tgt_sc0", [P, RUN], U8), TARGET, 0, RUN)]
        shift_scales(0)

        wd_raw = held("wd_raw", [P, PASSES, N], I32)
        edge_w = held("edge_w", [P, J], F32)
        bias = held("bias", [P, 2 * T], F32)
        nc.sync.dma_start(wd_raw[:], wd_words.rearrange("a p n i -> p a (n i)").bitcast(I32))
        load_two_planes((nc.sync, nc.sync), wd_sc_raw, wd_scales, 0)
        nc.sync.dma_start(edge_w[:], wgo)
        nc.sync.dma_start(bias[:, :PACK], b.rearrange("(p t) -> p t", t=PACK))

        def deal_words(name, raw, dtype, width):
            dealt = sb(name, [P, width], dtype)
            nc.scalar.copy(
                dealt[:].rearrange("p (h t m) -> p h m t", t=PACK, m=P),
                raw.rearrange("p (h m t) -> p h m t", t=PACK, m=P),
            )
            return dealt

        def deal_scales(name, raw):
            dealt = sb(name, [P, BANK], U8)
            nc.gpsimd.tensor_copy(
                dealt[:].rearrange("p (t m) -> p t m", t=PACK), raw.rearrange("p (m t) -> p t m", t=PACK)
            )
            return dealt

        ws_w = [deal_words("ws_w0", ws_raw[0][:].bitcast(U16), U16, R)[:]]
        wt_w = [deal_words(f"wt_w{a}", wt_raw[:, a, :].bitcast(U32), U32, R) for a in range(PASSES)]
        ws_late = [
            deal_words(f"ws_w1_{h}", ws_raw[1][:].bitcast(U16)[:, h * BANK : (h + 1) * BANK], U16, BANK) for h in range(2)
        ]
        ws_sc = [deal_scales(f"ws_sc{i}", ws_sc_raw[:, i * BANK : (i + 1) * BANK]) for i in range(2 * PASSES)]
        wt_sc = [deal_scales(f"wt_sc{i}", wt_sc_raw[:, i * BANK : (i + 1) * BANK]) for i in range(2)]
        add_page("wt_sc_raw")
        wd_w = sb("wd_w", [P, PASSES * N], I32)
        nc.gpsimd.tensor_copy(
            wd_w[:].rearrange("p (a t m) -> p a t m", a=PASSES, t=PACK),
            wd_raw[:].rearrange("p a (m t) -> p a t m", t=PACK),
        )
        wd_sc = deal_scales("wd_sc", wd_sc_raw[:])

        picked = {}

        def gather(first_chunk, count, a, side, dst):
            for i in range(count):
                picked[first_chunk + i, a, side] = dst[:, i * CHUNK : (i + 1) * CHUNK]
            window = tab_w[a][:].bitcast(U32)
            nc.vector.tensor_copy(dst, window.indirect(entries(lists[side], first_chunk * CHUNK, count * CHUNK)))

        gather(0, 1, 0, SOURCE, sb("picked0_0_s", [P, CHUNK], U32)[:])
        for first_chunk, count, side in ((0, 1, TARGET), (1, 3, SOURCE), (1, 3, TARGET)):
            gather(first_chunk, count, 0, side, sb(f"picked{first_chunk}_0_{side}", [P, count * CHUNK], U32)[:])
        gather(0, 1, 1, TARGET, sb("picked0_1_t", [P, CHUNK], U32)[:])
        gather(0, 1, 1, SOURCE, sb("picked0_1_s", [P, CHUNK], U32)[:])
        gather(1, 2, 1, SOURCE, placed(lag1, "picked1_1_s", [P, 2 * CHUNK], U32, 0)[:])
        gather(1, 3, 1, TARGET, sb("picked1_1_t", [P, 3 * CHUNK], U32)[:])

        acc, h_in = {}, {}
        zero_bias = placed(lag2, "zero_bias", [P, 2 * CHUNK], F32, 0)
        nc.vector.memset(zero_bias[:, :FEW_WORDS], 0.0)
        relu_bias = {(0, k): zero_bias[:, :1] for k in range(4)}

        def slices(c, k):
            n = MOVING[c]
            per_bank = BANK // n
            group, rest = divmod(k * per_bank, PASSES * PACK)
            return [(slice(i * n, (i + 1) * n), P * (rest + i), slice(group * n, (group + 1) * n)) for i in range(per_bank)]

        def first_pass(c, k, a, side, start=False, stop=False, only=None):
            if start:
                acc[c, k] = bank(f"a{c}_{k}", FIRST_BANKS[c][k])
            parts = slices(c, k)
            for i, (cols, col, edges) in enumerate(parts):
                if only is not None and i != only:
                    continue
                first, last = c * CHUNK + edges.start, c * CHUNK + edges.stop
                if side == SOURCE:
                    w = (ws_late[col // BANK][:, col % BANK : col % BANK + P] if a else ws_w[0][:, col : col + P]).bitcast(FP4X4)
                    w_scale = ws_sc[2 * a + col // BANK][:, col % BANK : col % BANK + P]
                    run = first // RUN
                    v_scale = (src_sc, shifted)[a][run][:, first - run * RUN : last - run * RUN]
                else:
                    w = wt_w[a][:, col : col + P].bitcast(FP8X4)
                    w_scale = wt_sc[col // BANK][ROWS * (a + 1) : P, col % BANK : col % BANK + P]
                    run = first // RUN
                    v_scale = tgt_sc[run][ROWS * a : P, first - run * RUN : last - run * RUN]
                nc.tensor.matmul_mx(
                    out=acc[c, k][:, cols], lhsT=w, lhsT_scale=w_scale,
                    rhs=picked[c, a, side][:, edges].bitcast(FP8X4), rhs_scale=v_scale,
                    start=start and i == 0, stop=stop and i == len(parts) - 1,
                )

        def relu(c, k):
            if c not in h_in:
                h_in[c] = sb(f"h_in{c}", [P, PASSES * CHUNK * PACK], BF16)
            parts = slices(c, k)
            half, t = divmod(parts[0][1] // P, PACK)
            nc.scalar.activation(
                h_in[c][:].rearrange("p (a j i) -> p a j i", a=PASSES, i=PACK)[:, half, parts[0][2], t : t + len(parts)],
                acc[c, k][:].rearrange("p (i j) -> p j i", i=len(parts)),
                ACT.Relu,
                bias=relu_bias.get((c, k), 0.0),
            )

        def finish_bank(c, k):
            first_pass(c, k, 1, TARGET)
            first_pass(c, k, 1, SOURCE, stop=True)
            relu(c, k)

        def whole_bank(c, k):
            first_pass(c, k, 0, SOURCE, start=True)
            first_pass(c, k, 0, TARGET)
            finish_bank(c, k)

        h_w, h_sc = {}, {}

        def quantise_h(c):
            h_w[c] = sb(f"h_w{c}", [P, PASSES * CHUNK], U32)
            shape = [P, PASSES * CHUNK]
            h_sc[c] = sb(f"h_sc{c}", shape, U8) if c else placed(lag5, "h_sc0", shape, U8, 0)
            nc.vector.quantize_mx(out=h_w[c][:].bitcast(FP8X4), scales=h_sc[c][:], in_=h_in[c][:])

        def second(out, c, t):
            for a in range(PASSES):
                nc.tensor.matmul_mx(
                    out=out, lhsT=wd_w[:, a * N + P * t : a * N + P * (t + 1)].bitcast(FP8X4),
                    lhsT_scale=wd_sc[ROWS * a : P, P * t : P * (t + 1)],
                    rhs=h_w[c][:, a * CHUNK : (a + 1) * CHUNK].bitcast(FP8X4),
                    rhs_scale=h_sc[c][:, a * CHUNK : (a + 1) * CHUNK],
                    start=(a == 0), stop=(a == PASSES - 1),
                )

        def put(t, first_chunk, count, msg, y):
            first, edges = first_chunk * CHUNK, count * CHUNK
            nc.scalar.activation(msg, y, ACT.Identity, bias=bias[:, t : t + 1])
            nc.vector.tensor_tensor(
                pages[t][:].indirect(entries(lists[TARGET], first, edges)), msg, edge_w[:, first : first + edges], MULT,
            )

        def part(tile, i):
            return tile[:, i * CHUNK : (i + 1) * CHUNK]

        lagging = {}

        def second_stage(c):
            early = bank(f"early{c}", SECOND_BANKS[c][0])
            lagging[c] = bank(f"lag{c}", SECOND_BANKS[c][1])
            for t in range(PACK):
                second(part((early, lagging[c])[t // 2], t % 2), c, t)
            for t in range(2):
                put(t, c, 1, sb(f"msg{c}_{t}", [P, CHUNK], F32)[:], part(early, t))

        def lagging_page(c, t, pool, offset):
            put(t, c, 1, placed(pool, f"msg{c}_{t}", [P, CHUNK], F32, offset)[:], part(lagging[c], t - 2))

        for c, side in ((0, SOURCE), (0, TARGET), (1, SOURCE)):
            for k in (0, 2, 1, 3) if c == 0 else range(4):
                first_pass(c, k, 0, side, start=(side == SOURCE))
        for k in (0, 2):
            first_pass(0, k, 1, TARGET)
        for k in (0, 2):
            first_pass(0, k, 1, SOURCE, stop=True)
            relu(0, k)
        for k in (1, 3):
            first_pass(0, k, 1, SOURCE)
            first_pass(0, k, 1, TARGET, stop=True)
            relu(0, k)
        src_sc.append(gather_scales(held("src_sc1", [P, RUN], U8, "ws_raw1"), SOURCE, RUN, RUN))
        shift_scales(1)
        quantise_h(0)
        tgt_sc.append(gather_scales(placed(lag2, "tgt_sc1", [P, RUN], U8, WORD * CHUNK), TARGET, RUN, RUN))
        gather(CHUNKS - 1, 1, 1, SOURCE, placed(lag2, "picked3_1_s", [P, CHUNK], U32, 0)[:])
        for k in range(4):
            first_pass(1, k, 1, SOURCE, only=0)
            first_pass(1, k, 0, TARGET)
            first_pass(1, k, 1, TARGET)
            first_pass(1, k, 1, SOURCE, stop=True, only=1)
            relu(1, k)
            if k == 0:
                second_stage(0)
                late_zero = placed(lag5, "late_zero", [P, FEW_WORDS], F32, 0)
                nc.gpsimd.memset(late_zero[:], 0.0)
                relu_bias[1, 1] = late_zero[:, :1]
                pages.append(placed(lag5, "page3", [P, T], F32, ALIGN))
                nc.gpsimd.memset(pages[3][:].bitcast(I32), 0)
        quantise_h(1)
        lagging_page(0, 2, lag0, 0)
        lagging_page(0, 3, lag0, WORD * CHUNK)
        for k in range(3):
            whole_bank(2, k)
        second_stage(1)
        whole_bank(2, 3)
        quantise_h(2)
        lagging_page(1, 2, lag1, 0)
        for k in range(3):
            whole_bank(3, k)
        last = [bank("last0", LAST_BANKS[0])]
        msgs = [sb(f"msg_last{t}", [P, 2 * CHUNK], F32) for t in range(PACK)]
        second(part(last[0], 0), 2, 0)
        put(0, 2, 1, part(msgs[0], 0), part(last[0], 0))
        whole_bank(3, 3)
        quantise_h(3)
        lagging_page(1, 3, lag2, 0)
        last.extend(bank(f"last{t}", LAST_BANKS[t]) for t in range(1, PACK))
        for t in range(1, PACK):
            second(part(last[t], 0), 2, t)
        second(part(last[0], 1), 3, 0)
        put(0, 3, 1, part(msgs[0], 1), part(last[0], 1))
        for t in range(1, PACK):
            second(part(last[t], 1), 3, t)
            put(t, 2, 2, msgs[t][:], last[t][:])

        out_rows = out_0.rearrange("(p t) c -> p t c", t=PACK)
        pieces = len(OUT_WIDTHS)
        starts = [sum(OUT_WIDTHS[:i]) for i in range(pieces)]
        pairs = [
            placed(at["bias"][0], f"pairs{i}", [P, 2, w, 2], BF16, at["bias"][1] + 2 * WORD * starts[i])
            for i, w in enumerate(OUT_WIDTHS)
        ]
        for t in range(PACK):
            nc.sync.dma_start(out_rows[:, t, :], pages[t][:])
            for i, w in enumerate(OUT_WIDTHS):
                first = VECTOR_ROUNDS if i == 0 and t >= 2 else 0
                if first:
                    nc.vector.tensor_copy(pairs[i][:, t // 2, :first, t % 2], pages[t][:, :first])
                nc.scalar.copy(pairs[i][:, t // 2, first:, t % 2], pages[t][:, starts[i] + first : starts[i] + w])

        out_sc = sb("out_sc", [P, BANK], U8)
        out_words = out_1[0].rearrange("p t i -> p (t i)").bitcast(I32)
        codes = [sb(f"codes{i}", [P, BANK], I32) for i in range(T // BANK)]
        woven = []

        def weave(i):
            woven.append(sb(f"woven{i}", [P, OUT_WIDTHS[i] * PACK], BF16))
            word_copy = nc.vector.tensor_copy if i < pieces - SCALAR_WEAVES else nc.scalar.copy
            shares = (slice(VECTOR_ROUNDS, None), slice(0, VECTOR_ROUNDS)) if i == 0 else (slice(None),)
            for share in shares:
                word_copy(
                    woven[i][:].bitcast(F32).rearrange("p (c u) -> p c u", u=2)[:, share],
                    pairs[i][:].rearrange("p u c e -> p u (c e)").bitcast(F32).rearrange("p u c -> p c u")[:, share],
                )

        def quantise_piece(i):
            block, first = divmod(starts[i], BANK)
            cols = slice(first, first + OUT_WIDTHS[i])
            nc.vector.quantize_mx(
                out=codes[block][:, cols].bitcast(FP8X4), scales=out_sc[ROWS * block : P, cols], in_=woven[i][:]
            )
            if i == pieces - 1:
                nc.sync.dma_start(out_words[:, starts[i] :], codes[block][:, cols])
            elif i == pieces - 2:
                nc.sync.dma_start(out_words[:, block * BANK : starts[-1]], codes[block][:, : cols.stop])
            elif cols.stop == BANK:
                nc.sync.dma_start(out_words[:, block * BANK : (block + 1) * BANK], codes[block][:])

        weave(0)
        weave(1)
        for i in range(pieces):
            quantise_piece(i)
            if i + 2 < pieces:
                weave(i + 2)
        for q in range(QUADRANTS):
            (nc.scalar, nc.sync)[q % 2].dma_start(
                out_2[0, ROWS * q : ROWS * (q + 1), :].rearrange("s (i c) -> i s c", c=BANK).bitcast(I32),
                out_sc[QUAD * q : QUAD * q + ROWS * ROWS, :].bitcast(I32),
            )
